import numpy as np
import ml_dtypes


def mxq(x, axis, fmt="e4m3"):
    dtype, down = {"e4m3": (ml_dtypes.float8_e4m3fn, 7), "e5m2": (ml_dtypes.float8_e5m2, 14)}[fmt]
    v = np.moveaxis(np.asarray(x, np.float32).astype(ml_dtypes.bfloat16).astype(np.float64), axis, -1)
    blocks = v.reshape(v.shape[:-1] + (-1, 32))
    amax = np.abs(blocks).max(-1, keepdims=True)
    byte = np.maximum(np.where(amax > 0, np.frexp(amax)[1] - 1 + 127, 0) - down, 1)
    scale = np.exp2(byte - 127.0)
    codes = (blocks / scale).astype(np.float32).astype(dtype).astype(np.float64)
    return np.moveaxis((codes * scale).reshape(v.shape), -1, axis)


WIDE = False


def mx_kscale(k):
    if not WIDE:
        return np.ones(k)
    levels = np.array([10, -10, 5, -5, 0])
    if k % 512:
        return np.exp2(np.random.permutation(np.resize(levels, k // 32))).repeat(32)
    a = np.empty((k // 512, 16))
    for p in range(k // 512):
        a[p, :8] = np.random.permutation(np.resize(levels, 8))
        for g in range(8):
            far = levels[np.abs(levels - a[p, g]) >= 10]
            a[p, g + 8] = far[np.random.randint(len(far))]
    return np.exp2(a.ravel()).repeat(32)


def f64(x):
    return np.asarray(x).astype(np.float64)


def striped(idx):
    return np.tile(idx.reshape(-1, 16).T, (8, 1)).astype(np.uint16)


def unstriped(offs):
    return offs[:16].T.reshape(-1).astype(np.int64)


E2M1 = np.array([0.0, 0.5, 1.0, 1.5, 2.0, 3.0, 4.0, 6.0, -0.0, -0.5, -1.0, -1.5, -2.0, -3.0, -4.0, -6.0])


def pack_weight(w, fmt):
    k, n = w.shape
    w = f64(np.asarray(w, np.float32).astype(ml_dtypes.bfloat16)).reshape(k // 32, 32, n)
    amax = np.abs(w).max(1)
    if fmt == "e4m3":
        byte = np.frexp(amax)[1] - 1 + 127 - 7
    else:
        mant, ex = np.frexp(amax / 6.0)
        byte = np.where(mant > 0.5, ex, ex - 1) + 127
    byte = np.clip(np.where(amax > 0, byte, 1), 1, 254)
    scaled = (w * np.exp2(127.0 - byte)[:, None, :]).reshape(k, n).astype(np.float32)
    by_word = np.ascontiguousarray(scaled.reshape(k // 512, 128, 4, n).transpose(0, 1, 3, 2))
    if fmt == "e4m3":
        words = by_word.astype(ml_dtypes.float8_e4m3fn).view(np.uint8)
    else:
        c = by_word.astype(ml_dtypes.float4_e2m1fn).view(np.uint8) & 0xF
        words = (c[..., 0::2] | (c[..., 1::2] << 4)).reshape(k // 512, 128, 2 * n)
    return np.ascontiguousarray(words), np.ascontiguousarray(byte.astype(np.uint8).reshape(k // 512, 16, n))


def unpack_weight(words, scales, fmt):
    g, _, n = scales.shape
    words = np.ascontiguousarray(words).reshape(g, 128, n, -1)
    if fmt == "e4m3":
        vals = words.view(ml_dtypes.float8_e4m3fn).astype(np.float64)
    else:
        nib = np.empty((g, 128, n, 4), np.uint8)
        nib[..., 0::2] = words & 0xF
        nib[..., 1::2] = words >> 4
        vals = E2M1[nib]
    vals = vals * np.repeat(np.exp2(scales.astype(np.float64) - 127.0), 8, axis=1)[..., None]
    return vals.transpose(0, 1, 3, 2).reshape(g * 512, n)


def gelu(v):
    return 0.5 * v * (1.0 + np.tanh(np.sqrt(2.0 / np.pi) * (v + 0.044715 * v**3)))


K, T, S, H, N = 1024, 4096, 1024, 1024, 384

def setup_inputs():
    n = np.random.standard_normal
    s = mx_kscale(K)[:, None]
    u = mx_kscale(H)[:, None]
    tab_words, tab_scales = pack_weight(n((K, T)) * s, "e2m1")
    w1 = (0.6 * n((K, H)) / np.sqrt(K) / s).astype(np.float32)
    w2_words, w2_scales = pack_weight(0.6 * n((K, H)) / np.sqrt(K) / s, "e4m3")
    w3_words, w3_scales = pack_weight(2.0 * n((H, N)) / np.sqrt(H) / u, "e2m1")
    return {
        "tab_words": tab_words, "tab_scales": tab_scales,
        "offs": striped(np.random.permutation(T)[:S]),
        "offs2": striped(np.random.permutation(T)[:S]),
        "w1": w1,
        "w2_words": w2_words, "w2_scales": w2_scales,
        "gain": (np.exp(0.3 * n(H)) * u[:, 0]).astype(np.float32),
        "w3_words": w3_words, "w3_scales": w3_scales,
        "clinic": (0.7 * n(N)).astype(np.float32),
    }

def reference(tab_words, tab_scales, offs, offs2, w1, w2_words, w2_scales, gain,
              w3_words, w3_scales, clinic):
    TW = unpack_weight(tab_words, tab_scales, "e2m1")
    v = TW[:, unstriped(offs)]
    v2 = TW[:, unstriped(offs2)]
    w1q = mxq(f64(w1), 0, "e4m3")
    w2q = unpack_weight(w2_words, w2_scales, "e4m3")
    w3q = unpack_weight(w3_words, w3_scales, "e2m1")
    ra = np.exp(w1q.T @ v)
    rb = np.exp(w2q.T @ v2)
    h = f64(gain)[:, None] / (ra + rb)
    hq = mxq(h, 0, "e4m3")
    return (w3q.T @ hq) + f64(clinic)[:, None]

@@ -1,0 +1,250 @@
+from contextlib import ExitStack
+
+import concourse.mybir as mybir
+from concourse.masks import make_identity
+
+K, T, S, H, N = 1024, 4096, 1024, 1024, 384
+FLOPS = 2 * (2 * K * H * S + H * N * S)
+
+F32 = mybir.dt.float32
+BF16 = mybir.dt.bfloat16
+I32 = mybir.dt.int32
+U32 = mybir.dt.uint32
+U16 = mybir.dt.uint16
+U8 = mybir.dt.uint8
+FP8X4 = mybir.dt.float8_e4m3fn_x4
+FP4X4 = mybir.dt.float4_e2m1fn_x4
+ACT = mybir.ActivationFunctionType
+ALU = mybir.AluOpType
+
+P = 128
+PACK = 4
+PASS = P * PACK
+HALF = 512
+TILES = HALF // P
+OUT_TILES = N // P
+PAIR = 2
+SPARE = 24
+LIVE = 100
+
+
+def tile_list_partner_invitation_scores_kernel(
+    tc, tab_words, tab_scales, offs, offs2, w1, w2_words, w2_scales, gain, w3_words, w3_scales, clinic, out
+):
+    nc = tc.nc
+    with ExitStack() as ctx:
+        keep = ctx.enter_context(tc.tile_pool(name="keep", bufs=1))
+        ring = ctx.enter_context(tc.tile_pool(name="ring", bufs=2))
+        psum = ctx.enter_context(tc.psum_pool(name="psum", bufs=1))
+
+        def held(name, shape, dtype, tag=""):
+            return keep.tile(shape, dtype, name=name, tag=tag or name, align_bytes=64)
+
+        partner_list = keep.tile([P, S // 16], U16, name="partner_list")
+        case_list = keep.tile([P, S // 16], U16, name="case_list")
+        table = [held("table%d" % a, [P, T], U16) for a in range(2)]
+        table_scales = held("table_scales", [P, T], U8)
+        w2_codes = held("w2_codes", [P, 2, H], U32)
+        w2_planes = held("w2_planes", [P, 2, H], U8)
+        w3_codes = held("w3_codes", [P, 2, 2 * N], U8)
+        w3_planes = held("w3_planes", [P, 2, N], U8)
+        w1_raw = [[held("w1_raw%d%d" % (c, a), [P, PACK, HALF], F32) for a in range(2)] for c in range(2)]
+        gain_t = held("gain_t", [P, 2, PACK], F32)
+        gain_inv = held("gain_inv", [P, 2, PACK], F32)
+        clinic_t = held("clinic_t", [P, OUT_TILES], F32)
+        identity = held("identity", [P, P], F32)
+        planes = [[held("planes%d%d" % (s, a), [P, S], U8) for a in range(2)] for s in range(2)]
+
+        for q in range(4):
+            nc.vector.memset(table_scales[32 * q : 32 * q + SPARE, :].bitcast(I32), 0)
+        for s in range(2):
+            for a in range(2):
+                nc.vector.memset(planes[s][a][96:P, :].bitcast(I32), 0)
+        nc.vector.memset(w3_planes[:].bitcast(I32), 0)
+        nc.gpsimd.memset(w2_planes[:].bitcast(I32), 0)
+        for q in range(4):
+            nc.gpsimd.dma_start(
+                w2_planes[32 * q : 32 * q + 4, :, :].bitcast(I32),
+                w2_scales[:, 4 * q : 4 * q + 4, :].rearrange("a r c -> r a c").bitcast(I32),
+            )
+        make_identity(nc, identity[:])
+
+        nc.sync.dma_start(partner_list[:], offs2)
+        for q in range(4):
+            nc.sync.dma_start(
+                table_scales[32 * q + SPARE : 32 * (q + 1), :].bitcast(I32),
+                tab_scales[:, 4 * q : 4 * q + 4, :].bitcast(I32),
+            )
+        nc.sync.dma_start(case_list[:], offs)
+        cut = T // 2 - T // 32
+        nc.sync.dma_start(table[1][:].bitcast(I32)[:, 0:cut], tab_words[1].bitcast(I32)[:, 0:cut])
+        nc.sync.dma_start(table[0][:].bitcast(I32), tab_words[0].bitcast(I32))
+        nc.sync.dma_start(table[1][:].bitcast(I32)[:, cut : T // 2], tab_words[1].bitcast(I32)[:, cut : T // 2])
+        nc.sync.dma_start(w2_codes[:].bitcast(I32), w2_words.rearrange("a p c i -> p a (c i)").bitcast(I32))
+        for c in range(2):
+            for a in range(2):
+                nc.sync.dma_start(
+                    w1_raw[c][a][:],
+                    w1[PASS * a : PASS * (a + 1), HALF * c : HALF * (c + 1)].rearrange("(p j) r -> p j r", j=PACK),
+                )
+        nc.sync.dma_start(w3_codes[:].bitcast(I32), w3_words.rearrange("a p b -> p a b").bitcast(I32))
+        for q in range(4):
+            nc.sync.dma_start(
+                w3_planes[32 * q : 32 * q + 4, :, :].bitcast(I32),
+                w3_scales[:, 4 * q : 4 * q + 4, :].rearrange("a r c -> r a c").bitcast(I32),
+            )
+        nc.sync.dma_start(gain_t[:], gain.rearrange("(c p t) -> p c t", c=2, t=PACK))
+        with nc.allow_non_contiguous_dma(reason="one offset a partition"):
+            nc.sync.dma_start(clinic_t[:], clinic.rearrange("(n p) -> p n", p=P))
+
+        def gather_scales(s, offsets, queue):
+            picked = held("picked_scales%d" % s, [P, S], U8)
+            nc.vector.tensor_copy(picked[:], table_scales[:].indirect(offsets[:]))
+            for a in range(2):
+                top = SPARE + 4 * a
+                queue.dma_start(planes[s][a][0:LIVE, :].bitcast(I32), picked[top : top + LIVE, :].bitcast(I32))
+            return planes[s]
+
+        def gather_words(s, offsets, h):
+            picked = [held("picked%d%d%d" % (s, h, a), [P, HALF], U16) for a in range(2)]
+            for a in range(2):
+                nc.vector.tensor_copy(picked[a][:], table[a][:].indirect(offsets[:, 32 * h : 32 * (h + 1)]))
+            return picked
+
+        def quantise_w1(c):
+            codes, scale_planes, rounded = [], [], []
+            for a in range(2):
+                grouped = ring.tile([P, HALF, PACK], BF16, name="w1_grouped", align_bytes=64)
+                nc.vector.tensor_copy(
+                    grouped[:].rearrange("p (n i) j -> p n j i", i=PAIR),
+                    w1_raw[c][a][:].rearrange("p j (n i) -> p n j i", i=PAIR),
+                )
+                rounded.append(grouped)
+            for a in range(2):
+                code = held("w1_codes%d%d" % (c, a), [P, HALF], U32, tag=("root%d" % a if c == 1 else ""))
+                plane = held("w1_planes%d%d" % (c, a), [P, HALF], U8)
+                nc.vector.quantize_mx(
+                    out=code[:].bitcast(FP8X4), scales=plane[:], in_=rounded[a][:].rearrange("p n j -> p (n j)")
+                )
+                codes.append(code[:])
+                scale_planes.append(plane[:])
+            return codes, scale_planes
+
+        def first_stage(feature, words, word_planes, h, w_codes, w_planes):
+            for jt in range(TILES):
+                bank = psum.tile([P, HALF], F32, name="acc", tag="acc", bufs=3)
+                for a in range(2):
+                    nc.tensor.matmul_mx(
+                        out=bank[:],
+                        lhsT=words[a][:, P * jt : P * (jt + 1)].bitcast(FP4X4),
+                        lhsT_scale=word_planes[a][:, HALF * h + P * jt : HALF * h + P * (jt + 1)],
+                        rhs=w_codes[a].bitcast(FP8X4),
+                        rhs_scale=w_planes[a],
+                        start=(a == 0),
+                        stop=(a == 1),
+                    )
+                nc.scalar.activation(
+                    feature[:, TILES * h + jt, :].rearrange("p (t m) -> p t m", t=PACK),
+                    bank[:].rearrange("p (m t) -> p t m", t=PACK),
+                    ACT.Exp,
+                )
+
+        rb = [held("rb%d" % c, [P, 2 * TILES, HALF], F32) for c in range(2)]
+        ra = [held("ra%d" % c, [P, 2 * TILES, HALF], F32) for c in range(2)]
+        partner_planes = gather_scales(0, partner_list, nc.scalar)
+        case_planes = gather_scales(1, case_list, nc.sync)
+        for h in range(2):
+            words = gather_words(0, partner_list, h)
+            for c in range(2):
+                first_stage(
+                    rb[c], words, partner_planes, h,
+                    [w2_codes[:, a, HALF * c : HALF * (c + 1)] for a in range(2)],
+                    [w2_planes[:, a, HALF * c : HALF * (c + 1)] for a in range(2)],
+                )
+        case_words = {}
+        for c in range(2):
+            if c == 0:
+                case_words[0] = gather_words(1, case_list, 0)
+            w_codes, w_planes = quantise_w1(c)
+            if c == 0:
+                case_words[1] = gather_words(1, case_list, 1)
+            for h in range(2):
+                first_stage(ra[c], case_words[h], case_planes, h, w_codes, w_planes)
+        nc.vector.reciprocal(gain_inv[:], gain_t[:])
+
+        terms = {}
+        for c, h, tag in ((0, 0, "w1_raw11"), (0, 1, "w1_raw10"), (1, 0, "w1_raw01"), (1, 1, "")):
+            rows = slice(TILES * h, TILES * (h + 1))
+            if tag:
+                total = held("total%d%d" % (c, h), [P, TILES, HALF], F32, tag=tag)
+                nc.vector.tensor_tensor(total[:], ra[c][:, rows, :], rb[c][:, rows, :], ALU.add)
+            for jt in range(TILES):
+                if tag:
+                    terms[c, TILES * h + jt] = [total[:, jt, :]]
+                else:
+                    terms[c, TILES * h + jt] = [ra[c][:, TILES * h + jt, :], rb[c][:, TILES * h + jt, :]]
+
+        def make_h(first, tiles, c):
+            width = P * tiles
+            root = held("root%d%d" % (first, c), [P, PACK, width], F32, tag="root%d" % c)
+            per_bank = HALF // width
+            for t0 in range(0, PACK, per_bank):
+                bank = psum.tile([P, per_bank, width], F32, name="turned", tag="turned", bufs=5)
+                for t in range(t0, t0 + per_bank):
+                    for jt in range(tiles):
+                        pieces = terms[c, first + jt]
+                        for i, term in enumerate(pieces):
+                            nc.tensor.matmul(
+                                bank[:, t - t0, P * jt : P * (jt + 1)],
+                                lhsT=term[:, P * t : P * (t + 1)],
+                                rhs=identity[:],
+                                start=(i == 0),
+                                stop=(i == len(pieces) - 1),
+                                is_transpose=True,
+                            )
+                for t in range(t0, t0 + per_bank):
+                    nc.scalar.activation(
+                        root[:, t, :], bank[:, t - t0, :], ACT.Abs_reciprocal_sqrt, scale=gain_inv[:, c, t : t + 1]
+                    )
+            grouped = ring.tile([P, width, PACK], BF16, name="h_grouped", align_bytes=64)
+            pairs = root[:].rearrange("p t (n i) -> p n t i", i=PAIR)
+            nc.vector.tensor_tensor(grouped[:].rearrange("p (n i) t -> p n t i", i=PAIR), pairs, pairs, ALU.mult)
+            code = held("h_codes%d%d" % (first, c), [P, width], U32)
+            plane = held("h_planes%d%d" % (first, c), [P, width], U8)
+            nc.vector.quantize_mx(
+                out=code[:].bitcast(FP8X4), scales=plane[:], in_=grouped[:].rearrange("p n t -> p (n t)")
+            )
+            return code, plane
+
+        def second_stage(first, tiles, operands, tag, bufs, on_vector):
+            width = P * tiles
+            step = HALF if width == HALF else P
+            banks = [psum.tile([P, width], F32, name="sums", tag=tag, bufs=bufs) for n in range(OUT_TILES)]
+            for c in range(2):
+                code, plane = operands[c]
+                for n in range(OUT_TILES):
+                    for j0 in range(0, width, step):
+                        nc.tensor.matmul_mx(
+                            out=banks[n][:, j0 : j0 + step],
+                            lhsT=w3_codes[:, c, 2 * P * n : 2 * P * (n + 1)].bitcast(FP4X4),
+                            lhsT_scale=w3_planes[:, c, P * n : P * (n + 1)],
+                            rhs=code[:, j0 : j0 + step].bitcast(FP8X4),
+                            rhs_scale=plane[:, j0 : j0 + step],
+                            start=(c == 0 and j0 == 0),
+                            stop=(c == 1 and j0 + step == width),
+                        )
+            for n in range(OUT_TILES):
+                scores = held("scores%d%d" % (first, n), [P, width], F32)
+                if n in on_vector:
+                    nc.vector.tensor_scalar(scores[:], banks[n][:], clinic_t[:, n : n + 1], None, ALU.add)
+                else:
+                    nc.scalar.activation(scores[:], banks[n][:], ACT.Identity, bias=clinic_t[:, n : n + 1])
+                nc.sync.dma_start(out[P * n : P * (n + 1), P * first : P * first + width], scores[:])
+
+        head = [make_h(0, 2, c) for c in range(2)]
+        middle = [make_h(2, 4, 0)]
+        second_stage(0, 2, head, "acc", 3, ())
+        middle.append(make_h(2, 4, 1))
+        tail = [make_h(6, 2, c) for c in range(2)]
+        second_stage(2, 4, middle, "acc", 3, ())
+        second_stage(6, 2, tail, "turned", 5, (1,))

@@ -48,25 +48,19 @@ def tile_list_partner_invitation_scores_kernel(
         w2_planes = held("w2_planes", [P, 2, H], U8)
         w3_codes = held("w3_codes", [P, 2, 2 * N], U8)
         w3_planes = held("w3_planes", [P, 2, N], U8)
-        w1_raw = [[held("w1_raw%d%d" % (c, a), [P, PACK, HALF], F32) for a in range(2)] for c in range(2)]
         gain_t = held("gain_t", [P, 2, PACK], F32)
         gain_inv = held("gain_inv", [P, 2, PACK], F32)
         clinic_t = held("clinic_t", [P, OUT_TILES], F32)
         identity = held("identity", [P, P], F32)
         planes = [[held("planes%d%d" % (s, a), [P, S], U8) for a in range(2)] for s in range(2)]
 
+        nc.vector.memset(w2_planes[:].bitcast(I32), 0)
         for q in range(4):
             nc.vector.memset(table_scales[32 * q : 32 * q + SPARE, :].bitcast(I32), 0)
         for s in range(2):
             for a in range(2):
                 nc.vector.memset(planes[s][a][96:P, :].bitcast(I32), 0)
         nc.vector.memset(w3_planes[:].bitcast(I32), 0)
-        nc.gpsimd.memset(w2_planes[:].bitcast(I32), 0)
-        for q in range(4):
-            nc.gpsimd.dma_start(
-                w2_planes[32 * q : 32 * q + 4, :, :].bitcast(I32),
-                w2_scales[:, 4 * q : 4 * q + 4, :].rearrange("a r c -> r a c").bitcast(I32),
-            )
         make_identity(nc, identity[:])
 
         nc.sync.dma_start(partner_list[:], offs2)
@@ -75,38 +69,28 @@ def tile_list_partner_invitation_scores_kernel(
                 table_scales[32 * q + SPARE : 32 * (q + 1), :].bitcast(I32),
                 tab_scales[:, 4 * q : 4 * q + 4, :].bitcast(I32),
             )
+        for a in range(2):
+            nc.sync.dma_start(table[a][:].bitcast(I32), tab_words[a].bitcast(I32))
         nc.sync.dma_start(case_list[:], offs)
-        cut = T // 2 - T // 32
-        nc.sync.dma_start(table[1][:].bitcast(I32)[:, 0:cut], tab_words[1].bitcast(I32)[:, 0:cut])
-        nc.sync.dma_start(table[0][:].bitcast(I32), tab_words[0].bitcast(I32))
-        nc.sync.dma_start(table[1][:].bitcast(I32)[:, cut : T // 2], tab_words[1].bitcast(I32)[:, cut : T // 2])
-        nc.sync.dma_start(w2_codes[:].bitcast(I32), w2_words.rearrange("a p c i -> p a (c i)").bitcast(I32))
-        for c in range(2):
-            for a in range(2):
-                nc.sync.dma_start(
-                    w1_raw[c][a][:],
-                    w1[PASS * a : PASS * (a + 1), HALF * c : HALF * (c + 1)].rearrange("(p j) r -> p j r", j=PACK),
-                )
-        nc.sync.dma_start(w3_codes[:].bitcast(I32), w3_words.rearrange("a p b -> p a b").bitcast(I32))
         for q in range(4):
             nc.sync.dma_start(
-                w3_planes[32 * q : 32 * q + 4, :, :].bitcast(I32),
-                w3_scales[:, 4 * q : 4 * q + 4, :].rearrange("a r c -> r a c").bitcast(I32),
+                w2_planes[32 * q : 32 * q + 4, :, :].bitcast(I32),
+                w2_scales[:, 4 * q : 4 * q + 4, :].rearrange("a r c -> r a c").bitcast(I32),
             )
-        nc.sync.dma_start(gain_t[:], gain.rearrange("(c p t) -> p c t", c=2, t=PACK))
-        with nc.allow_non_contiguous_dma(reason="one offset a partition"):
-            nc.sync.dma_start(clinic_t[:], clinic.rearrange("(n p) -> p n", p=P))
+        nc.sync.dma_start(w2_codes[:].bitcast(I32), w2_words.rearrange("a p c i -> p a (c i)").bitcast(I32))
 
         def gather_scales(s, offsets, queue):
-            picked = held("picked_scales%d" % s, [P, S], U8)
+            picked = held("picked_scales%d" % s, [P, S], U8, tag="picked_scales")
             nc.vector.tensor_copy(picked[:], table_scales[:].indirect(offsets[:]))
             for a in range(2):
                 top = SPARE + 4 * a
                 queue.dma_start(planes[s][a][0:LIVE, :].bitcast(I32), picked[top : top + LIVE, :].bitcast(I32))
             return planes[s]
 
+        partner_planes = gather_scales(0, partner_list, nc.scalar)
+
         def gather_words(s, offsets, h):
-            picked = [held("picked%d%d%d" % (s, h, a), [P, HALF], U16) for a in range(2)]
+            picked = [held("picked%d%d%d" % (s, h, a), [P, HALF], U16, tag=("rounded%d" % a if (s, h) == (1, 1) else "")) for a in range(2)]
             for a in range(2):
                 nc.vector.tensor_copy(picked[a][:], table[a][:].indirect(offsets[:, 32 * h : 32 * (h + 1)]))
             return picked
@@ -114,10 +98,10 @@ def tile_list_partner_invitation_scores_kernel(
         def quantise_w1(c):
             codes, scale_planes, rounded = [], [], []
             for a in range(2):
-                grouped = ring.tile([P, HALF, PACK], BF16, name="w1_grouped", align_bytes=64)
+                grouped = held("w1_grouped%d%d" % (c, a), [P, HALF, PACK], BF16, tag=("rounded%d" % a if c == 0 else ""))
                 nc.vector.tensor_copy(
                     grouped[:].rearrange("p (n i) j -> p n j i", i=PAIR),
-                    w1_raw[c][a][:].rearrange("p j (n i) -> p n j i", i=PAIR),
+                    w1_raw[c][:, a, :, :].rearrange("p j (n i) -> p n j i", i=PAIR),
                 )
                 rounded.append(grouped)
             for a in range(2):
@@ -151,13 +135,29 @@ def tile_list_partner_invitation_scores_kernel(
 
         rb = [held("rb%d" % c, [P, 2 * TILES, HALF], F32) for c in range(2)]
         ra = [held("ra%d" % c, [P, 2 * TILES, HALF], F32) for c in range(2)]
-        partner_planes = gather_scales(0, partner_list, nc.scalar)
+        partner_words = [gather_words(0, partner_list, h) for h in range(2)]
+        w1_raw = [held("w1_raw%d" % c, [P, 2, PACK, HALF], F32, tag="shared%d" % c) for c in range(2)]
+        for c in range(2):
+            for a in range(2):
+                nc.sync.dma_start(
+                    w1_raw[c][:, a, :, :],
+                    w1[PASS * a : PASS * (a + 1), HALF * c : HALF * (c + 1)].rearrange("(p j) r -> p j r", j=PACK),
+                )
         case_planes = gather_scales(1, case_list, nc.sync)
+        nc.sync.dma_start(w3_codes[:].bitcast(I32), w3_words.rearrange("a p b -> p a b").bitcast(I32))
+        for q in range(4):
+            nc.sync.dma_start(
+                w3_planes[32 * q : 32 * q + 4, :, :].bitcast(I32),
+                w3_scales[:, 4 * q : 4 * q + 4, :].rearrange("a r c -> r a c").bitcast(I32),
+            )
+        nc.sync.dma_start(gain_t[:], gain.rearrange("(c p t) -> p c t", c=2, t=PACK))
+        with nc.allow_non_contiguous_dma(reason="one offset a partition"):
+            nc.sync.dma_start(clinic_t[:], clinic.rearrange("(n p) -> p n", p=P))
+
         for h in range(2):
-            words = gather_words(0, partner_list, h)
             for c in range(2):
                 first_stage(
-                    rb[c], words, partner_planes, h,
+                    rb[c], partner_words[h], partner_planes, h,
                     [w2_codes[:, a, HALF * c : HALF * (c + 1)] for a in range(2)],
                     [w2_planes[:, a, HALF * c : HALF * (c + 1)] for a in range(2)],
                 )
@@ -173,16 +173,17 @@ def tile_list_partner_invitation_scores_kernel(
         nc.vector.reciprocal(gain_inv[:], gain_t[:])
 
         terms = {}
-        for c, h, tag in ((0, 0, "w1_raw11"), (0, 1, "w1_raw10"), (1, 0, "w1_raw01"), (1, 1, "")):
-            rows = slice(TILES * h, TILES * (h + 1))
-            if tag:
-                total = held("total%d%d" % (c, h), [P, TILES, HALF], F32, tag=tag)
-                nc.vector.tensor_tensor(total[:], ra[c][:, rows, :], rb[c][:, rows, :], ALU.add)
-            for jt in range(TILES):
-                if tag:
-                    terms[c, TILES * h + jt] = [total[:, jt, :]]
-                else:
-                    terms[c, TILES * h + jt] = [ra[c][:, TILES * h + jt, :], rb[c][:, TILES * h + jt, :]]
+        totals = [held("total%d" % c, [P, 2 * TILES, HALF], F32, tag="shared%d" % (1 - c)) for c in range(2)]
+        for c in range(2):
+            for h in range(2):
+                rows = slice(TILES * h, TILES * (h + 1))
+                if (c, h) != (1, 1):
+                    nc.vector.tensor_tensor(totals[c][:, rows, :], ra[c][:, rows, :], rb[c][:, rows, :], ALU.add)
+                for jt in range(rows.start, rows.stop):
+                    if (c, h) != (1, 1):
+                        terms[c, jt] = [totals[c][:, jt, :]]
+                    else:
+                        terms[c, jt] = [ra[c][:, jt, :], rb[c][:, jt, :]]
 
         def make_h(first, tiles, c):
             width = P * tiles

@@ -44,7 +44,7 @@ def tile_list_partner_invitation_scores_kernel(
         case_list = keep.tile([P, S // 16], U16, name="case_list")
         table = [held("table%d" % a, [P, T], U16) for a in range(2)]
         table_scales = held("table_scales", [P, T], U8)
-        w2_codes = held("w2_codes", [P, 2, H], U32)
+        w2_codes = [held("w2_codes%d" % c, [P, 2, HALF], U32) for c in range(2)]
         w2_planes = held("w2_planes", [P, 2, H], U8)
         w3_codes = held("w3_codes", [P, 2, 2 * N], U8)
         w3_planes = held("w3_planes", [P, 2, N], U8)
@@ -69,18 +69,20 @@ def tile_list_partner_invitation_scores_kernel(
                 table_scales[32 * q + SPARE : 32 * (q + 1), :].bitcast(I32),
                 tab_scales[:, 4 * q : 4 * q + 4, :].bitcast(I32),
             )
+        nc.sync.dma_start(case_list[:], offs)
         for a in range(2):
             nc.sync.dma_start(table[a][:].bitcast(I32), tab_words[a].bitcast(I32))
-        nc.sync.dma_start(case_list[:], offs)
         for q in range(4):
             nc.sync.dma_start(
                 w2_planes[32 * q : 32 * q + 4, :, :].bitcast(I32),
                 w2_scales[:, 4 * q : 4 * q + 4, :].rearrange("a r c -> r a c").bitcast(I32),
             )
-        nc.sync.dma_start(w2_codes[:].bitcast(I32), w2_words.rearrange("a p c i -> p a (c i)").bitcast(I32))
+        w2_view = w2_words.rearrange("a p c i -> p a (c i)").bitcast(I32)
+        for c in range(2):
+            nc.sync.dma_start(w2_codes[c][:].bitcast(I32), w2_view[:, :, HALF * c : HALF * (c + 1)])
 
         def gather_scales(s, offsets, queue):
-            picked = held("picked_scales%d" % s, [P, S], U8, tag="picked_scales")
+            picked = held("picked_scales%d" % s, [P, S], U8, tag="picked_scales%d" % s)
             nc.vector.tensor_copy(picked[:], table_scales[:].indirect(offsets[:]))
             for a in range(2):
                 top = SPARE + 4 * a
@@ -88,9 +90,12 @@ def tile_list_partner_invitation_scores_kernel(
             return planes[s]
 
         partner_planes = gather_scales(0, partner_list, nc.scalar)
+        case_planes = gather_scales(1, case_list, nc.scalar)
+
+        after = {(0, 1, 0): "picked_scales0", (1, 0, 0): "picked_scales1", (1, 1, 0): "rounded0", (1, 1, 1): "rounded1"}
 
         def gather_words(s, offsets, h):
-            picked = [held("picked%d%d%d" % (s, h, a), [P, HALF], U16, tag=("rounded%d" % a if (s, h) == (1, 1) else "")) for a in range(2)]
+            picked = [held("picked%d%d%d" % (s, h, a), [P, HALF], U16, tag=after.get((s, h, a), "")) for a in range(2)]
             for a in range(2):
                 nc.vector.tensor_copy(picked[a][:], table[a][:].indirect(offsets[:, 32 * h : 32 * (h + 1)]))
             return picked
@@ -143,7 +148,6 @@ def tile_list_partner_invitation_scores_kernel(
                     w1_raw[c][:, a, :, :],
                     w1[PASS * a : PASS * (a + 1), HALF * c : HALF * (c + 1)].rearrange("(p j) r -> p j r", j=PACK),
                 )
-        case_planes = gather_scales(1, case_list, nc.sync)
         nc.sync.dma_start(w3_codes[:].bitcast(I32), w3_words.rearrange("a p b -> p a b").bitcast(I32))
         for q in range(4):
             nc.sync.dma_start(
@@ -158,7 +162,7 @@ def tile_list_partner_invitation_scores_kernel(
             for c in range(2):
                 first_stage(
                     rb[c], partner_words[h], partner_planes, h,
-                    [w2_codes[:, a, HALF * c : HALF * (c + 1)] for a in range(2)],
+                    [w2_codes[c][:, a, :] for a in range(2)],
                     [w2_planes[:, a, HALF * c : HALF * (c + 1)] for a in range(2)],
                 )
         case_words = {}
@@ -172,18 +176,11 @@ def tile_list_partner_invitation_scores_kernel(
                 first_stage(ra[c], case_words[h], case_planes, h, w_codes, w_planes)
         nc.vector.reciprocal(gain_inv[:], gain_t[:])
 
-        terms = {}
         totals = [held("total%d" % c, [P, 2 * TILES, HALF], F32, tag="shared%d" % (1 - c)) for c in range(2)]
         for c in range(2):
             for h in range(2):
                 rows = slice(TILES * h, TILES * (h + 1))
-                if (c, h) != (1, 1):
-                    nc.vector.tensor_tensor(totals[c][:, rows, :], ra[c][:, rows, :], rb[c][:, rows, :], ALU.add)
-                for jt in range(rows.start, rows.stop):
-                    if (c, h) != (1, 1):
-                        terms[c, jt] = [totals[c][:, jt, :]]
-                    else:
-                        terms[c, jt] = [ra[c][:, jt, :], rb[c][:, jt, :]]
+                nc.vector.tensor_tensor(totals[c][:, rows, :], ra[c][:, rows, :], rb[c][:, rows, :], ALU.add)
 
         def make_h(first, tiles, c):
             width = P * tiles
@@ -193,16 +190,11 @@ def tile_list_partner_invitation_scores_kernel(
                 bank = psum.tile([P, per_bank, width], F32, name="turned", tag="turned", bufs=5)
                 for t in range(t0, t0 + per_bank):
                     for jt in range(tiles):
-                        pieces = terms[c, first + jt]
-                        for i, term in enumerate(pieces):
-                            nc.tensor.matmul(
-                                bank[:, t - t0, P * jt : P * (jt + 1)],
-                                lhsT=term[:, P * t : P * (t + 1)],
-                                rhs=identity[:],
-                                start=(i == 0),
-                                stop=(i == len(pieces) - 1),
-                                is_transpose=True,
-                            )
+                        nc.tensor.transpose(
+                            bank[:, t - t0, P * jt : P * (jt + 1)],
+                            totals[c][:, first + jt, P * t : P * (t + 1)],
+                            identity[:],
+                        )
                 for t in range(t0, t0 + per_bank):
                     nc.scalar.activation(
                         root[:, t, :], bank[:, t - t0, :], ACT.Abs_reciprocal_sqrt, scale=gain_inv[:, c, t : t + 1]

@@ -20,12 +20,15 @@ ALU = mybir.AluOpType
 P = 128
 PACK = 4
 PASS = P * PACK
+QUADRANTS = 4
 HALF = 512
 TILES = HALF // P
 OUT_TILES = N // P
-PAIR = 2
+LIST_COLUMNS = HALF // 16
+NEIGHBOURS = 2
 SPARE = 24
 LIVE = 100
+TURN_BANKS = 5
 
 
 def tile_list_partner_invitation_scores_kernel(
@@ -40,6 +43,16 @@ def tile_list_partner_invitation_scores_kernel(
         def held(name, shape, dtype, tag=""):
             return keep.tile(shape, dtype, name=name, tag=tag or name, align_bytes=64)
 
+        def bank_tile(index, shape):
+            return psum.tile(shape, F32, name="bank%d" % index, tag="bank%d" % index)
+
+        def load_planes(planes, scales):
+            for q in range(QUADRANTS):
+                nc.sync.dma_start(
+                    planes[32 * q : 32 * q + 4, :, :].bitcast(I32),
+                    scales[:, 4 * q : 4 * q + 4, :].rearrange("a r c -> r a c").bitcast(I32),
+                )
+
         partner_list = keep.tile([P, S // 16], U16, name="partner_list")
         case_list = keep.tile([P, S // 16], U16, name="case_list")
         table = [held("table%d" % a, [P, T], U16) for a in range(2)]
@@ -52,76 +65,68 @@ def tile_list_partner_invitation_scores_kernel(
         gain_inv = held("gain_inv", [P, 2, PACK], F32)
         clinic_t = held("clinic_t", [P, OUT_TILES], F32)
         identity = held("identity", [P, P], F32)
-        planes = [[held("planes%d%d" % (s, a), [P, S], U8) for a in range(2)] for s in range(2)]
+        partner_planes = [held("partner_planes%d" % a, [P, S], U8) for a in range(2)]
+        case_planes = [held("case_planes%d" % a, [P, S], U8) for a in range(2)]
 
+        for q in range(QUADRANTS):
+            engine = nc.vector if q < QUADRANTS // 2 else nc.gpsimd
+            engine.memset(table_scales[32 * q : 32 * q + SPARE, :].bitcast(I32), 0)
         nc.vector.memset(w2_planes[:].bitcast(I32), 0)
-        for q in range(4):
-            nc.vector.memset(table_scales[32 * q : 32 * q + SPARE, :].bitcast(I32), 0)
-        for s in range(2):
-            for a in range(2):
-                nc.vector.memset(planes[s][a][96:P, :].bitcast(I32), 0)
+        for plane in partner_planes + case_planes:
+            nc.vector.memset(plane[96:P, :].bitcast(I32), 0)
         nc.vector.memset(w3_planes[:].bitcast(I32), 0)
         make_identity(nc, identity[:])
 
         nc.sync.dma_start(partner_list[:], offs2)
-        for q in range(4):
+        for q in range(QUADRANTS):
             nc.sync.dma_start(
                 table_scales[32 * q + SPARE : 32 * (q + 1), :].bitcast(I32),
                 tab_scales[:, 4 * q : 4 * q + 4, :].bitcast(I32),
             )
-        nc.sync.dma_start(case_list[:], offs)
-        for a in range(2):
-            nc.sync.dma_start(table[a][:].bitcast(I32), tab_words[a].bitcast(I32))
-        for q in range(4):
-            nc.sync.dma_start(
-                w2_planes[32 * q : 32 * q + 4, :, :].bitcast(I32),
-                w2_scales[:, 4 * q : 4 * q + 4, :].rearrange("a r c -> r a c").bitcast(I32),
-            )
+        words_in = [tab_words[a].bitcast(I32) for a in range(2)]
+        for cols in (slice(0, T // 4), slice(T // 4, T // 2)):
+            nc.sync.dma_start(table[0][:].bitcast(I32)[:, cols], words_in[0][:, cols])
+        nc.sync.dma_start(table[1][:].bitcast(I32), words_in[1])
+        load_planes(w2_planes, w2_scales)
         w2_view = w2_words.rearrange("a p c i -> p a (c i)").bitcast(I32)
-        for c in range(2):
-            nc.sync.dma_start(w2_codes[c][:].bitcast(I32), w2_view[:, :, HALF * c : HALF * (c + 1)])
+        nc.sync.dma_start(w2_codes[0][:].bitcast(I32), w2_view[:, :, 0:HALF])
 
-        def gather_scales(s, offsets, queue):
-            picked = held("picked_scales%d" % s, [P, S], U8, tag="picked_scales%d" % s)
+        def gather_scales(name, offsets, planes, queue):
+            picked = held(name, [P, S], U8, tag="picked_scales")
             nc.vector.tensor_copy(picked[:], table_scales[:].indirect(offsets[:]))
             for a in range(2):
                 top = SPARE + 4 * a
-                queue.dma_start(planes[s][a][0:LIVE, :].bitcast(I32), picked[top : top + LIVE, :].bitcast(I32))
-            return planes[s]
+                queue.dma_start(planes[a][0:LIVE, :].bitcast(I32), picked[top : top + LIVE, :].bitcast(I32))
 
-        partner_planes = gather_scales(0, partner_list, nc.scalar)
-        case_planes = gather_scales(1, case_list, nc.scalar)
-
-        after = {(0, 1, 0): "picked_scales0", (1, 0, 0): "picked_scales1", (1, 1, 0): "rounded0", (1, 1, 1): "rounded1"}
-
-        def gather_words(s, offsets, h):
-            picked = [held("picked%d%d%d" % (s, h, a), [P, HALF], U16, tag=after.get((s, h, a), "")) for a in range(2)]
+        def gather_words(name, offsets, h, tags=("", "")):
+            picked = [held("%s%d%d" % (name, h, a), [P, HALF], U16, tag=tags[a]) for a in range(2)]
             for a in range(2):
-                nc.vector.tensor_copy(picked[a][:], table[a][:].indirect(offsets[:, 32 * h : 32 * (h + 1)]))
+                columns = offsets[:, LIST_COLUMNS * h : LIST_COLUMNS * (h + 1)]
+                nc.vector.tensor_copy(picked[a][:], table[a][:].indirect(columns))
             return picked
 
-        def quantise_w1(c):
+        def quantise_w1(c, rounded_tags=("", ""), code_tags=("", "")):
             codes, scale_planes, rounded = [], [], []
             for a in range(2):
-                grouped = held("w1_grouped%d%d" % (c, a), [P, HALF, PACK], BF16, tag=("rounded%d" % a if c == 0 else ""))
+                grouped = held("w1_grouped%d%d" % (c, a), [P, HALF, PACK], BF16, tag=rounded_tags[a])
                 nc.vector.tensor_copy(
-                    grouped[:].rearrange("p (n i) j -> p n j i", i=PAIR),
-                    w1_raw[c][:, a, :, :].rearrange("p j (n i) -> p n j i", i=PAIR),
+                    grouped[:].rearrange("p (n e) i -> p n i e", e=NEIGHBOURS),
+                    w1_raw[c][:, a, :, :].rearrange("p i (n e) -> p n i e", e=NEIGHBOURS),
                 )
                 rounded.append(grouped)
             for a in range(2):
-                code = held("w1_codes%d%d" % (c, a), [P, HALF], U32, tag=("root%d" % a if c == 1 else ""))
+                code = held("w1_codes%d%d" % (c, a), [P, HALF], U32, tag=code_tags[a])
                 plane = held("w1_planes%d%d" % (c, a), [P, HALF], U8)
                 nc.vector.quantize_mx(
-                    out=code[:].bitcast(FP8X4), scales=plane[:], in_=rounded[a][:].rearrange("p n j -> p (n j)")
+                    out=code[:].bitcast(FP8X4), scales=plane[:], in_=rounded[a][:].rearrange("p n i -> p (n i)")
                 )
                 codes.append(code[:])
                 scale_planes.append(plane[:])
             return codes, scale_planes
 
-        def first_stage(feature, words, word_planes, h, w_codes, w_planes):
+        def first_stage(feature, h, words, word_planes, w_codes, w_planes):
             for jt in range(TILES):
-                bank = psum.tile([P, HALF], F32, name="acc", tag="acc", bufs=3)
+                bank = bank_tile(TILES * h + jt, [P, HALF])
                 for a in range(2):
                     nc.tensor.matmul_mx(
                         out=bank[:],
@@ -138,56 +143,60 @@ def tile_list_partner_invitation_scores_kernel(
                     ACT.Exp,
                 )
 
+        gather_scales("partner_scales", partner_list, partner_planes, nc.scalar)
+        nc.sync.dma_start(case_list[:], offs)
+        nc.sync.dma_start(w2_codes[1][:].bitcast(I32), w2_view[:, :, HALF : 2 * HALF])
         rb = [held("rb%d" % c, [P, 2 * TILES, HALF], F32) for c in range(2)]
         ra = [held("ra%d" % c, [P, 2 * TILES, HALF], F32) for c in range(2)]
-        partner_words = [gather_words(0, partner_list, h) for h in range(2)]
-        w1_raw = [held("w1_raw%d" % c, [P, 2, PACK, HALF], F32, tag="shared%d" % c) for c in range(2)]
+        partner_words = [gather_words("partner_words", partner_list, h) for h in range(2)]
+        w1_raw = [held("w1_raw%d" % c, [P, 2, PACK, HALF], F32) for c in range(2)]
         for c in range(2):
             for a in range(2):
                 nc.sync.dma_start(
                     w1_raw[c][:, a, :, :],
-                    w1[PASS * a : PASS * (a + 1), HALF * c : HALF * (c + 1)].rearrange("(p j) r -> p j r", j=PACK),
+                    w1[PASS * a : PASS * (a + 1), HALF * c : HALF * (c + 1)].rearrange("(p i) r -> p i r", i=PACK),
                 )
+        gather_scales("case_scales", case_list, case_planes, nc.sync)
         nc.sync.dma_start(w3_codes[:].bitcast(I32), w3_words.rearrange("a p b -> p a b").bitcast(I32))
-        for q in range(4):
-            nc.sync.dma_start(
-                w3_planes[32 * q : 32 * q + 4, :, :].bitcast(I32),
-                w3_scales[:, 4 * q : 4 * q + 4, :].rearrange("a r c -> r a c").bitcast(I32),
-            )
+        load_planes(w3_planes, w3_scales)
         nc.sync.dma_start(gain_t[:], gain.rearrange("(c p t) -> p c t", c=2, t=PACK))
         with nc.allow_non_contiguous_dma(reason="one offset a partition"):
             nc.sync.dma_start(clinic_t[:], clinic.rearrange("(n p) -> p n", p=P))
 
-        for h in range(2):
-            for c in range(2):
+        for c in range(2):
+            for h in range(2):
                 first_stage(
-                    rb[c], partner_words[h], partner_planes, h,
+                    rb[c],
+                    h,
+                    partner_words[h],
+                    partner_planes,
                     [w2_codes[c][:, a, :] for a in range(2)],
                     [w2_planes[:, a, HALF * c : HALF * (c + 1)] for a in range(2)],
                 )
-        case_words = {}
-        for c in range(2):
-            if c == 0:
-                case_words[0] = gather_words(1, case_list, 0)
-            w_codes, w_planes = quantise_w1(c)
-            if c == 0:
-                case_words[1] = gather_words(1, case_list, 1)
-            for h in range(2):
-                first_stage(ra[c], case_words[h], case_planes, h, w_codes, w_planes)
+
+        rounded_tags = ("rounded0", "rounded1")
+        case_words = [gather_words("case_words", case_list, 0)]
+        w_codes, w_planes = quantise_w1(0, rounded_tags=rounded_tags)
+        case_words.append(gather_words("case_words", case_list, 1, tags=rounded_tags))
+        for h in range(2):
+            first_stage(ra[0], h, case_words[h], case_planes, w_codes, w_planes)
+        w_codes, w_planes = quantise_w1(1, code_tags=("root0", "root1"))
+        for h in range(2):
+            first_stage(ra[1], h, case_words[h], case_planes, w_codes, w_planes)
         nc.vector.reciprocal(gain_inv[:], gain_t[:])
 
-        totals = [held("total%d" % c, [P, 2 * TILES, HALF], F32, tag="shared%d" % (1 - c)) for c in range(2)]
+        totals = [held("total%d" % c, [P, 2 * TILES, HALF], F32, tag="w1_raw%d" % (1 - c)) for c in range(2)]
         for c in range(2):
             for h in range(2):
                 rows = slice(TILES * h, TILES * (h + 1))
                 nc.vector.tensor_tensor(totals[c][:, rows, :], ra[c][:, rows, :], rb[c][:, rows, :], ALU.add)
 
-        def make_h(first, tiles, c):
+        def make_h(first, tiles, c, turn):
             width = P * tiles
             root = held("root%d%d" % (first, c), [P, PACK, width], F32, tag="root%d" % c)
             per_bank = HALF // width
             for t0 in range(0, PACK, per_bank):
-                bank = psum.tile([P, per_bank, width], F32, name="turned", tag="turned", bufs=5)
+                bank = bank_tile((turn + t0 // per_bank) % TURN_BANKS, [P, per_bank, width])
                 for t in range(t0, t0 + per_bank):
                     for jt in range(tiles):
                         nc.tensor.transpose(
@@ -200,8 +209,8 @@ def tile_list_partner_invitation_scores_kernel(
                         root[:, t, :], bank[:, t - t0, :], ACT.Abs_reciprocal_sqrt, scale=gain_inv[:, c, t : t + 1]
                     )
             grouped = ring.tile([P, width, PACK], BF16, name="h_grouped", align_bytes=64)
-            pairs = root[:].rearrange("p t (n i) -> p n t i", i=PAIR)
-            nc.vector.tensor_tensor(grouped[:].rearrange("p (n i) t -> p n t i", i=PAIR), pairs, pairs, ALU.mult)
+            y = root[:].rearrange("p t (n e) -> p n t e", e=NEIGHBOURS)
+            nc.vector.tensor_tensor(grouped[:].rearrange("p (n e) t -> p n t e", e=NEIGHBOURS), y, y, ALU.mult)
             code = held("h_codes%d%d" % (first, c), [P, width], U32)
             plane = held("h_planes%d%d" % (first, c), [P, width], U8)
             nc.vector.quantize_mx(
@@ -209,10 +218,10 @@ def tile_list_partner_invitation_scores_kernel(
             )
             return code, plane
 
-        def second_stage(first, tiles, operands, tag, bufs, on_vector):
+        def second_stage(first, tiles, operands, first_bank, on_vector=()):
             width = P * tiles
             step = HALF if width == HALF else P
-            banks = [psum.tile([P, width], F32, name="sums", tag=tag, bufs=bufs) for n in range(OUT_TILES)]
+            banks = [bank_tile(first_bank + n, [P, width]) for n in range(OUT_TILES)]
             for c in range(2):
                 code, plane = operands[c]
                 for n in range(OUT_TILES):
@@ -234,10 +243,10 @@ def tile_list_partner_invitation_scores_kernel(
                     nc.scalar.activation(scores[:], banks[n][:], ACT.Identity, bias=clinic_t[:, n : n + 1])
                 nc.sync.dma_start(out[P * n : P * (n + 1), P * first : P * first + width], scores[:])
 
-        head = [make_h(0, 2, c) for c in range(2)]
-        middle = [make_h(2, 4, 0)]
-        second_stage(0, 2, head, "acc", 3, ())
-        middle.append(make_h(2, 4, 1))
-        tail = [make_h(6, 2, c) for c in range(2)]
-        second_stage(2, 4, middle, "acc", 3, ())
-        second_stage(6, 2, tail, "turned", 5, (1,))
+        head = [make_h(0, 2, c, turn=2 * c) for c in range(2)]
+        middle = [make_h(2, 4, 0, turn=4)]
+        second_stage(0, 2, head, TURN_BANKS)
+        middle.append(make_h(2, 4, 1, turn=8))
+        tail = [make_h(6, 2, c, turn=12 + 2 * c) for c in range(2)]
+        second_stage(2, 4, middle, TURN_BANKS)
+        second_stage(6, 2, tail, 16 % TURN_BANKS, on_vector=(1,))

@@ -185,11 +185,11 @@ def tile_list_partner_invitation_scores_kernel(
             first_stage(ra[1], h, case_words[h], case_planes, w_codes, w_planes)
         nc.vector.reciprocal(gain_inv[:], gain_t[:])
 
-        totals = [held("total%d" % c, [P, 2 * TILES, HALF], F32, tag="w1_raw%d" % (1 - c)) for c in range(2)]
-        for c in range(2):
-            for h in range(2):
-                rows = slice(TILES * h, TILES * (h + 1))
-                nc.vector.tensor_tensor(totals[c][:, rows, :], ra[c][:, rows, :], rb[c][:, rows, :], ALU.add)
+        total = held("total", [P, 2 * TILES, HALF], F32, tag="w1_raw1")
+        for h in range(2):
+            rows = slice(TILES * h, TILES * (h + 1))
+            nc.vector.tensor_tensor(total[:, rows, :], ra[0][:, rows, :], rb[0][:, rows, :], ALU.add)
+        terms = [[total], [rb[1], ra[1]]]
 
         def make_h(first, tiles, c, turn):
             width = P * tiles
@@ -199,11 +199,15 @@ def tile_list_partner_invitation_scores_kernel(
                 bank = bank_tile((turn + t0 // per_bank) % TURN_BANKS, [P, per_bank, width])
                 for t in range(t0, t0 + per_bank):
                     for jt in range(tiles):
-                        nc.tensor.transpose(
-                            bank[:, t - t0, P * jt : P * (jt + 1)],
-                            totals[c][:, first + jt, P * t : P * (t + 1)],
-                            identity[:],
-                        )
+                        for term in terms[c]:
+                            nc.tensor.matmul(
+                                bank[:, t - t0, P * jt : P * (jt + 1)],
+                                term[:, first + jt, P * t : P * (t + 1)],
+                                identity[:],
+                                start=term is terms[c][0],
+                                stop=term is terms[c][-1],
+                                is_transpose=True,
+                            )
                 for t in range(t0, t0 + per_bank):
                     nc.scalar.activation(
                         root[:, t, :], bank[:, t - t0, :], ACT.Abs_reciprocal_sqrt, scale=gain_inv[:, c, t : t + 1]

@@ -26,7 +26,10 @@ TILES = HALF // P
 OUT_TILES = N // P
 LIST_COLUMNS = HALF // 16
 NEIGHBOURS = 2
-SPARE = 24
+RAISED = 16
+ROUND = 256
+CHUNKS = (2, 2, 2, 1, 1)
+ROOTS = 4
 LIVE = 100
 TURN_BANKS = 5
 
@@ -65,58 +68,61 @@ def tile_list_partner_invitation_scores_kernel(
         gain_inv = held("gain_inv", [P, 2, PACK], F32)
         clinic_t = held("clinic_t", [P, OUT_TILES], F32)
         identity = held("identity", [P, P], F32)
-        partner_planes = [held("partner_planes%d" % a, [P, S], U8) for a in range(2)]
-        case_planes = [held("case_planes%d" % a, [P, S], U8) for a in range(2)]
+        lowered = {name: held(name + "_lowered", [P, S], U8) for name in ("partner", "case")}
 
-        for q in range(QUADRANTS):
-            engine = nc.vector if q < QUADRANTS // 2 else nc.gpsimd
-            engine.memset(table_scales[32 * q : 32 * q + SPARE, :].bitcast(I32), 0)
+        nc.gpsimd.memset(table_scales[:].bitcast(I32), 0)
         nc.vector.memset(w2_planes[:].bitcast(I32), 0)
-        for plane in partner_planes + case_planes:
+        for plane in lowered.values():
             nc.vector.memset(plane[96:P, :].bitcast(I32), 0)
         nc.vector.memset(w3_planes[:].bitcast(I32), 0)
         make_identity(nc, identity[:])
 
         nc.sync.dma_start(partner_list[:], offs2)
-        for q in range(QUADRANTS):
+        nc.sync.dma_start(gain_t[:], gain.rearrange("(c p t) -> p c t", c=2, t=PACK))
+        for r in range(4):
             nc.sync.dma_start(
-                table_scales[32 * q + SPARE : 32 * (q + 1), :].bitcast(I32),
-                tab_scales[:, 4 * q : 4 * q + 4, :].bitcast(I32),
+                table_scales[r:P:RAISED, :].bitcast(I32),
+                tab_scales.rearrange("a (q r) t -> r q a t", r=4)[r].bitcast(I32),
             )
-        words_in = [tab_words[a].bitcast(I32) for a in range(2)]
-        for cols in (slice(0, T // 4), slice(T // 4, T // 2)):
-            nc.sync.dma_start(table[0][:].bitcast(I32)[:, cols], words_in[0][:, cols])
-        nc.sync.dma_start(table[1][:].bitcast(I32), words_in[1])
-        load_planes(w2_planes, w2_scales)
         w2_view = w2_words.rearrange("a p c i -> p a (c i)").bitcast(I32)
-        nc.sync.dma_start(w2_codes[0][:].bitcast(I32), w2_view[:, :, 0:HALF])
+        nc.sync.dma_start(table[0][:].bitcast(I32), tab_words[0].bitcast(I32))
+        nc.sync.dma_start(w2_codes[0][:, 0, :].bitcast(I32), w2_view[:, 0, 0:HALF])
+        load_planes(w2_planes, w2_scales)
+        nc.sync.dma_start(table[1][:].bitcast(I32), tab_words[1].bitcast(I32))
 
-        def gather_scales(name, offsets, planes, queue):
-            picked = held(name, [P, S], U8, tag="picked_scales")
+        def gather_scales(name, offsets):
+            picked = held(name + "_picked", [P, S], U8)
             nc.vector.tensor_copy(picked[:], table_scales[:].indirect(offsets[:]))
-            for a in range(2):
-                top = SPARE + 4 * a
-                queue.dma_start(planes[a][0:LIVE, :].bitcast(I32), picked[top : top + LIVE, :].bitcast(I32))
+            return [picked, lowered[name]]
 
-        def gather_words(name, offsets, h, tags=("", "")):
-            picked = [held("%s%d%d" % (name, h, a), [P, HALF], U16, tag=tags[a]) for a in range(2)]
+        def lower_scales(planes):
+            nc.sync.dma_start(planes[1][0:LIVE, :].bitcast(I32), planes[0][RAISED : RAISED + LIVE, :].bitcast(I32))
+
+        def gather_words(name, offsets, h, tag=""):
+            picked = held("%s%d" % (name, h), [P, 2, HALF], U16, tag=tag)
             for a in range(2):
                 columns = offsets[:, LIST_COLUMNS * h : LIST_COLUMNS * (h + 1)]
-                nc.vector.tensor_copy(picked[a][:], table[a][:].indirect(columns))
-            return picked
+                nc.vector.tensor_copy(picked[:, a, :], table[a][:].indirect(columns))
+            return [picked[:, a, :] for a in range(2)]
 
-        def quantise_w1(c, rounded_tags=("", ""), code_tags=("", "")):
+        def quantise_w1(first, width, rounded_tags=("", ""), code_tags=("", "", "", "")):
+            c, r0 = divmod(first, HALF)
             codes, scale_planes, rounded = [], [], []
             for a in range(2):
-                grouped = held("w1_grouped%d%d" % (c, a), [P, HALF, PACK], BF16, tag=rounded_tags[a])
-                nc.vector.tensor_copy(
-                    grouped[:].rearrange("p (n e) i -> p n i e", e=NEIGHBOURS),
-                    w1_raw[c][:, a, :, :].rearrange("p i (n e) -> p n i e", e=NEIGHBOURS),
-                )
+                grouped = held("w1_grouped%d_%d" % (first, a), [P, width, PACK], BF16, tag=rounded_tags[a])
+                for n0 in range(0, width, ROUND):
+                    nc.gpsimd.tensor_scalar(
+                        grouped[:, n0 : n0 + ROUND, :],
+                        w1_raw[c][a][:, :, r0 + n0 : r0 + n0 + ROUND].rearrange("p i n -> p n i"),
+                        1.0,
+                        0.0,
+                        ALU.mult,
+                        ALU.add,
+                    )
                 rounded.append(grouped)
             for a in range(2):
-                code = held("w1_codes%d%d" % (c, a), [P, HALF], U32, tag=code_tags[a])
-                plane = held("w1_planes%d%d" % (c, a), [P, HALF], U8)
+                code = held("w1_codes%d_%d" % (first, a), [P, width], U32, tag=code_tags[a])
+                plane = held("w1_planes%d_%d" % (first, a), [P, width], U8, tag=code_tags[a + 2])
                 nc.vector.quantize_mx(
                     out=code[:].bitcast(FP8X4), scales=plane[:], in_=rounded[a][:].rearrange("p n i -> p (n i)")
                 )
@@ -124,42 +130,52 @@ def tile_list_partner_invitation_scores_kernel(
                 scale_planes.append(plane[:])
             return codes, scale_planes
 
-        def first_stage(feature, h, words, word_planes, w_codes, w_planes):
-            for jt in range(TILES):
-                bank = bank_tile(TILES * h + jt, [P, HALF])
-                for a in range(2):
-                    nc.tensor.matmul_mx(
-                        out=bank[:],
-                        lhsT=words[a][:, P * jt : P * (jt + 1)].bitcast(FP4X4),
-                        lhsT_scale=word_planes[a][:, HALF * h + P * jt : HALF * h + P * (jt + 1)],
-                        rhs=w_codes[a].bitcast(FP8X4),
-                        rhs_scale=w_planes[a],
-                        start=(a == 0),
-                        stop=(a == 1),
-                    )
+        def first_stage(feature, h, words, word_planes, w_codes, w_planes, first_bank, r0=0, width=HALF, passes=(1, 0)):
+            per_bank = HALF // width
+            for j0 in range(0, TILES, per_bank):
+                bank = bank_tile(first_bank + j0 // per_bank, [P, per_bank, width])
+                for jt in range(j0, j0 + per_bank):
+                    for a in passes:
+                        nc.tensor.matmul_mx(
+                            out=bank[:, jt - j0, :],
+                            lhsT=words[a][:, P * jt : P * (jt + 1)].bitcast(FP4X4),
+                            lhsT_scale=word_planes[a][:, HALF * h + P * jt : HALF * h + P * (jt + 1)],
+                            rhs=w_codes[a].bitcast(FP8X4),
+                            rhs_scale=w_planes[a],
+                            start=(a == passes[0]),
+                            stop=(a == passes[1]),
+                        )
+                rows = slice(TILES * h + j0, TILES * h + j0 + per_bank)
                 nc.scalar.activation(
-                    feature[:, TILES * h + jt, :].rearrange("p (t m) -> p t m", t=PACK),
-                    bank[:].rearrange("p (m t) -> p t m", t=PACK),
+                    feature[:, rows, :].rearrange("p j (t m) -> p j t m", t=PACK)[
+                        :, :, :, r0 // PACK : (r0 + width) // PACK
+                    ],
+                    bank[:].rearrange("p j (m t) -> p j t m", t=PACK),
                     ACT.Exp,
                 )
 
-        gather_scales("partner_scales", partner_list, partner_planes, nc.scalar)
-        nc.sync.dma_start(case_list[:], offs)
+        partner_planes = gather_scales("partner", partner_list)
+        nc.sync.dma_start(w2_codes[0][:, 1, :].bitcast(I32), w2_view[:, 1, 0:HALF])
+        lower_scales(partner_planes)
         nc.sync.dma_start(w2_codes[1][:].bitcast(I32), w2_view[:, :, HALF : 2 * HALF])
+        nc.sync.dma_start(case_list[:], offs)
         rb = [held("rb%d" % c, [P, 2 * TILES, HALF], F32) for c in range(2)]
         ra = [held("ra%d" % c, [P, 2 * TILES, HALF], F32) for c in range(2)]
         partner_words = [gather_words("partner_words", partner_list, h) for h in range(2)]
-        w1_raw = [held("w1_raw%d" % c, [P, 2, PACK, HALF], F32) for c in range(2)]
+        w1_raw = [
+            [held("w1_raw%d%d" % (c, a), [P, PACK, HALF], F32, tag="") for a in range(2)]
+            for c in range(2)
+        ]
+        case_planes = gather_scales("case", case_list)
         for c in range(2):
             for a in range(2):
                 nc.sync.dma_start(
-                    w1_raw[c][:, a, :, :],
+                    w1_raw[c][a][:],
                     w1[PASS * a : PASS * (a + 1), HALF * c : HALF * (c + 1)].rearrange("(p i) r -> p i r", i=PACK),
                 )
-        gather_scales("case_scales", case_list, case_planes, nc.sync)
+        lower_scales(case_planes)
         nc.sync.dma_start(w3_codes[:].bitcast(I32), w3_words.rearrange("a p b -> p a b").bitcast(I32))
         load_planes(w3_planes, w3_scales)
-        nc.sync.dma_start(gain_t[:], gain.rearrange("(c p t) -> p c t", c=2, t=PACK))
         with nc.allow_non_contiguous_dma(reason="one offset a partition"):
             nc.sync.dma_start(clinic_t[:], clinic.rearrange("(n p) -> p n", p=P))
 
@@ -172,28 +188,35 @@ def tile_list_partner_invitation_scores_kernel(
                     partner_planes,
                     [w2_codes[c][:, a, :] for a in range(2)],
                     [w2_planes[:, a, HALF * c : HALF * (c + 1)] for a in range(2)],
+                    first_bank=TILES * h,
+                    passes=(0, 1) if (c, h) == (0, 0) else (1, 0),
                 )
 
         rounded_tags = ("rounded0", "rounded1")
         case_words = [gather_words("case_words", case_list, 0)]
-        w_codes, w_planes = quantise_w1(0, rounded_tags=rounded_tags)
-        case_words.append(gather_words("case_words", case_list, 1, tags=rounded_tags))
+        w_codes, w_planes = quantise_w1(0, HALF, rounded_tags=rounded_tags)
+        case_words.append(gather_words("case_words", case_list, 1))
         for h in range(2):
-            first_stage(ra[0], h, case_words[h], case_planes, w_codes, w_planes)
-        w_codes, w_planes = quantise_w1(1, code_tags=("root0", "root1"))
-        for h in range(2):
-            first_stage(ra[1], h, case_words[h], case_planes, w_codes, w_planes)
+            first_stage(ra[0], h, case_words[h], case_planes, w_codes, w_planes, TILES * h)
+        piece = HALF // 2
+        for g in range(2):
+            w_codes, w_planes = quantise_w1(
+                HALF + piece * g, piece, code_tags=("root0", "root1", "root2", "root3") if g else ("", "", "", "")
+            )
+            for h in range(2):
+                first_stage(ra[1], h, case_words[h], case_planes, w_codes, w_planes, TILES * g + 2 * h, piece * g, piece)
         nc.vector.reciprocal(gain_inv[:], gain_t[:])
 
-        total = held("total", [P, 2 * TILES, HALF], F32, tag="w1_raw1")
-        for h in range(2):
-            rows = slice(TILES * h, TILES * (h + 1))
-            nc.vector.tensor_tensor(total[:, rows, :], ra[0][:, rows, :], rb[0][:, rows, :], ALU.add)
-        terms = [[total], [rb[1], ra[1]]]
+        totals = [held("total%d" % c, [P, 2 * TILES, HALF], F32, tag="w1_raw1%d" % (1 - c)) for c in range(2)]
+        for c in range(2):
+            for h in range(2):
+                rows = slice(TILES * h, TILES * (h + 1))
+                nc.vector.tensor_tensor(totals[c][:, rows, :], ra[c][:, rows, :], rb[c][:, rows, :], ALU.add)
+        terms = [[total] for total in totals]
 
-        def make_h(first, tiles, c, turn):
+        def make_root(step, first, tiles, c, turn):
             width = P * tiles
-            root = held("root%d%d" % (first, c), [P, PACK, width], F32, tag="root%d" % c)
+            root = held("root_%d" % step, [P, PACK, width], F32, tag="root%d" % (step % ROOTS))
             per_bank = HALF // width
             for t0 in range(0, PACK, per_bank):
                 bank = bank_tile((turn + t0 // per_bank) % TURN_BANKS, [P, per_bank, width])
@@ -212,45 +235,55 @@ def tile_list_partner_invitation_scores_kernel(
                     nc.scalar.activation(
                         root[:, t, :], bank[:, t - t0, :], ACT.Abs_reciprocal_sqrt, scale=gain_inv[:, c, t : t + 1]
                     )
+            return root
+
+        def square(root, width):
             grouped = ring.tile([P, width, PACK], BF16, name="h_grouped", align_bytes=64)
             y = root[:].rearrange("p t (n e) -> p n t e", e=NEIGHBOURS)
             nc.vector.tensor_tensor(grouped[:].rearrange("p (n e) t -> p n t e", e=NEIGHBOURS), y, y, ALU.mult)
-            code = held("h_codes%d%d" % (first, c), [P, width], U32)
-            plane = held("h_planes%d%d" % (first, c), [P, width], U8)
+            return grouped
+
+        def quantise_h(step, grouped, width):
+            code = held("h_codes%d" % step, [P, width], U32)
+            plane = held("h_planes%d" % step, [P, width], U8)
             nc.vector.quantize_mx(
                 out=code[:].bitcast(FP8X4), scales=plane[:], in_=grouped[:].rearrange("p n t -> p (n t)")
             )
             return code, plane
 
-        def second_stage(first, tiles, operands, first_bank, on_vector=()):
+        def second_stage(first, tiles, operands, first_bank, last):
             width = P * tiles
-            step = HALF if width == HALF else P
             banks = [bank_tile(first_bank + n, [P, width]) for n in range(OUT_TILES)]
             for c in range(2):
                 code, plane = operands[c]
                 for n in range(OUT_TILES):
-                    for j0 in range(0, width, step):
-                        nc.tensor.matmul_mx(
-                            out=banks[n][:, j0 : j0 + step],
-                            lhsT=w3_codes[:, c, 2 * P * n : 2 * P * (n + 1)].bitcast(FP4X4),
-                            lhsT_scale=w3_planes[:, c, P * n : P * (n + 1)],
-                            rhs=code[:, j0 : j0 + step].bitcast(FP8X4),
-                            rhs_scale=plane[:, j0 : j0 + step],
-                            start=(c == 0 and j0 == 0),
-                            stop=(c == 1 and j0 + step == width),
-                        )
+                    nc.tensor.matmul_mx(
+                        out=banks[n][:],
+                        lhsT=w3_codes[:, c, 2 * P * n : 2 * P * (n + 1)].bitcast(FP4X4),
+                        lhsT_scale=w3_planes[:, c, P * n : P * (n + 1)],
+                        rhs=code[:].bitcast(FP8X4),
+                        rhs_scale=plane[:],
+                        start=(c == 0),
+                        stop=(c == 1),
+                    )
             for n in range(OUT_TILES):
                 scores = held("scores%d%d" % (first, n), [P, width], F32)
-                if n in on_vector:
+                if last and n == 1:
                     nc.vector.tensor_scalar(scores[:], banks[n][:], clinic_t[:, n : n + 1], None, ALU.add)
                 else:
                     nc.scalar.activation(scores[:], banks[n][:], ACT.Identity, bias=clinic_t[:, n : n + 1])
                 nc.sync.dma_start(out[P * n : P * (n + 1), P * first : P * first + width], scores[:])
 
-        head = [make_h(0, 2, c, turn=2 * c) for c in range(2)]
-        middle = [make_h(2, 4, 0, turn=4)]
-        second_stage(0, 2, head, TURN_BANKS)
-        middle.append(make_h(2, 4, 1, turn=8))
-        tail = [make_h(6, 2, c, turn=12 + 2 * c) for c in range(2)]
-        second_stage(2, 4, middle, TURN_BANKS)
-        second_stage(6, 2, tail, 16 % TURN_BANKS, on_vector=(1,))
+        first, turn, waiting = 0, 0, None
+        for index, tiles in enumerate(CHUNKS):
+            made = []
+            for c in range(2):
+                step = 2 * index + c
+                root = make_root(step, first, tiles, c, turn)
+                made.append(quantise_h(step, square(root, P * tiles), P * tiles))
+                turn = turn + tiles
+            if waiting is not None:
+                second_stage(*waiting, TURN_BANKS, False)
+            waiting = (first, tiles, made)
+            first = first + tiles
+        second_stage(*waiting, turn % TURN_BANKS if turn % TURN_BANKS + OUT_TILES <= TURN_BANKS else 0, True)

@@ -40,7 +40,7 @@ def tile_list_partner_invitation_scores_kernel(
     nc = tc.nc
     with ExitStack() as ctx:
         keep = ctx.enter_context(tc.tile_pool(name="keep", bufs=1))
-        ring = ctx.enter_context(tc.tile_pool(name="ring", bufs=2))
+        ring = ctx.enter_context(tc.tile_pool(name="ring", bufs=3))
         psum = ctx.enter_context(tc.psum_pool(name="psum", bufs=1))
 
         def held(name, shape, dtype, tag=""):
@@ -157,7 +157,6 @@ def tile_list_partner_invitation_scores_kernel(
         partner_planes = gather_scales("partner", partner_list)
         nc.sync.dma_start(w2_codes[0][:, 1, :].bitcast(I32), w2_view[:, 1, 0:HALF])
         lower_scales(partner_planes)
-        nc.sync.dma_start(w2_codes[1][:].bitcast(I32), w2_view[:, :, HALF : 2 * HALF])
         nc.sync.dma_start(case_list[:], offs)
         rb = [held("rb%d" % c, [P, 2 * TILES, HALF], F32) for c in range(2)]
         ra = [held("ra%d" % c, [P, 2 * TILES, HALF], F32) for c in range(2)]
@@ -169,11 +168,14 @@ def tile_list_partner_invitation_scores_kernel(
         case_planes = gather_scales("case", case_list)
         for c in range(2):
             for a in range(2):
+                if (c, a) == (1, 0):
+                    lower_scales(case_planes)
+                if (c, a) == (0, 1):
+                    nc.sync.dma_start(w2_codes[1][:].bitcast(I32), w2_view[:, :, HALF : 2 * HALF])
                 nc.sync.dma_start(
                     w1_raw[c][a][:],
                     w1[PASS * a : PASS * (a + 1), HALF * c : HALF * (c + 1)].rearrange("(p i) r -> p i r", i=PACK),
                 )
-        lower_scales(case_planes)
         nc.sync.dma_start(w3_codes[:].bitcast(I32), w3_words.rearrange("a p b -> p a b").bitcast(I32))
         load_planes(w3_planes, w3_scales)
         with nc.allow_non_contiguous_dma(reason="one offset a partition"):
@@ -274,16 +276,15 @@ def tile_list_partner_invitation_scores_kernel(
                     nc.scalar.activation(scores[:], banks[n][:], ACT.Identity, bias=clinic_t[:, n : n + 1])
                 nc.sync.dma_start(out[P * n : P * (n + 1), P * first : P * first + width], scores[:])
 
-        first, turn, waiting = 0, 0, None
-        for index, tiles in enumerate(CHUNKS):
-            made = []
-            for c in range(2):
-                step = 2 * index + c
-                root = make_root(step, first, tiles, c, turn)
-                made.append(quantise_h(step, square(root, P * tiles), P * tiles))
-                turn = turn + tiles
-            if waiting is not None:
-                second_stage(*waiting, TURN_BANKS, False)
-            waiting = (first, tiles, made)
-            first = first + tiles
-        second_stage(*waiting, turn % TURN_BANKS if turn % TURN_BANKS + OUT_TILES <= TURN_BANKS else 0, True)
+        starts = [sum(CHUNKS[:index]) for index in range(len(CHUNKS))]
+        steps = [(starts[index], tiles, c) for index, tiles in enumerate(CHUNKS) for c in range(2)]
+        squared, made, turn = [], [], 0
+        for step, (first, tiles, c) in enumerate(steps):
+            squared.append(square(make_root(step, first, tiles, c, turn), P * tiles))
+            turn = turn + tiles
+            if step > 0:
+                made.append(quantise_h(step - 1, squared[step - 1], P * steps[step - 1][1]))
+            if step > 1 and c == 1:
+                second_stage(*steps[step - 2][:2], made[step - 3 : step - 1], TURN_BANKS, False)
+        made.append(quantise_h(len(steps) - 1, squared[-1], P * CHUNKS[-1]))
+        second_stage(*steps[-1][:2], made[-2:], turn % TURN_BANKS, True)

@@ -1,3 +1,4 @@
+import math
 from contextlib import ExitStack
 
 import concourse.mybir as mybir
@@ -27,7 +28,8 @@ OUT_TILES = N // P
 LIST_COLUMNS = HALF // 16
 NEIGHBOURS = 2
 RAISED = 16
-ROUND = 256
+ROUND = 1024
+TURNED, DEALT = 0, 1
 CHUNKS = (2, 2, 2, 1, 1)
 ROOTS = 4
 LIVE = 100
@@ -105,73 +107,71 @@ def tile_list_partner_invitation_scores_kernel(
                 nc.vector.tensor_copy(picked[:, a, :], table[a][:].indirect(columns))
             return [picked[:, a, :] for a in range(2)]
 
-        def quantise_w1(first, width, rounded_tags=("", ""), code_tags=("", "", "", "")):
-            c, r0 = divmod(first, HALF)
-            codes, scale_planes, rounded = [], [], []
-            for a in range(2):
-                grouped = held("w1_grouped%d_%d" % (first, a), [P, width, PACK], BF16, tag=rounded_tags[a])
-                for n0 in range(0, width, ROUND):
-                    nc.gpsimd.tensor_scalar(
-                        grouped[:, n0 : n0 + ROUND, :],
-                        w1_raw[c][a][:, :, r0 + n0 : r0 + n0 + ROUND].rearrange("p i n -> p n i"),
-                        1.0,
-                        0.0,
-                        ALU.mult,
-                        ALU.add,
-                    )
-                rounded.append(grouped)
-            for a in range(2):
-                code = held("w1_codes%d_%d" % (first, a), [P, width], U32, tag=code_tags[a])
-                plane = held("w1_planes%d_%d" % (first, a), [P, width], U8, tag=code_tags[a + 2])
-                nc.vector.quantize_mx(
-                    out=code[:].bitcast(FP8X4), scales=plane[:], in_=rounded[a][:].rearrange("p n i -> p (n i)")
-                )
-                codes.append(code[:])
-                scale_planes.append(plane[:])
-            return codes, scale_planes
+        def round_on_gpsimd(rounded, raw):
+            step = ROUND * rounded.shape[1] // math.prod(rounded.shape[1:])
+            for n0 in range(0, rounded.shape[1], step):
+                piece = slice(n0, n0 + step)
+                nc.gpsimd.tensor_scalar(rounded[:, piece], raw[:, piece], 1.0, 0.0, ALU.mult, ALU.add)
 
-        def first_stage(feature, h, words, word_planes, w_codes, w_planes, first_bank, r0=0, width=HALF, passes=(1, 0)):
+        def quantise(name, values, width, tags=("", "")):
+            code = held(name + "_codes", [P, width], U32, tag=tags[0])
+            plane = held(name + "_plane", [P, width], U8, tag=tags[1])
+            nc.vector.quantize_mx(out=code[:].bitcast(FP8X4), scales=plane[:], in_=values)
+            return code[:], plane[:]
+
+        def product(out_ap, stationary, moving, passes):
+            for a in passes:
+                nc.tensor.matmul_mx(
+                    out=out_ap,
+                    lhsT=stationary[a][0],
+                    lhsT_scale=stationary[a][1],
+                    rhs=moving[a][0],
+                    rhs_scale=moving[a][1],
+                    start=(a == passes[0]),
+                    stop=(a == passes[1]),
+                )
+
+        def picked_columns(words, planes, h, j0, width):
+            return [
+                (words[a][:, j0 : j0 + width].bitcast(FP4X4), planes[a][:, HALF * h + j0 : HALF * h + j0 + width])
+                for a in range(2)
+            ]
+
+        def weight_columns(weight, r0, width):
+            return [(code[:, r0 : r0 + width].bitcast(FP8X4), plane[:, r0 : r0 + width]) for code, plane in weight]
+
+        def turned_stage(feature, h, words, planes, weight, first_bank, width=HALF, passes=(1, 0)):
             per_bank = HALF // width
             for j0 in range(0, TILES, per_bank):
                 bank = bank_tile(first_bank + j0 // per_bank, [P, per_bank, width])
                 for jt in range(j0, j0 + per_bank):
-                    for a in passes:
-                        nc.tensor.matmul_mx(
-                            out=bank[:, jt - j0, :],
-                            lhsT=words[a][:, P * jt : P * (jt + 1)].bitcast(FP4X4),
-                            lhsT_scale=word_planes[a][:, HALF * h + P * jt : HALF * h + P * (jt + 1)],
-                            rhs=w_codes[a].bitcast(FP8X4),
-                            rhs_scale=w_planes[a],
-                            start=(a == passes[0]),
-                            stop=(a == passes[1]),
-                        )
+                    stationary = picked_columns(words, planes, h, P * jt, P)
+                    product(bank[:, jt - j0, :], stationary, weight_columns(weight, 0, width), passes)
                 rows = slice(TILES * h + j0, TILES * h + j0 + per_bank)
                 nc.scalar.activation(
-                    feature[:, rows, :].rearrange("p j (t m) -> p j t m", t=PACK)[
-                        :, :, :, r0 // PACK : (r0 + width) // PACK
-                    ],
+                    feature[:, rows, :].rearrange("p j (t m) -> p j t m", t=PACK),
                     bank[:].rearrange("p j (m t) -> p j t m", t=PACK),
                     ACT.Exp,
                 )
 
+        def dealt_stage(feature, h, words, planes, weight):
+            for t in range(PACK):
+                bank = bank_tile(TILES * h + t, [P, HALF])
+                product(bank[:], weight_columns(weight, P * t, P), picked_columns(words, planes, h, 0, HALF), (1, 0))
+                nc.scalar.activation(feature[:, t, :], bank[:], ACT.Exp)
+
         partner_planes = gather_scales("partner", partner_list)
         nc.sync.dma_start(w2_codes[0][:, 1, :].bitcast(I32), w2_view[:, 1, 0:HALF])
         lower_scales(partner_planes)
+        nc.sync.dma_start(w2_codes[1][:].bitcast(I32), w2_view[:, :, HALF : 2 * HALF])
         nc.sync.dma_start(case_list[:], offs)
-        rb = [held("rb%d" % c, [P, 2 * TILES, HALF], F32) for c in range(2)]
-        ra = [held("ra%d" % c, [P, 2 * TILES, HALF], F32) for c in range(2)]
         partner_words = [gather_words("partner_words", partner_list, h) for h in range(2)]
-        w1_raw = [
-            [held("w1_raw%d%d" % (c, a), [P, PACK, HALF], F32, tag="") for a in range(2)]
-            for c in range(2)
-        ]
         case_planes = gather_scales("case", case_list)
-        for c in range(2):
+        w1_raw = [[held("w1_raw%d%d" % (c, a), [P, PACK, HALF], F32) for a in range(2)] for c in range(2)]
+        for c in (DEALT, TURNED):
+            if c == TURNED:
+                lower_scales(case_planes)
             for a in range(2):
-                if (c, a) == (1, 0):
-                    lower_scales(case_planes)
-                if (c, a) == (0, 1):
-                    nc.sync.dma_start(w2_codes[1][:].bitcast(I32), w2_view[:, :, HALF : 2 * HALF])
                 nc.sync.dma_start(
                     w1_raw[c][a][:],
                     w1[PASS * a : PASS * (a + 1), HALF * c : HALF * (c + 1)].rearrange("(p i) r -> p i r", i=PACK),
@@ -181,92 +181,127 @@ def tile_list_partner_invitation_scores_kernel(
         with nc.allow_non_contiguous_dma(reason="one offset a partition"):
             nc.sync.dma_start(clinic_t[:], clinic.rearrange("(n p) -> p n", p=P))
 
-        for c in range(2):
-            for h in range(2):
-                first_stage(
-                    rb[c],
-                    h,
-                    partner_words[h],
-                    partner_planes,
-                    [w2_codes[c][:, a, :] for a in range(2)],
-                    [w2_planes[:, a, HALF * c : HALF * (c + 1)] for a in range(2)],
-                    first_bank=TILES * h,
-                    passes=(0, 1) if (c, h) == (0, 0) else (1, 0),
-                )
-
-        rounded_tags = ("rounded0", "rounded1")
-        case_words = [gather_words("case_words", case_list, 0)]
-        w_codes, w_planes = quantise_w1(0, HALF, rounded_tags=rounded_tags)
-        case_words.append(gather_words("case_words", case_list, 1))
+        rb_turned = held("rb_turned", [P, 2 * TILES, HALF], F32)
+        w2_turned = [(w2_codes[TURNED][:, a, :], w2_planes[:, a, 0:HALF]) for a in range(2)]
         for h in range(2):
-            first_stage(ra[0], h, case_words[h], case_planes, w_codes, w_planes, TILES * h)
-        piece = HALF // 2
-        for g in range(2):
-            w_codes, w_planes = quantise_w1(
-                HALF + piece * g, piece, code_tags=("root0", "root1", "root2", "root3") if g else ("", "", "", "")
+            passes = (1, 0) if h else (0, 1)
+            turned_stage(rb_turned, h, partner_words[h], partner_planes, w2_turned, TILES * h, passes=passes)
+
+        dealt_codes = held("dealt_codes", [P, 2, HALF], U32)
+        dealt_planes = held("dealt_planes", [P, 2, HALF], U8)
+        for a in range(2):
+            nc.gpsimd.tensor_copy(
+                dealt_codes[:, a, :].rearrange("p (t n e) -> p n t e", t=PACK, e=PACK),
+                w2_codes[DEALT][:, a, :].rearrange("p (n e t) -> p n t e", t=PACK, e=PACK),
             )
+        nc.vector.tensor_copy(
+            dealt_planes[:].rearrange("p a (t m) -> p a t m", t=PACK),
+            w2_planes[:, :, HALF : 2 * HALF].rearrange("p a (m t) -> p a t m", t=PACK),
+        )
+        w2_dealt = [(dealt_codes[:, a, :], dealt_planes[:, a, :]) for a in range(2)]
+        rb_dealt = [held("rb_dealt%d" % h, [P, PACK, HALF], F32) for h in range(2)]
+        for h in range(2):
+            dealt_stage(rb_dealt[h], h, partner_words[h], partner_planes, w2_dealt)
+
+        case_words = [gather_words("case_words", case_list, 0)]
+        rounded = [held("rounded_dealt%d" % a, [P, PACK, P, PACK], BF16) for a in range(2)]
+        for a in range(2):
+            round_on_gpsimd(
+                rounded[a][:].rearrange("p t m i -> p m t i"),
+                w1_raw[DEALT][a][:].rearrange("p i (m t) -> p m t i", t=PACK),
+            )
+        w1_dealt = [
+            quantise("w1_dealt%d" % a, rounded[a][:].rearrange("p t m i -> p (t m i)"), HALF) for a in range(2)
+        ]
+        case_words.append(gather_words("case_words", case_list, 1))
+        ra_dealt = [held("ra_dealt%d" % h, [P, PACK, HALF], F32) for h in range(2)]
+        for h in range(2):
+            dealt_stage(ra_dealt[h], h, case_words[h], case_planes, w1_dealt)
+
+        piece = HALF // 2
+        ra_turned = [held("ra_turned%d" % g, [P, 2 * TILES, piece], F32) for g in range(2)]
+        for g in range(2):
+            rounded = [held("rounded_turned%d%d" % (g, a), [P, piece, PACK], BF16) for a in range(2)]
+            for a in range(2):
+                raw = w1_raw[TURNED][a][:, :, piece * g : piece * (g + 1)]
+                if g == 0:
+                    round_on_gpsimd(rounded[a][:], raw.rearrange("p i n -> p n i"))
+                else:
+                    nc.vector.tensor_copy(
+                        rounded[a][:].rearrange("p (n e) i -> p n i e", e=NEIGHBOURS),
+                        raw.rearrange("p i (n e) -> p n i e", e=NEIGHBOURS),
+                    )
+            weight = [
+                quantise(
+                    "w1_turned%d%d" % (g, a),
+                    rounded[a][:].rearrange("p n i -> p (n i)"),
+                    piece,
+                    tags=("root%d" % a, "root%d" % (a + 2)) if g else ("", ""),
+                )
+                for a in range(2)
+            ]
             for h in range(2):
-                first_stage(ra[1], h, case_words[h], case_planes, w_codes, w_planes, TILES * g + 2 * h, piece * g, piece)
+                turned_stage(ra_turned[g], h, case_words[h], case_planes, weight, TILES * g + 2 * h, piece)
         nc.vector.reciprocal(gain_inv[:], gain_t[:])
 
-        totals = [held("total%d" % c, [P, 2 * TILES, HALF], F32, tag="w1_raw1%d" % (1 - c)) for c in range(2)]
-        for c in range(2):
-            for h in range(2):
-                rows = slice(TILES * h, TILES * (h + 1))
-                nc.vector.tensor_tensor(totals[c][:, rows, :], ra[c][:, rows, :], rb[c][:, rows, :], ALU.add)
-        terms = [[total] for total in totals]
+        total_dealt = [held("total_dealt%d" % h, [P, PACK, HALF], F32, tag="w1_raw%d%d" % (TURNED, 1 - h)) for h in range(2)]
+        for h in range(2):
+            nc.vector.tensor_tensor(total_dealt[h][:], ra_dealt[h][:], rb_dealt[h][:], ALU.add)
+        total_turned = held("total_turned", [P, 2 * TILES, HALF], F32)
+        for g, rows in ((0, slice(0, 2 * TILES)), (1, slice(0, TILES)), (1, slice(TILES, 2 * TILES))):
+            columns = slice(P // 2 * g, P // 2 * (g + 1))
+            total, partner = [
+                x[:, rows, :].rearrange("p j (t m) -> p j t m", t=PACK)[:, :, :, columns]
+                for x in (total_turned, rb_turned)
+            ]
+            case = ra_turned[g][:, rows, :].rearrange("p j (t m) -> p j t m", t=PACK)
+            nc.vector.tensor_tensor(total, case, partner, ALU.add)
 
         def make_root(step, first, tiles, c, turn):
             width = P * tiles
             root = held("root_%d" % step, [P, PACK, width], F32, tag="root%d" % (step % ROOTS))
+
+            def root_of(t, values):
+                nc.scalar.activation(root[:, t, :], values, ACT.Abs_reciprocal_sqrt, scale=gain_inv[:, c, t : t + 1])
+
+            if c == DEALT:
+                h, jt = divmod(first, TILES)
+                for t in range(PACK):
+                    root_of(t, total_dealt[h][:, t, P * jt : P * jt + width])
+                return root
             per_bank = HALF // width
             for t0 in range(0, PACK, per_bank):
                 bank = bank_tile((turn + t0 // per_bank) % TURN_BANKS, [P, per_bank, width])
                 for t in range(t0, t0 + per_bank):
                     for jt in range(tiles):
-                        for term in terms[c]:
-                            nc.tensor.matmul(
-                                bank[:, t - t0, P * jt : P * (jt + 1)],
-                                term[:, first + jt, P * t : P * (t + 1)],
-                                identity[:],
-                                start=term is terms[c][0],
-                                stop=term is terms[c][-1],
-                                is_transpose=True,
-                            )
+                        nc.tensor.transpose(
+                            bank[:, t - t0, P * jt : P * (jt + 1)],
+                            total_turned[:, first + jt, P * t : P * (t + 1)],
+                            identity[:],
+                        )
                 for t in range(t0, t0 + per_bank):
-                    nc.scalar.activation(
-                        root[:, t, :], bank[:, t - t0, :], ACT.Abs_reciprocal_sqrt, scale=gain_inv[:, c, t : t + 1]
-                    )
+                    root_of(t, bank[:, t - t0, :])
             return root
 
         def square(root, width):
             grouped = ring.tile([P, width, PACK], BF16, name="h_grouped", align_bytes=64)
             y = root[:].rearrange("p t (n e) -> p n t e", e=NEIGHBOURS)
             nc.vector.tensor_tensor(grouped[:].rearrange("p (n e) t -> p n t e", e=NEIGHBOURS), y, y, ALU.mult)
-            return grouped
+            return grouped[:].rearrange("p n t -> p (n t)")
 
-        def quantise_h(step, grouped, width):
-            code = held("h_codes%d" % step, [P, width], U32)
-            plane = held("h_planes%d" % step, [P, width], U8)
-            nc.vector.quantize_mx(
-                out=code[:].bitcast(FP8X4), scales=plane[:], in_=grouped[:].rearrange("p n t -> p (n t)")
-            )
-            return code, plane
-
-        def second_stage(first, tiles, operands, first_bank, last):
+        def second_stage(first, tiles, operands, indices, last):
             width = P * tiles
-            banks = [bank_tile(first_bank + n, [P, width]) for n in range(OUT_TILES)]
-            for c in range(2):
-                code, plane = operands[c]
+            banks = [bank_tile(index, [P, width]) for index in indices]
+            for c, (code, plane) in zip((DEALT, TURNED), operands):
                 for n in range(OUT_TILES):
                     nc.tensor.matmul_mx(
                         out=banks[n][:],
                         lhsT=w3_codes[:, c, 2 * P * n : 2 * P * (n + 1)].bitcast(FP4X4),
                         lhsT_scale=w3_planes[:, c, P * n : P * (n + 1)],
-                        rhs=code[:].bitcast(FP8X4),
-                        rhs_scale=plane[:],
-                        start=(c == 0),
-                        stop=(c == 1),
+                        rhs=code.bitcast(FP8X4),
+                        rhs_scale=plane,
+                        start=(c == DEALT),
+                        stop=(c == TURNED),
                     )
             for n in range(OUT_TILES):
                 scores = held("scores%d%d" % (first, n), [P, width], F32)
@@ -277,14 +312,15 @@ def tile_list_partner_invitation_scores_kernel(
                 nc.sync.dma_start(out[P * n : P * (n + 1), P * first : P * first + width], scores[:])
 
         starts = [sum(CHUNKS[:index]) for index in range(len(CHUNKS))]
-        steps = [(starts[index], tiles, c) for index, tiles in enumerate(CHUNKS) for c in range(2)]
+        steps = [(starts[index], tiles, c) for index, tiles in enumerate(CHUNKS) for c in (DEALT, TURNED)]
         squared, made, turn = [], [], 0
         for step, (first, tiles, c) in enumerate(steps):
             squared.append(square(make_root(step, first, tiles, c, turn), P * tiles))
-            turn = turn + tiles
+            if c == TURNED:
+                turn = turn + tiles
             if step > 0:
-                made.append(quantise_h(step - 1, squared[step - 1], P * steps[step - 1][1]))
-            if step > 1 and c == 1:
-                second_stage(*steps[step - 2][:2], made[step - 3 : step - 1], TURN_BANKS, False)
-        made.append(quantise_h(len(steps) - 1, squared[-1], P * CHUNKS[-1]))
-        second_stage(*steps[-1][:2], made[-2:], turn % TURN_BANKS, True)
+                made.append(quantise("h%d" % (step - 1), squared[step - 1], P * steps[step - 1][1]))
+            if step > 1 and c == TURNED:
+                second_stage(*steps[step - 2][:2], made[step - 3 : step - 1], range(TURN_BANKS, TURN_BANKS + OUT_TILES), False)
+        made.append(quantise("h%d" % (len(steps) - 1), squared[-1], P * CHUNKS[-1]))
+        second_stage(*steps[-1][:2], made[-2:], [(turn + n) % TURN_BANKS for n in range(OUT_TILES)], True)

@@ -140,7 +140,7 @@ def tile_list_partner_invitation_scores_kernel(
         def weight_columns(weight, r0, width):
             return [(code[:, r0 : r0 + width].bitcast(FP8X4), plane[:, r0 : r0 + width]) for code, plane in weight]
 
-        def turned_stage(feature, h, words, planes, weight, first_bank, width=HALF, passes=(1, 0)):
+        def turned_stage(feature, h, words, planes, weight, first_bank, r0=0, width=HALF, passes=(1, 0)):
             per_bank = HALF // width
             for j0 in range(0, TILES, per_bank):
                 bank = bank_tile(first_bank + j0 // per_bank, [P, per_bank, width])
@@ -149,7 +149,9 @@ def tile_list_partner_invitation_scores_kernel(
                     product(bank[:, jt - j0, :], stationary, weight_columns(weight, 0, width), passes)
                 rows = slice(TILES * h + j0, TILES * h + j0 + per_bank)
                 nc.scalar.activation(
-                    feature[:, rows, :].rearrange("p j (t m) -> p j t m", t=PACK),
+                    feature[:, rows, :].rearrange("p j (t m) -> p j t m", t=PACK)[
+                        :, :, :, r0 // PACK : (r0 + width) // PACK
+                    ],
                     bank[:].rearrange("p j (m t) -> p j t m", t=PACK),
                     ACT.Exp,
                 )
@@ -219,7 +221,7 @@ def tile_list_partner_invitation_scores_kernel(
             dealt_stage(ra_dealt[h], h, case_words[h], case_planes, w1_dealt)
 
         piece = HALF // 2
-        ra_turned = [held("ra_turned%d" % g, [P, 2 * TILES, piece], F32) for g in range(2)]
+        ra_turned = held("ra_turned", [P, 2 * TILES, HALF], F32)
         for g in range(2):
             rounded = [held("rounded_turned%d%d" % (g, a), [P, piece, PACK], BF16) for a in range(2)]
             for a in range(2):
@@ -241,21 +243,14 @@ def tile_list_partner_invitation_scores_kernel(
                 for a in range(2)
             ]
             for h in range(2):
-                turned_stage(ra_turned[g], h, case_words[h], case_planes, weight, TILES * g + 2 * h, piece)
+                turned_stage(ra_turned, h, case_words[h], case_planes, weight, TILES * g + 2 * h, piece * g, piece)
         nc.vector.reciprocal(gain_inv[:], gain_t[:])
 
         total_dealt = [held("total_dealt%d" % h, [P, PACK, HALF], F32, tag="w1_raw%d%d" % (TURNED, 1 - h)) for h in range(2)]
         for h in range(2):
             nc.vector.tensor_tensor(total_dealt[h][:], ra_dealt[h][:], rb_dealt[h][:], ALU.add)
-        total_turned = held("total_turned", [P, 2 * TILES, HALF], F32)
-        for g, rows in ((0, slice(0, 2 * TILES)), (1, slice(0, TILES)), (1, slice(TILES, 2 * TILES))):
-            columns = slice(P // 2 * g, P // 2 * (g + 1))
-            total, partner = [
-                x[:, rows, :].rearrange("p j (t m) -> p j t m", t=PACK)[:, :, :, columns]
-                for x in (total_turned, rb_turned)
-            ]
-            case = ra_turned[g][:, rows, :].rearrange("p j (t m) -> p j t m", t=PACK)
-            nc.vector.tensor_tensor(total, case, partner, ALU.add)
+        total_turned = held("total_turned", [P, TILES, HALF], F32)
+        nc.vector.tensor_tensor(total_turned[:], ra_turned[:, TILES:, :], rb_turned[:, TILES:, :], ALU.add)
 
         def make_root(step, first, tiles, c, turn):
             width = P * tiles
@@ -274,11 +269,19 @@ def tile_list_partner_invitation_scores_kernel(
                 bank = bank_tile((turn + t0 // per_bank) % TURN_BANKS, [P, per_bank, width])
                 for t in range(t0, t0 + per_bank):
                     for jt in range(tiles):
-                        nc.tensor.transpose(
-                            bank[:, t - t0, P * jt : P * (jt + 1)],
-                            total_turned[:, first + jt, P * t : P * (t + 1)],
-                            identity[:],
-                        )
+                        tile = first + jt
+                        terms = [rb_turned[:, tile, :], ra_turned[:, tile, :]]
+                        if tile >= TILES:
+                            terms = [total_turned[:, tile - TILES, :]]
+                        for index, term in enumerate(terms):
+                            nc.tensor.matmul(
+                                bank[:, t - t0, P * jt : P * (jt + 1)],
+                                term[:, P * t : P * (t + 1)],
+                                identity[:],
+                                start=(index == 0),
+                                stop=(index == len(terms) - 1),
+                                is_transpose=True,
+                            )
                 for t in range(t0, t0 + per_bank):
                     root_of(t, bank[:, t - t0, :])
             return root

@@ -208,14 +208,16 @@ def tile_list_partner_invitation_scores_kernel(
         case_words = [gather_words("case_words", case_list, 0)]
         rounded = [held("rounded_dealt%d" % a, [P, PACK, P, PACK], BF16) for a in range(2)]
         for a in range(2):
-            round_on_gpsimd(
-                rounded[a][:].rearrange("p t m i -> p m t i"),
-                w1_raw[DEALT][a][:].rearrange("p i (m t) -> p m t i", t=PACK),
-            )
+            values = rounded[a][:].rearrange("p t m i -> p m t i")
+            raw = w1_raw[DEALT][a][:].rearrange("p i (m t) -> p m t i", t=PACK)
+            shared = P // 2 if a else P
+            round_on_gpsimd(values[:, 0:shared], raw[:, 0:shared])
+            if shared < P:
+                nc.vector.tensor_copy(values[:, shared:P], raw[:, shared:P])
         w1_dealt = [
             quantise("w1_dealt%d" % a, rounded[a][:].rearrange("p t m i -> p (t m i)"), HALF) for a in range(2)
         ]
-        case_words.append(gather_words("case_words", case_list, 1))
+        case_words.append(gather_words("case_words", case_list, 1, tag="rounded_dealt1"))
         ra_dealt = [held("ra_dealt%d" % h, [P, PACK, HALF], F32) for h in range(2)]
         for h in range(2):
             dealt_stage(ra_dealt[h], h, case_words[h], case_planes, w1_dealt)
@@ -226,7 +228,7 @@ def tile_list_partner_invitation_scores_kernel(
             rounded = [held("rounded_turned%d%d" % (g, a), [P, piece, PACK], BF16) for a in range(2)]
             for a in range(2):
                 raw = w1_raw[TURNED][a][:, :, piece * g : piece * (g + 1)]
-                if g == 0:
+                if a == 0:
                     round_on_gpsimd(rounded[a][:], raw.rearrange("p i n -> p n i"))
                 else:
                     nc.vector.tensor_copy(

@@ -196,7 +196,7 @@ def tile_list_partner_invitation_scores_kernel(
                 dealt_codes[:, a, :].rearrange("p (t n e) -> p n t e", t=PACK, e=PACK),
                 w2_codes[DEALT][:, a, :].rearrange("p (n e t) -> p n t e", t=PACK, e=PACK),
             )
-        nc.vector.tensor_copy(
+        nc.gpsimd.tensor_copy(
             dealt_planes[:].rearrange("p a (t m) -> p a t m", t=PACK),
             w2_planes[:, :, HALF : 2 * HALF].rearrange("p a (m t) -> p a t m", t=PACK),
         )
@@ -210,10 +210,10 @@ def tile_list_partner_invitation_scores_kernel(
         for a in range(2):
             values = rounded[a][:].rearrange("p t m i -> p m t i")
             raw = w1_raw[DEALT][a][:].rearrange("p i (m t) -> p m t i", t=PACK)
-            shared = P // 2 if a else P
-            round_on_gpsimd(values[:, 0:shared], raw[:, 0:shared])
-            if shared < P:
-                nc.vector.tensor_copy(values[:, shared:P], raw[:, shared:P])
+            if a == 0:
+                round_on_gpsimd(values, raw)
+            else:
+                nc.vector.tensor_copy(values, raw)
         w1_dealt = [
             quantise("w1_dealt%d" % a, rounded[a][:].rearrange("p t m i -> p (t m i)"), HALF) for a in range(2)
         ]

@@ -51,9 +51,9 @@ def tile_list_partner_invitation_scores_kernel(
         def bank_tile(index, shape):
             return psum.tile(shape, F32, name="bank%d" % index, tag="bank%d" % index)
 
-        def load_planes(planes, scales):
+        def load_planes(queue, planes, scales):
             for q in range(QUADRANTS):
-                nc.sync.dma_start(
+                queue.dma_start(
                     planes[32 * q : 32 * q + 4, :, :].bitcast(I32),
                     scales[:, 4 * q : 4 * q + 4, :].rearrange("a r c -> r a c").bitcast(I32),
                 )
@@ -74,22 +74,21 @@ def tile_list_partner_invitation_scores_kernel(
 
         nc.gpsimd.memset(table_scales[:].bitcast(I32), 0)
         nc.vector.memset(w2_planes[:].bitcast(I32), 0)
+        load_planes(nc.gpsimd, w2_planes, w2_scales)
         for plane in lowered.values():
             nc.vector.memset(plane[96:P, :].bitcast(I32), 0)
         nc.vector.memset(w3_planes[:].bitcast(I32), 0)
         make_identity(nc, identity[:])
 
         nc.sync.dma_start(partner_list[:], offs2)
-        nc.sync.dma_start(gain_t[:], gain.rearrange("(c p t) -> p c t", c=2, t=PACK))
+        w2_view = w2_words.rearrange("a p c i -> p a (c i)").bitcast(I32)
+        nc.sync.dma_start(w2_codes[0][:, 0, :].bitcast(I32), w2_view[:, 0, 0:HALF])
         for r in range(4):
             nc.sync.dma_start(
                 table_scales[r:P:RAISED, :].bitcast(I32),
                 tab_scales.rearrange("a (q r) t -> r q a t", r=4)[r].bitcast(I32),
             )
-        w2_view = w2_words.rearrange("a p c i -> p a (c i)").bitcast(I32)
         nc.sync.dma_start(table[0][:].bitcast(I32), tab_words[0].bitcast(I32))
-        nc.sync.dma_start(w2_codes[0][:, 0, :].bitcast(I32), w2_view[:, 0, 0:HALF])
-        load_planes(w2_planes, w2_scales)
         nc.sync.dma_start(table[1][:].bitcast(I32), tab_words[1].bitcast(I32))
 
         def gather_scales(name, offsets):
@@ -97,8 +96,8 @@ def tile_list_partner_invitation_scores_kernel(
             nc.vector.tensor_copy(picked[:], table_scales[:].indirect(offsets[:]))
             return [picked, lowered[name]]
 
-        def lower_scales(planes):
-            nc.sync.dma_start(planes[1][0:LIVE, :].bitcast(I32), planes[0][RAISED : RAISED + LIVE, :].bitcast(I32))
+        def lower_scales(queue, planes):
+            queue.dma_start(planes[1][0:LIVE, :].bitcast(I32), planes[0][RAISED : RAISED + LIVE, :].bitcast(I32))
 
         def gather_words(name, offsets, h, tag=""):
             picked = held("%s%d" % (name, h), [P, 2, HALF], U16, tag=tag)
@@ -164,7 +163,7 @@ def tile_list_partner_invitation_scores_kernel(
 
         partner_planes = gather_scales("partner", partner_list)
         nc.sync.dma_start(w2_codes[0][:, 1, :].bitcast(I32), w2_view[:, 1, 0:HALF])
-        lower_scales(partner_planes)
+        lower_scales(nc.scalar, partner_planes)
         nc.sync.dma_start(w2_codes[1][:].bitcast(I32), w2_view[:, :, HALF : 2 * HALF])
         nc.sync.dma_start(case_list[:], offs)
         partner_words = [gather_words("partner_words", partner_list, h) for h in range(2)]
@@ -172,14 +171,15 @@ def tile_list_partner_invitation_scores_kernel(
         w1_raw = [[held("w1_raw%d%d" % (c, a), [P, PACK, HALF], F32) for a in range(2)] for c in range(2)]
         for c in (DEALT, TURNED):
             if c == TURNED:
-                lower_scales(case_planes)
+                lower_scales(nc.sync, case_planes)
             for a in range(2):
                 nc.sync.dma_start(
                     w1_raw[c][a][:],
                     w1[PASS * a : PASS * (a + 1), HALF * c : HALF * (c + 1)].rearrange("(p i) r -> p i r", i=PACK),
                 )
         nc.sync.dma_start(w3_codes[:].bitcast(I32), w3_words.rearrange("a p b -> p a b").bitcast(I32))
-        load_planes(w3_planes, w3_scales)
+        nc.sync.dma_start(gain_t[:], gain.rearrange("(c p t) -> p c t", c=2, t=PACK))
+        load_planes(nc.sync, w3_planes, w3_scales)
         with nc.allow_non_contiguous_dma(reason="one offset a partition"):
             nc.sync.dma_start(clinic_t[:], clinic.rearrange("(n p) -> p n", p=P))
 

@@ -43,10 +43,14 @@ def tile_list_partner_invitation_scores_kernel(
     with ExitStack() as ctx:
         keep = ctx.enter_context(tc.tile_pool(name="keep", bufs=1))
         ring = ctx.enter_context(tc.tile_pool(name="ring", bufs=3))
+        reused = ctx.enter_context(tc.tile_pool(name="reused", bufs=1))
         psum = ctx.enter_context(tc.psum_pool(name="psum", bufs=1))
 
         def held(name, shape, dtype, tag=""):
             return keep.tile(shape, dtype, name=name, tag=tag or name, align_bytes=64)
+
+        def placed(name, shape, dtype, offset):
+            return reused.tile(shape, dtype, name=name, align_bytes=64, offset=offset)
 
         def bank_tile(index, shape):
             return psum.tile(shape, F32, name="bank%d" % index, tag="bank%d" % index)
@@ -82,7 +86,7 @@ def tile_list_partner_invitation_scores_kernel(
 
         nc.sync.dma_start(partner_list[:], offs2)
         w2_view = w2_words.rearrange("a p c i -> p a (c i)").bitcast(I32)
-        nc.sync.dma_start(w2_codes[0][:, 0, :].bitcast(I32), w2_view[:, 0, 0:HALF])
+        nc.sync.dma_start(w2_codes[DEALT][:].bitcast(I32), w2_view[:, :, HALF : 2 * HALF])
         for r in range(4):
             nc.sync.dma_start(
                 table_scales[r:P:RAISED, :].bitcast(I32),
@@ -99,8 +103,7 @@ def tile_list_partner_invitation_scores_kernel(
         def lower_scales(queue, planes):
             queue.dma_start(planes[1][0:LIVE, :].bitcast(I32), planes[0][RAISED : RAISED + LIVE, :].bitcast(I32))
 
-        def gather_words(name, offsets, h, tag=""):
-            picked = held("%s%d" % (name, h), [P, 2, HALF], U16, tag=tag)
+        def gather_words(picked, offsets, h):
             for a in range(2):
                 columns = offsets[:, LIST_COLUMNS * h : LIST_COLUMNS * (h + 1)]
                 nc.vector.tensor_copy(picked[:, a, :], table[a][:].indirect(columns))
@@ -155,24 +158,34 @@ def tile_list_partner_invitation_scores_kernel(
                     ACT.Exp,
                 )
 
-        def dealt_stage(feature, h, words, planes, weight):
+        def dealt_stage(feature, h, words, planes, weight, passes=(1, 0)):
             for t in range(PACK):
                 bank = bank_tile(TILES * h + t, [P, HALF])
-                product(bank[:], weight_columns(weight, P * t, P), picked_columns(words, planes, h, 0, HALF), (1, 0))
+                product(bank[:], weight_columns(weight, P * t, P), picked_columns(words, planes, h, 0, HALF), passes)
                 nc.scalar.activation(feature[:, t, :], bank[:], ACT.Exp)
 
         partner_planes = gather_scales("partner", partner_list)
-        nc.sync.dma_start(w2_codes[0][:, 1, :].bitcast(I32), w2_view[:, 1, 0:HALF])
+        dealt_codes = held("dealt_codes", [P, 2, HALF], U32)
+        dealt_planes = held("dealt_planes", [P, 2, HALF], U8)
+        for a in range(2):
+            nc.scalar.copy(
+                dealt_codes[:, a, :].rearrange("p (t n e) -> p n t e", t=PACK, e=PACK),
+                w2_codes[DEALT][:, a, :].rearrange("p (n e t) -> p n t e", t=PACK, e=PACK),
+            )
+        nc.gpsimd.tensor_copy(
+            dealt_planes[:].rearrange("p a (t m) -> p a t m", t=PACK),
+            w2_planes[:, :, HALF : 2 * HALF].rearrange("p a (m t) -> p a t m", t=PACK),
+        )
         lower_scales(nc.scalar, partner_planes)
-        nc.sync.dma_start(w2_codes[1][:].bitcast(I32), w2_view[:, :, HALF : 2 * HALF])
+        nc.sync.dma_start(w2_codes[TURNED][:].bitcast(I32), w2_view[:, :, 0:HALF])
         nc.sync.dma_start(case_list[:], offs)
-        partner_words = [gather_words("partner_words", partner_list, h) for h in range(2)]
+        partner_words = [gather_words(held("partner_words%d" % h, [P, 2, HALF], U16), partner_list, h) for h in range(2)]
         case_planes = gather_scales("case", case_list)
         w1_raw = [[held("w1_raw%d%d" % (c, a), [P, PACK, HALF], F32) for a in range(2)] for c in range(2)]
         for c in (DEALT, TURNED):
-            if c == TURNED:
-                lower_scales(nc.sync, case_planes)
             for a in range(2):
+                if (c, a) == (TURNED, 1):
+                    lower_scales(nc.sync, case_planes)
                 nc.sync.dma_start(
                     w1_raw[c][a][:],
                     w1[PASS * a : PASS * (a + 1), HALF * c : HALF * (c + 1)].rearrange("(p i) r -> p i r", i=PACK),
@@ -183,30 +196,19 @@ def tile_list_partner_invitation_scores_kernel(
         with nc.allow_non_contiguous_dma(reason="one offset a partition"):
             nc.sync.dma_start(clinic_t[:], clinic.rearrange("(n p) -> p n", p=P))
 
-        rb_turned = held("rb_turned", [P, 2 * TILES, HALF], F32)
-        w2_turned = [(w2_codes[TURNED][:, a, :], w2_planes[:, a, 0:HALF]) for a in range(2)]
-        for h in range(2):
-            passes = (1, 0) if h else (0, 1)
-            turned_stage(rb_turned, h, partner_words[h], partner_planes, w2_turned, TILES * h, passes=passes)
-
-        dealt_codes = held("dealt_codes", [P, 2, HALF], U32)
-        dealt_planes = held("dealt_planes", [P, 2, HALF], U8)
-        for a in range(2):
-            nc.gpsimd.tensor_copy(
-                dealt_codes[:, a, :].rearrange("p (t n e) -> p n t e", t=PACK, e=PACK),
-                w2_codes[DEALT][:, a, :].rearrange("p (n e t) -> p n t e", t=PACK, e=PACK),
-            )
-        nc.gpsimd.tensor_copy(
-            dealt_planes[:].rearrange("p a (t m) -> p a t m", t=PACK),
-            w2_planes[:, :, HALF : 2 * HALF].rearrange("p a (m t) -> p a t m", t=PACK),
-        )
         w2_dealt = [(dealt_codes[:, a, :], dealt_planes[:, a, :]) for a in range(2)]
         rb_dealt = [held("rb_dealt%d" % h, [P, PACK, HALF], F32) for h in range(2)]
         for h in range(2):
-            dealt_stage(rb_dealt[h], h, partner_words[h], partner_planes, w2_dealt)
+            passes = (1, 0) if h else (0, 1)
+            dealt_stage(rb_dealt[h], h, partner_words[h], partner_planes, w2_dealt, passes)
 
-        case_words = [gather_words("case_words", case_list, 0)]
-        rounded = [held("rounded_dealt%d" % a, [P, PACK, P, PACK], BF16) for a in range(2)]
+        rb_turned = held("rb_turned", [P, 2 * TILES, HALF], F32)
+        w2_turned = [(w2_codes[TURNED][:, a, :], w2_planes[:, a, 0:HALF]) for a in range(2)]
+        for h in range(2):
+            turned_stage(rb_turned, h, partner_words[h], partner_planes, w2_turned, TILES * h)
+
+        case_words = [gather_words(held("case_words0", [P, 2, HALF], U16), case_list, 0)]
+        rounded = [placed("rounded_dealt%d" % a, [P, PACK, P, PACK], BF16, 4096 * a) for a in range(2)]
         for a in range(2):
             values = rounded[a][:].rearrange("p t m i -> p m t i")
             raw = w1_raw[DEALT][a][:].rearrange("p i (m t) -> p m t i", t=PACK)
@@ -217,7 +219,7 @@ def tile_list_partner_invitation_scores_kernel(
         w1_dealt = [
             quantise("w1_dealt%d" % a, rounded[a][:].rearrange("p t m i -> p (t m i)"), HALF) for a in range(2)
         ]
-        case_words.append(gather_words("case_words", case_list, 1, tag="rounded_dealt1"))
+        case_words.append(gather_words(placed("case_words1", [P, 2, HALF], U16, 3072), case_list, 1))
         ra_dealt = [held("ra_dealt%d" % h, [P, PACK, HALF], F32) for h in range(2)]
         for h in range(2):
             dealt_stage(ra_dealt[h], h, case_words[h], case_planes, w1_dealt)
@@ -225,7 +227,10 @@ def tile_list_partner_invitation_scores_kernel(
         piece = HALF // 2
         ra_turned = held("ra_turned", [P, 2 * TILES, HALF], F32)
         for g in range(2):
-            rounded = [held("rounded_turned%d%d" % (g, a), [P, piece, PACK], BF16) for a in range(2)]
+            rounded = [
+                placed("rounded_turned%d0" % g, [P, piece, PACK], BF16, 5120 + 2048 * g),
+                held("rounded_turned%d1" % g, [P, piece, PACK], BF16),
+            ]
             for a in range(2):
                 raw = w1_raw[TURNED][a][:, :, piece * g : piece * (g + 1)]
                 if a == 0:

@@ -32,7 +32,6 @@ ROUND = 1024
 TURNED, DEALT = 0, 1
 CHUNKS = (2, 2, 2, 1, 1)
 ROOTS = 4
-LIVE = 100
 TURN_BANKS = 5
 
 
@@ -76,7 +75,7 @@ def tile_list_partner_invitation_scores_kernel(
         identity = held("identity", [P, P], F32)
         lowered = {name: held(name + "_lowered", [P, S], U8) for name in ("partner", "case")}
 
-        nc.gpsimd.memset(table_scales[:].bitcast(I32), 0)
+        nc.vector.memset(table_scales[:].bitcast(I32), 0)
         nc.vector.memset(w2_planes[:].bitcast(I32), 0)
         load_planes(nc.gpsimd, w2_planes, w2_scales)
         for plane in lowered.values():
@@ -86,7 +85,8 @@ def tile_list_partner_invitation_scores_kernel(
 
         nc.sync.dma_start(partner_list[:], offs2)
         w2_view = w2_words.rearrange("a p c i -> p a (c i)").bitcast(I32)
-        nc.sync.dma_start(w2_codes[DEALT][:].bitcast(I32), w2_view[:, :, HALF : 2 * HALF])
+        nc.sync.dma_start(w2_codes[DEALT][:, 0, :].bitcast(I32), w2_view[:, 0, HALF : 2 * HALF])
+        nc.sync.dma_start(gain_t[:], gain.rearrange("(c p t) -> p c t", c=2, t=PACK))
         for r in range(4):
             nc.sync.dma_start(
                 table_scales[r:P:RAISED, :].bitcast(I32),
@@ -101,7 +101,11 @@ def tile_list_partner_invitation_scores_kernel(
             return [picked, lowered[name]]
 
         def lower_scales(queue, planes):
-            queue.dma_start(planes[1][0:LIVE, :].bitcast(I32), planes[0][RAISED : RAISED + LIVE, :].bitcast(I32))
+            for first, count in ((0, 64), (64, 32), (96, 4)):
+                queue.dma_start(
+                    planes[1][first : first + count, :].bitcast(I32),
+                    planes[0][RAISED + first : RAISED + first + count, :].bitcast(I32),
+                )
 
         def gather_words(picked, offsets, h):
             for a in range(2):
@@ -165,6 +169,7 @@ def tile_list_partner_invitation_scores_kernel(
                 nc.scalar.activation(feature[:, t, :], bank[:], ACT.Exp)
 
         partner_planes = gather_scales("partner", partner_list)
+        nc.sync.dma_start(w2_codes[DEALT][:, 1, :].bitcast(I32), w2_view[:, 1, HALF : 2 * HALF])
         dealt_codes = held("dealt_codes", [P, 2, HALF], U32)
         dealt_planes = held("dealt_planes", [P, 2, HALF], U8)
         for a in range(2):
@@ -172,10 +177,10 @@ def tile_list_partner_invitation_scores_kernel(
                 dealt_codes[:, a, :].rearrange("p (t n e) -> p n t e", t=PACK, e=PACK),
                 w2_codes[DEALT][:, a, :].rearrange("p (n e t) -> p n t e", t=PACK, e=PACK),
             )
-        nc.gpsimd.tensor_copy(
-            dealt_planes[:].rearrange("p a (t m) -> p a t m", t=PACK),
-            w2_planes[:, :, HALF : 2 * HALF].rearrange("p a (m t) -> p a t m", t=PACK),
-        )
+            nc.gpsimd.tensor_copy(
+                dealt_planes[:, a, :].rearrange("p (t m) -> p t m", t=PACK),
+                w2_planes[:, a, HALF : 2 * HALF].rearrange("p (m t) -> p t m", t=PACK),
+            )
         lower_scales(nc.scalar, partner_planes)
         nc.sync.dma_start(w2_codes[TURNED][:].bitcast(I32), w2_view[:, :, 0:HALF])
         nc.sync.dma_start(case_list[:], offs)
@@ -191,7 +196,6 @@ def tile_list_partner_invitation_scores_kernel(
                     w1[PASS * a : PASS * (a + 1), HALF * c : HALF * (c + 1)].rearrange("(p i) r -> p i r", i=PACK),
                 )
         nc.sync.dma_start(w3_codes[:].bitcast(I32), w3_words.rearrange("a p b -> p a b").bitcast(I32))
-        nc.sync.dma_start(gain_t[:], gain.rearrange("(c p t) -> p c t", c=2, t=PACK))
         load_planes(nc.sync, w3_planes, w3_scales)
         with nc.allow_non_contiguous_dma(reason="one offset a partition"):
             nc.sync.dma_start(clinic_t[:], clinic.rearrange("(n p) -> p n", p=P))

@@ -1,4 +1,3 @@
-import math
 from contextlib import ExitStack
 
 import concourse.mybir as mybir
@@ -28,11 +27,10 @@ OUT_TILES = N // P
 LIST_COLUMNS = HALF // 16
 NEIGHBOURS = 2
 RAISED = 16
-ROUND = 1024
-TURNED, DEALT = 0, 1
-CHUNKS = (2, 2, 2, 1, 1)
-ROOTS = 4
-TURN_BANKS = 5
+FIRST, SECOND = 1, 0
+CHUNKS = (1, 1, 2, 2, 1, 1)
+AHEAD = 4
+RAW_AT = 37888
 
 
 def tile_list_partner_invitation_scores_kernel(
@@ -41,7 +39,6 @@ def tile_list_partner_invitation_scores_kernel(
     nc = tc.nc
     with ExitStack() as ctx:
         keep = ctx.enter_context(tc.tile_pool(name="keep", bufs=1))
-        ring = ctx.enter_context(tc.tile_pool(name="ring", bufs=3))
         reused = ctx.enter_context(tc.tile_pool(name="reused", bufs=1))
         psum = ctx.enter_context(tc.psum_pool(name="psum", bufs=1))
 
@@ -70,23 +67,26 @@ def tile_list_partner_invitation_scores_kernel(
         w3_codes = held("w3_codes", [P, 2, 2 * N], U8)
         w3_planes = held("w3_planes", [P, 2, N], U8)
         gain_t = held("gain_t", [P, 2, PACK], F32)
-        gain_inv = held("gain_inv", [P, 2, PACK], F32)
+        log_gain = held("log_gain", [P, 2, PACK], F32, tag="dealt_codes%d" % FIRST)
+        bias = held("bias", [P, 2, PACK], F32)
+        gain_inv = held("gain_inv", [P, PACK], F32)
         clinic_t = held("clinic_t", [P, OUT_TILES], F32)
         identity = held("identity", [P, P], F32)
         lowered = {name: held(name + "_lowered", [P, S], U8) for name in ("partner", "case")}
 
         nc.vector.memset(table_scales[:].bitcast(I32), 0)
-        nc.vector.memset(w2_planes[:].bitcast(I32), 0)
+        nc.gpsimd.memset(w2_planes[:].bitcast(I32), 0)
         load_planes(nc.gpsimd, w2_planes, w2_scales)
-        for plane in lowered.values():
-            nc.vector.memset(plane[96:P, :].bitcast(I32), 0)
-        nc.vector.memset(w3_planes[:].bitcast(I32), 0)
+        for words in [plane[96:P, :] for plane in lowered.values()] + [w3_planes[:].rearrange("p a n -> p (a n)")]:
+            words = words.bitcast(I32)
+            nc.vector.memset(words[:, 0:1], 0)
+            nc.vector.memset(words[:, 1:], 0)
         make_identity(nc, identity[:])
 
         nc.sync.dma_start(partner_list[:], offs2)
         w2_view = w2_words.rearrange("a p c i -> p a (c i)").bitcast(I32)
-        nc.sync.dma_start(w2_codes[DEALT][:, 0, :].bitcast(I32), w2_view[:, 0, HALF : 2 * HALF])
         nc.sync.dma_start(gain_t[:], gain.rearrange("(c p t) -> p c t", c=2, t=PACK))
+        nc.sync.dma_start(w2_codes[FIRST][:, 0, :].bitcast(I32), w2_view[:, 0, HALF * FIRST : HALF * (FIRST + 1)])
         for r in range(4):
             nc.sync.dma_start(
                 table_scales[r:P:RAISED, :].bitcast(I32),
@@ -113,17 +113,8 @@ def tile_list_partner_invitation_scores_kernel(
                 nc.vector.tensor_copy(picked[:, a, :], table[a][:].indirect(columns))
             return [picked[:, a, :] for a in range(2)]
 
-        def round_on_gpsimd(rounded, raw):
-            step = ROUND * rounded.shape[1] // math.prod(rounded.shape[1:])
-            for n0 in range(0, rounded.shape[1], step):
-                piece = slice(n0, n0 + step)
-                nc.gpsimd.tensor_scalar(rounded[:, piece], raw[:, piece], 1.0, 0.0, ALU.mult, ALU.add)
-
-        def quantise(name, values, width, tags=("", "")):
-            code = held(name + "_codes", [P, width], U32, tag=tags[0])
-            plane = held(name + "_plane", [P, width], U8, tag=tags[1])
-            nc.vector.quantize_mx(out=code[:].bitcast(FP8X4), scales=plane[:], in_=values)
-            return code[:], plane[:]
+        def quantise(code, plane, values):
+            nc.vector.quantize_mx(out=code.bitcast(FP8X4), scales=plane, in_=values)
 
         def product(out_ap, stationary, moving, passes):
             for a in passes:
@@ -146,195 +137,219 @@ def tile_list_partner_invitation_scores_kernel(
         def weight_columns(weight, r0, width):
             return [(code[:, r0 : r0 + width].bitcast(FP8X4), plane[:, r0 : r0 + width]) for code, plane in weight]
 
-        def turned_stage(feature, h, words, planes, weight, first_bank, r0=0, width=HALF, passes=(1, 0)):
-            per_bank = HALF // width
-            for j0 in range(0, TILES, per_bank):
-                bank = bank_tile(first_bank + j0 // per_bank, [P, per_bank, width])
-                for jt in range(j0, j0 + per_bank):
-                    stationary = picked_columns(words, planes, h, P * jt, P)
-                    product(bank[:, jt - j0, :], stationary, weight_columns(weight, 0, width), passes)
-                rows = slice(TILES * h + j0, TILES * h + j0 + per_bank)
-                nc.scalar.activation(
-                    feature[:, rows, :].rearrange("p j (t m) -> p j t m", t=PACK)[
-                        :, :, :, r0 // PACK : (r0 + width) // PACK
-                    ],
-                    bank[:].rearrange("p j (m t) -> p j t m", t=PACK),
-                    ACT.Exp,
-                )
+        def turned_stage(feature, h, words, planes, weight):
+            for jt in range(TILES):
+                bank = bank_tile(TILES * h + jt, [P, HALF])
+                product(bank[:], picked_columns(words, planes, h, P * jt, P), weight_columns(weight, 0, HALF), (1, 0))
+                nc.scalar.activation(feature[:, jt, :], bank[:], ACT.Exp)
 
-        def dealt_stage(feature, h, words, planes, weight, passes=(1, 0)):
+        def dealt_stage(feature, c, h, words, planes, weight, passes=(1, 0)):
             for t in range(PACK):
                 bank = bank_tile(TILES * h + t, [P, HALF])
                 product(bank[:], weight_columns(weight, P * t, P), picked_columns(words, planes, h, 0, HALF), passes)
-                nc.scalar.activation(feature[:, t, :], bank[:], ACT.Exp)
+                nc.scalar.activation(feature[:, t, :], bank[:], ACT.Exp, bias=bias[:, c, t : t + 1])
+
+        nc.scalar.activation(log_gain[:], gain_t[:], ACT.Ln)
+        nc.scalar.activation(bias[:], log_gain[:], ACT.Identity, scale=-1.0)
+        nc.scalar.activation(gain_inv[:], log_gain[:, SECOND, :], ACT.Exp, scale=-1.0)
 
         partner_planes = gather_scales("partner", partner_list)
-        nc.sync.dma_start(w2_codes[DEALT][:, 1, :].bitcast(I32), w2_view[:, 1, HALF : 2 * HALF])
-        dealt_codes = held("dealt_codes", [P, 2, HALF], U32)
-        dealt_planes = held("dealt_planes", [P, 2, HALF], U8)
-        for a in range(2):
-            nc.scalar.copy(
-                dealt_codes[:, a, :].rearrange("p (t n e) -> p n t e", t=PACK, e=PACK),
-                w2_codes[DEALT][:, a, :].rearrange("p (n e t) -> p n t e", t=PACK, e=PACK),
-            )
+        nc.sync.dma_start(w2_codes[FIRST][:, 1, :].bitcast(I32), w2_view[:, 1, HALF * FIRST : HALF * (FIRST + 1)])
+        dealt_codes = [held("dealt_codes%d" % c, [P, 2, HALF], U32) for c in range(2)]
+        dealt_planes = [held("dealt_planes%d" % c, [P, 2, HALF], U8) for c in range(2)]
+
+        def deal_planes(c, a):
             nc.gpsimd.tensor_copy(
-                dealt_planes[:, a, :].rearrange("p (t m) -> p t m", t=PACK),
-                w2_planes[:, a, HALF : 2 * HALF].rearrange("p (m t) -> p t m", t=PACK),
+                dealt_planes[c][:, a, :].rearrange("p (t m) -> p t m", t=PACK),
+                w2_planes[:, a, HALF * c : HALF * (c + 1)].rearrange("p (m t) -> p t m", t=PACK),
             )
+
+        def deal_codes(copy, c, a):
+            copy(
+                dealt_codes[c][:, a, :].rearrange("p (t n e) -> p n t e", t=PACK, e=PACK),
+                w2_codes[c][:, a, :].rearrange("p (n e t) -> p n t e", t=PACK, e=PACK),
+            )
+
+        for a in range(2):
+            deal_codes(nc.scalar.copy, FIRST, a)
+            deal_planes(FIRST, a)
         lower_scales(nc.scalar, partner_planes)
-        nc.sync.dma_start(w2_codes[TURNED][:].bitcast(I32), w2_view[:, :, 0:HALF])
+        nc.sync.dma_start(w2_codes[SECOND][:].bitcast(I32), w2_view[:, :, HALF * SECOND : HALF * (SECOND + 1)])
         nc.sync.dma_start(case_list[:], offs)
+        for a in range(2):
+            deal_planes(SECOND, a)
+        for a in range(2):
+            deal_codes(nc.gpsimd.tensor_copy, SECOND, a)
         partner_words = [gather_words(held("partner_words%d" % h, [P, 2, HALF], U16), partner_list, h) for h in range(2)]
         case_planes = gather_scales("case", case_list)
-        w1_raw = [[held("w1_raw%d%d" % (c, a), [P, PACK, HALF], F32) for a in range(2)] for c in range(2)]
-        for c in (DEALT, TURNED):
-            for a in range(2):
-                if (c, a) == (TURNED, 1):
-                    lower_scales(nc.sync, case_planes)
-                nc.sync.dma_start(
-                    w1_raw[c][a][:],
-                    w1[PASS * a : PASS * (a + 1), HALF * c : HALF * (c + 1)].rearrange("(p i) r -> p i r", i=PACK),
-                )
+        w1_raw = {}
+        for index, (c, a) in enumerate((c, a) for c in (FIRST, SECOND) for a in range(2)):
+            if (c, a) == (SECOND, 1):
+                lower_scales(nc.sync, case_planes)
+            w1_raw[c, a] = placed("w1_raw%d%d" % (c, a), [P, PACK, HALF], F32, RAW_AT + 8192 * index)
+            nc.sync.dma_start(
+                w1_raw[c, a][:],
+                w1[PASS * a : PASS * (a + 1), HALF * c : HALF * (c + 1)].rearrange("(p i) r -> p i r", i=PACK),
+            )
         nc.sync.dma_start(w3_codes[:].bitcast(I32), w3_words.rearrange("a p b -> p a b").bitcast(I32))
         load_planes(nc.sync, w3_planes, w3_scales)
         with nc.allow_non_contiguous_dma(reason="one offset a partition"):
             nc.sync.dma_start(clinic_t[:], clinic.rearrange("(n p) -> p n", p=P))
 
-        w2_dealt = [(dealt_codes[:, a, :], dealt_planes[:, a, :]) for a in range(2)]
-        rb_dealt = [held("rb_dealt%d" % h, [P, PACK, HALF], F32) for h in range(2)]
-        for h in range(2):
-            passes = (1, 0) if h else (0, 1)
-            dealt_stage(rb_dealt[h], h, partner_words[h], partner_planes, w2_dealt, passes)
+        quarters = [(c, h) for c in (FIRST, SECOND) for h in range(2)]
+        turned = quarters[-1]
+        rb = {q: held("rb%d%d" % q, [P, PACK, HALF], F32) for q in quarters}
+        ra = {q: held("ra%d%d" % q, [P, PACK, HALF], F32) for q in quarters}
 
-        rb_turned = held("rb_turned", [P, 2 * TILES, HALF], F32)
-        w2_turned = [(w2_codes[TURNED][:, a, :], w2_planes[:, a, 0:HALF]) for a in range(2)]
-        for h in range(2):
-            turned_stage(rb_turned, h, partner_words[h], partner_planes, w2_turned, TILES * h)
+        def stage(feature, c, h, words, planes, weight, passes=(1, 0)):
+            if (c, h) == turned:
+                turned_stage(feature[c, h], h, words, planes, weight)
+            else:
+                dealt_stage(feature[c, h], c, h, words, planes, weight, passes)
+
+        for c, h in quarters:
+            w2_dealt = [(dealt_codes[c][:, a, :], dealt_planes[c][:, a, :]) for a in range(2)]
+            passes = (0, 1) if (c, h) == quarters[0] else (1, 0)
+            stage(rb, c, h, partner_words[h], partner_planes, w2_dealt, passes)
+
+        def dealt_view(c, a):
+            return w1_raw[c, a][:].rearrange("p i (m t) -> p m t i", t=PACK)
+
+        def packed(name, offset=None):
+            code = placed(name, [P, HALF], U32, offset) if offset else held(name, [P, HALF], U32)
+            return code[:], held(name + "_plane", [P, HALF], U8)[:]
+
+        def quantise_w1(c, offsets, weight):
+            rounded = [placed("rounded%d%d" % (c, a), [P, PACK, P, PACK], BF16, offsets[a]) for a in range(2)]
+            values = [tile[:].rearrange("p t m i -> p m t i") for tile in rounded]
+            for m0 in range(0, P, P // 2):
+                piece = slice(m0, m0 + P // 2)
+                nc.gpsimd.tensor_scalar(values[0][:, piece], dealt_view(c, 0)[:, piece], 1.0, 0.0, ALU.mult, ALU.add)
+            nc.vector.tensor_copy(values[1], dealt_view(c, 1))
+            for u in range(2):
+                columns = slice(2 * P * u, 2 * P * (u + 1))
+                for (code, plane), tile in zip(weight, rounded):
+                    slices = tile[:, 2 * u : 2 * u + 2].rearrange("p t m i -> p (t m i)")
+                    quantise(code[:, columns], plane[:, columns], slices)
 
         case_words = [gather_words(held("case_words0", [P, 2, HALF], U16), case_list, 0)]
-        rounded = [placed("rounded_dealt%d" % a, [P, PACK, P, PACK], BF16, 4096 * a) for a in range(2)]
-        for a in range(2):
-            values = rounded[a][:].rearrange("p t m i -> p m t i")
-            raw = w1_raw[DEALT][a][:].rearrange("p i (m t) -> p m t i", t=PACK)
-            if a == 0:
-                round_on_gpsimd(values, raw)
-            else:
-                nc.vector.tensor_copy(values, raw)
-        w1_dealt = [
-            quantise("w1_dealt%d" % a, rounded[a][:].rearrange("p t m i -> p (t m i)"), HALF) for a in range(2)
-        ]
-        case_words.append(gather_words(placed("case_words1", [P, 2, HALF], U16, 3072), case_list, 1))
-        ra_dealt = [held("ra_dealt%d" % h, [P, PACK, HALF], F32) for h in range(2)]
+        w1_first = [packed("w1_first%d" % a) for a in range(2)]
+        quantise_w1(FIRST, (0, 4096), w1_first)
+        case_words.append(gather_words(placed("case_words1", [P, 2, HALF], U16, 5120), case_list, 1))
         for h in range(2):
-            dealt_stage(ra_dealt[h], h, case_words[h], case_planes, w1_dealt)
+            stage(ra, FIRST, h, case_words[h], case_planes, w1_first)
 
-        piece = HALF // 2
-        ra_turned = held("ra_turned", [P, 2 * TILES, HALF], F32)
-        for g in range(2):
-            rounded = [
-                placed("rounded_turned%d0" % g, [P, piece, PACK], BF16, 5120 + 2048 * g),
-                held("rounded_turned%d1" % g, [P, piece, PACK], BF16),
-            ]
-            for a in range(2):
-                raw = w1_raw[TURNED][a][:, :, piece * g : piece * (g + 1)]
-                if a == 0:
-                    round_on_gpsimd(rounded[a][:], raw.rearrange("p i n -> p n i"))
-                else:
-                    nc.vector.tensor_copy(
-                        rounded[a][:].rearrange("p (n e) i -> p n i e", e=NEIGHBOURS),
-                        raw.rearrange("p i (n e) -> p n i e", e=NEIGHBOURS),
-                    )
-            weight = [
-                quantise(
-                    "w1_turned%d%d" % (g, a),
-                    rounded[a][:].rearrange("p n i -> p (n i)"),
-                    piece,
-                    tags=("root%d" % a, "root%d" % (a + 2)) if g else ("", ""),
-                )
-                for a in range(2)
-            ]
-            for h in range(2):
-                turned_stage(ra_turned, h, case_words[h], case_planes, weight, TILES * g + 2 * h, piece * g, piece)
-        nc.vector.reciprocal(gain_inv[:], gain_t[:])
-
-        total_dealt = [held("total_dealt%d" % h, [P, PACK, HALF], F32, tag="w1_raw%d%d" % (TURNED, 1 - h)) for h in range(2)]
+        w1_second = [packed("w1_second0", RAW_AT + 32768), packed("w1_second1")]
+        quantise_w1(SECOND, (7168, 11264), w1_second)
         for h in range(2):
-            nc.vector.tensor_tensor(total_dealt[h][:], ra_dealt[h][:], rb_dealt[h][:], ALU.add)
-        total_turned = held("total_turned", [P, TILES, HALF], F32)
-        nc.vector.tensor_tensor(total_turned[:], ra_turned[:, TILES:, :], rb_turned[:, TILES:, :], ALU.add)
+            stage(ra, SECOND, h, case_words[h], case_planes, w1_second)
 
-        def make_root(step, first, tiles, c, turn):
-            width = P * tiles
-            root = held("root_%d" % step, [P, PACK, width], F32, tag="root%d" % (step % ROOTS))
-
-            def root_of(t, values):
-                nc.scalar.activation(root[:, t, :], values, ACT.Abs_reciprocal_sqrt, scale=gain_inv[:, c, t : t + 1])
-
-            if c == DEALT:
-                h, jt = divmod(first, TILES)
-                for t in range(PACK):
-                    root_of(t, total_dealt[h][:, t, P * jt : P * jt + width])
-                return root
-            per_bank = HALF // width
-            for t0 in range(0, PACK, per_bank):
-                bank = bank_tile((turn + t0 // per_bank) % TURN_BANKS, [P, per_bank, width])
-                for t in range(t0, t0 + per_bank):
-                    for jt in range(tiles):
-                        tile = first + jt
-                        terms = [rb_turned[:, tile, :], ra_turned[:, tile, :]]
-                        if tile >= TILES:
-                            terms = [total_turned[:, tile - TILES, :]]
-                        for index, term in enumerate(terms):
-                            nc.tensor.matmul(
-                                bank[:, t - t0, P * jt : P * (jt + 1)],
-                                term[:, P * t : P * (t + 1)],
-                                identity[:],
-                                start=(index == 0),
-                                stop=(index == len(terms) - 1),
-                                is_transpose=True,
-                            )
-                for t in range(t0, t0 + per_bank):
-                    root_of(t, bank[:, t - t0, :])
-            return root
-
-        def square(root, width):
-            grouped = ring.tile([P, width, PACK], BF16, name="h_grouped", align_bytes=64)
-            y = root[:].rearrange("p t (n e) -> p n t e", e=NEIGHBOURS)
-            nc.vector.tensor_tensor(grouped[:].rearrange("p (n e) t -> p n t e", e=NEIGHBOURS), y, y, ALU.mult)
-            return grouped[:].rearrange("p n t -> p (n t)")
-
-        def second_stage(first, tiles, operands, indices, last):
-            width = P * tiles
-            banks = [bank_tile(index, [P, width]) for index in indices]
-            for c, (code, plane) in zip((DEALT, TURNED), operands):
-                for n in range(OUT_TILES):
-                    nc.tensor.matmul_mx(
-                        out=banks[n][:],
-                        lhsT=w3_codes[:, c, 2 * P * n : 2 * P * (n + 1)].bitcast(FP4X4),
-                        lhsT_scale=w3_planes[:, c, P * n : P * (n + 1)],
-                        rhs=code.bitcast(FP8X4),
-                        rhs_scale=plane,
-                        start=(c == DEALT),
-                        stop=(c == TURNED),
+        total = placed("total", [P, 3, PACK, HALF], F32, 13312)
+        for index, q in enumerate(quarters[:-1]):
+            nc.vector.tensor_tensor(total[:, index], ra[q][:], rb[q][:], ALU.add)
+        sums = [bank_tile(t, [P, HALF]) for t in range(PACK)]
+        for jt in range(TILES):
+            for t in range(PACK):
+                for index, term in enumerate((rb[turned], ra[turned])):
+                    nc.tensor.matmul(
+                        sums[t][:, P * jt : P * (jt + 1)],
+                        term[:, jt, P * t : P * (t + 1)],
+                        identity[:],
+                        start=(index == 0),
+                        stop=(index == 1),
+                        is_transpose=True,
                     )
-            for n in range(OUT_TILES):
-                scores = held("scores%d%d" % (first, n), [P, width], F32)
-                if last and n == 1:
-                    nc.vector.tensor_scalar(scores[:], banks[n][:], clinic_t[:, n : n + 1], None, ALU.add)
-                else:
-                    nc.scalar.activation(scores[:], banks[n][:], ACT.Identity, bias=clinic_t[:, n : n + 1])
-                nc.sync.dma_start(out[P * n : P * (n + 1), P * first : P * first + width], scores[:])
 
         starts = [sum(CHUNKS[:index]) for index in range(len(CHUNKS))]
-        steps = [(starts[index], tiles, c) for index, tiles in enumerate(CHUNKS) for c in (DEALT, TURNED)]
-        squared, made, turn = [], [], 0
-        for step, (first, tiles, c) in enumerate(steps):
-            squared.append(square(make_root(step, first, tiles, c, turn), P * tiles))
-            if c == TURNED:
-                turn = turn + tiles
+        steps = [(starts[index], tiles, c) for index, tiles in enumerate(CHUNKS) for c in (FIRST, SECOND)]
+        roots = placed("roots", [P, 4 * PACK * HALF], F32, RAW_AT + 2048)
+        y, places = {}, {"used": 0, "bank": 0}
+
+        def root_room(width):
+            used = places["used"]
+            places["used"] = used + PACK * width
+            return roots[:, used : used + PACK * width].rearrange("p (t j) -> p t j", t=PACK)
+
+        def make_root(step):
+            first, tiles, c = steps[step]
+            h, jt = divmod(first, TILES)
+            if (c, h) != turned:
+                y[step] = root_room(P * tiles)
+                values = total[:, quarters.index((c, h)), :, P * jt : P * (jt + tiles)]
+                nc.scalar.activation(y[step], values, ACT.Abs_reciprocal_sqrt)
+                return
+            if jt % 2 == 0:
+                places["turned"] = root_room(2 * P)
+                for t in range(PACK):
+                    nc.scalar.activation(
+                        places["turned"][:, t, :],
+                        sums[t][:, P * jt : P * (jt + 2)],
+                        ACT.Abs_reciprocal_sqrt,
+                        scale=gain_inv[:, t : t + 1],
+                    )
+            y[step] = places["turned"][:, :, P * (jt % 2) : P * (jt % 2 + tiles)]
+
+        def square(step):
+            width = P * steps[step][1]
+            grouped = held("h_grouped%d" % step, [P, width, PACK], BF16)
+            values = y[step].rearrange("p t (n e) -> p n t e", e=NEIGHBOURS)
+            target = grouped[:].rearrange("p (n e) t -> p n t e", e=NEIGHBOURS)
+            nc.vector.tensor_tensor(target, values, values, ALU.mult)
+            return grouped[:].rearrange("p n t -> p (n t)")
+
+        def quantise_h(step):
+            width = P * steps[step][1]
+            code = held("h_codes%d" % step, [P, width], U32)
+            plane = held("h_plane%d" % step, [P, width], U8)
+            quantise(code[:], plane[:], squared[step])
+            return code[:], plane[:]
+
+        def multiply(chunk, operands):
+            width = P * CHUNKS[chunk]
+            last = chunk == len(CHUNKS) - 1
+            per_bank = 1 if last else HALF // width
+            views = []
+            for n0 in range(0, OUT_TILES, per_bank):
+                index = n0 if last else TILES + places["bank"] % TILES
+                places["bank"] = places["bank"] + 1
+                bank = bank_tile(index, [P, min(per_bank, OUT_TILES - n0), width])
+                views.extend(bank[:, n, :] for n in range(bank.shape[1]))
+            halves = list(zip((FIRST, SECOND), operands))
+            passes = [(n, half) for n in range(OUT_TILES) for half in halves]
+            if last:
+                passes = [(n, half) for half in halves for n in range(OUT_TILES)]
+            for n, (c, (code, plane)) in passes:
+                nc.tensor.matmul_mx(
+                    out=views[n],
+                    lhsT=w3_codes[:, c, 2 * P * n : 2 * P * (n + 1)].bitcast(FP4X4),
+                    lhsT_scale=w3_planes[:, c, P * n : P * (n + 1)],
+                    rhs=code.bitcast(FP8X4),
+                    rhs_scale=plane,
+                    start=(c == FIRST),
+                    stop=(c == SECOND),
+                )
+            return views
+
+        def store(chunk, views):
+            first, width = starts[chunk], P * CHUNKS[chunk]
+            for n in range(OUT_TILES):
+                scores = held("scores%d%d" % (chunk, n), [P, width], F32)
+                if chunk == len(CHUNKS) - 1 and n == 1:
+                    nc.vector.tensor_scalar(scores[:], views[n], clinic_t[:, n : n + 1], None, ALU.add)
+                else:
+                    nc.scalar.activation(scores[:], views[n], ACT.Identity, bias=clinic_t[:, n : n + 1])
+                nc.sync.dma_start(out[P * n : P * (n + 1), P * first : P * first + width], scores[:])
+
+        count = len(steps)
+        squared, made = {}, []
+        for step in range(AHEAD):
+            make_root(step)
+        for step in range(count + 1):
+            if step + AHEAD < count:
+                make_root(step + AHEAD)
+            if step < count:
+                squared[step] = square(step)
             if step > 0:
-                made.append(quantise("h%d" % (step - 1), squared[step - 1], P * steps[step - 1][1]))
-            if step > 1 and c == TURNED:
-                second_stage(*steps[step - 2][:2], made[step - 3 : step - 1], range(TURN_BANKS, TURN_BANKS + OUT_TILES), False)
-        made.append(quantise("h%d" % (len(steps) - 1), squared[-1], P * CHUNKS[-1]))
-        second_stage(*steps[-1][:2], made[-2:], [(turn + n) % TURN_BANKS for n in range(OUT_TILES)], True)
+                made.append(quantise_h(step - 1))
+                if step % 2 == 0:
+                    store(step // 2 - 1, multiply(step // 2 - 1, made[-2:]))

@@ -26,11 +26,29 @@ TILES = HALF // P
 OUT_TILES = N // P
 LIST_COLUMNS = HALF // 16
 NEIGHBOURS = 2
-RAISED = 16
+ROWS_AT = 96
 FIRST, SECOND = 1, 0
 CHUNKS = (1, 1, 2, 2, 1, 1)
 AHEAD = 4
-RAW_AT = 37888
+
+ROUNDED_AT = {(FIRST, 0): 0, (FIRST, 1): 4096, (SECOND, 0): 7168, (SECOND, 1): 11264}
+LATE_CASE_WORDS_AT = 5120
+TOTAL_AT = 13312
+W2_SECOND_AT = 15360
+W2_FIRST_AT = 18432
+W1_AT = {(FIRST, 0): 19456, (FIRST, 1): 27648, (SECOND, 0): 38656, (SECOND, 1): 46848}
+TABLE_SCALES_AT = 34816
+LATE_PARTNER_WORDS_AT = 35840
+W3_PLANES_AT = 37888
+LATE_PICKED_AT = 54528
+CLINIC_AT = 55040
+W3_CODES_AT = 55104
+ROOTS_AT = 56640
+TABLE_AT = ROOTS_AT
+DEALT_AT = TABLE_AT + 16384
+W1_CODES_AT = DEALT_AT + 8192
+EARLY_WORDS_AT = W1_CODES_AT + 6144
+EARLY_PICKED_AT = EARLY_WORDS_AT + 2048
 
 
 def tile_list_partner_invitation_scores_kernel(
@@ -42,14 +60,19 @@ def tile_list_partner_invitation_scores_kernel(
         reused = ctx.enter_context(tc.tile_pool(name="reused", bufs=1))
         psum = ctx.enter_context(tc.psum_pool(name="psum", bufs=1))
 
-        def held(name, shape, dtype, tag=""):
-            return keep.tile(shape, dtype, name=name, tag=tag or name, align_bytes=64)
+        def held(name, shape, dtype):
+            return keep.tile(shape, dtype, name=name, align_bytes=64)
 
         def placed(name, shape, dtype, offset):
             return reused.tile(shape, dtype, name=name, align_bytes=64, offset=offset)
 
         def bank_tile(index, shape):
             return psum.tile(shape, F32, name="bank%d" % index, tag="bank%d" % index)
+
+        def zero(rows):
+            words = rows.bitcast(I32)
+            nc.vector.memset(words[:, 0:1], 0)
+            nc.vector.memset(words[:, 1:], 0)
 
         def load_planes(queue, planes, scales):
             for q in range(QUADRANTS):
@@ -58,63 +81,122 @@ def tile_list_partner_invitation_scores_kernel(
                     scales[:, 4 * q : 4 * q + 4, :].rearrange("a r c -> r a c").bitcast(I32),
                 )
 
-        partner_list = keep.tile([P, S // 16], U16, name="partner_list")
-        case_list = keep.tile([P, S // 16], U16, name="case_list")
-        table = [held("table%d" % a, [P, T], U16) for a in range(2)]
-        table_scales = held("table_scales", [P, T], U8)
-        w2_codes = [held("w2_codes%d" % c, [P, 2, HALF], U32) for c in range(2)]
-        w2_planes = held("w2_planes", [P, 2, H], U8)
-        w3_codes = held("w3_codes", [P, 2, 2 * N], U8)
-        w3_planes = held("w3_planes", [P, 2, N], U8)
-        gain_t = held("gain_t", [P, 2, PACK], F32)
-        log_gain = held("log_gain", [P, 2, PACK], F32, tag="dealt_codes%d" % FIRST)
-        bias = held("bias", [P, 2, PACK], F32)
-        gain_inv = held("gain_inv", [P, PACK], F32)
-        clinic_t = held("clinic_t", [P, OUT_TILES], F32)
-        identity = held("identity", [P, P], F32)
-        lowered = {name: held(name + "_lowered", [P, S], U8) for name in ("partner", "case")}
-
-        nc.vector.memset(table_scales[:].bitcast(I32), 0)
-        nc.gpsimd.memset(w2_planes[:].bitcast(I32), 0)
-        load_planes(nc.gpsimd, w2_planes, w2_scales)
-        for words in [plane[96:P, :] for plane in lowered.values()] + [w3_planes[:].rearrange("p a n -> p (a n)")]:
-            words = words.bitcast(I32)
-            nc.vector.memset(words[:, 0:1], 0)
-            nc.vector.memset(words[:, 1:], 0)
-        make_identity(nc, identity[:])
-
-        nc.sync.dma_start(partner_list[:], offs2)
-        w2_view = w2_words.rearrange("a p c i -> p a (c i)").bitcast(I32)
-        nc.sync.dma_start(gain_t[:], gain.rearrange("(c p t) -> p c t", c=2, t=PACK))
-        nc.sync.dma_start(w2_codes[FIRST][:, 0, :].bitcast(I32), w2_view[:, 0, HALF * FIRST : HALF * (FIRST + 1)])
-        for r in range(4):
-            nc.sync.dma_start(
-                table_scales[r:P:RAISED, :].bitcast(I32),
-                tab_scales.rearrange("a (q r) t -> r q a t", r=4)[r].bitcast(I32),
-            )
-        nc.sync.dma_start(table[0][:].bitcast(I32), tab_words[0].bitcast(I32))
-        nc.sync.dma_start(table[1][:].bitcast(I32), tab_words[1].bitcast(I32))
-
-        def gather_scales(name, offsets):
-            picked = held(name + "_picked", [P, S], U8)
-            nc.vector.tensor_copy(picked[:], table_scales[:].indirect(offsets[:]))
-            return [picked, lowered[name]]
-
-        def lower_scales(queue, planes):
-            for first, count in ((0, 64), (64, 32), (96, 4)):
+        def lay_planes(queue, planes, picked):
+            for q in range(QUADRANTS):
                 queue.dma_start(
-                    planes[1][first : first + count, :].bitcast(I32),
-                    planes[0][RAISED + first : RAISED + first + count, :].bitcast(I32),
+                    planes[32 * q : 32 * q + 4, :, :].bitcast(I32),
+                    picked[ROWS_AT + 8 * q : ROWS_AT + 8 * (q + 1), :].bitcast(I32),
                 )
 
-        def gather_words(picked, offsets, h):
-            for a in range(2):
-                columns = offsets[:, LIST_COLUMNS * h : LIST_COLUMNS * (h + 1)]
-                nc.vector.tensor_copy(picked[:, a, :], table[a][:].indirect(columns))
-            return [picked[:, a, :] for a in range(2)]
+        partner_list = keep.tile([P, S // 16], U16, name="partner_list")
+        case_list = keep.tile([P, S // 16], U16, name="case_list")
+        table = [placed("table%d" % a, [P, T], U16, TABLE_AT + 2 * T * a) for a in range(2)]
+        table_scales = placed("table_scales", [P, T], U8, TABLE_SCALES_AT)
+        w2_first = [placed("w2_first0", [P, HALF], U32, W2_FIRST_AT), held("w2_first1", [P, HALF], U32)]
+        w2_planes = held("w2_planes", [P, 2, H], U8)
+        gain_t = held("gain_t", [P, 2, PACK], F32)
+        log_gain = placed("log_gain", [P, 2, PACK], F32, DEALT_AT + 4096 * FIRST)
+        bias = held("bias", [P, 2, PACK], F32)
+        gain_inv = held("gain_inv", [P, PACK], F32)
+        early_planes = held("early_planes", [P, 2, HALF], U8)
+        late_planes = held("late_planes", [P, 2, HALF + S], U8)
+
+        zero(table_scales[0:ROWS_AT, :])
+        zero(early_planes[:].rearrange("p a n -> p (a n)"))
+        zero(late_planes[:].rearrange("p a n -> p (a n)"))
+        nc.gpsimd.memset(w2_planes[:].bitcast(I32), 0)
+        load_planes(nc.gpsimd, w2_planes, w2_scales)
+
+        w2_view = w2_words.rearrange("a p c i -> p a (c i)").bitcast(I32)
+        first_columns = slice(HALF * FIRST, HALF * (FIRST + 1))
+        nc.scalar.dma_start(gain_t[:], gain.rearrange("(c p t) -> p c t", c=2, t=PACK))
+        nc.sync.dma_start(partner_list[:], offs2)
+        nc.sync.dma_start(
+            table_scales[ROWS_AT:P, :].bitcast(I32), tab_scales.rearrange("a b t -> b a t").bitcast(I32)
+        )
+        nc.sync.dma_start(w2_first[0][:].bitcast(I32), w2_view[:, 0, first_columns])
+        nc.sync.dma_start(table[0][:].bitcast(I32), tab_words[0].bitcast(I32))
+        nc.sync.dma_start(table[1][:].bitcast(I32), tab_words[1].bitcast(I32))
+        nc.sync.dma_start(w2_first[1][:].bitcast(I32), w2_view[:, 1, first_columns])
+        nc.sync.dma_start(case_list[:], offs)
+
+        def list_half(offsets, h):
+            return offsets[:, LIST_COLUMNS * h : LIST_COLUMNS * (h + 1)]
+
+        def gather(picked, window, offsets):
+            nc.vector.tensor_copy(picked, window[:].indirect(offsets))
+            return picked
 
         def quantise(code, plane, values):
             nc.vector.quantize_mx(out=code.bitcast(FP8X4), scales=plane, in_=values)
+
+        nc.scalar.activation(log_gain[:], gain_t[:], ACT.Ln)
+        nc.scalar.activation(bias[:], log_gain[:], ACT.Identity, scale=-1.0)
+        nc.scalar.activation(gain_inv[:], log_gain[:, SECOND, :], ACT.Exp, scale=-1.0)
+
+        early_picked = placed("early_picked", [P, HALF], U8, EARLY_PICKED_AT)
+        late_picked = placed("late_picked", [P, HALF + S], U8, LATE_PICKED_AT)
+        gather(early_picked[:], table_scales, list_half(partner_list, 0))
+        lay_planes(nc.scalar, early_planes, early_picked)
+        gather(late_picked[:, 0:HALF], table_scales, list_half(partner_list, 1))
+
+        dealt_codes = [placed("dealt_codes%d" % c, [P, 2, HALF], U32, DEALT_AT + 4096 * c) for c in range(2)]
+        dealt_planes = [held("dealt_planes%d" % c, [P, 2, HALF], U8) for c in range(2)]
+
+        def deal_planes(c, a):
+            nc.gpsimd.tensor_copy(
+                dealt_planes[c][:, a, :].rearrange("p (t m) -> p t m", t=PACK),
+                w2_planes[:, a, HALF * c : HALF * (c + 1)].rearrange("p (m t) -> p t m", t=PACK),
+            )
+
+        def deal_codes(copy, c, a, words):
+            copy(
+                dealt_codes[c][:, a, :].rearrange("p (t n e) -> p n t e", t=PACK, e=PACK),
+                words.rearrange("p (n e t) -> p n t e", t=PACK, e=PACK),
+            )
+
+        for a in range(2):
+            deal_codes(nc.scalar.copy, FIRST, a, w2_first[a][:])
+            deal_planes(FIRST, a)
+
+        early_words = placed("early_words", [P, 2, HALF], U16, EARLY_WORDS_AT)
+        partner_words = [[gather(early_words[:, a, :], table[a], list_half(partner_list, 0)) for a in range(2)]]
+        gather(late_picked[:, HALF:], table_scales, case_list[:])
+        late_words = [
+            held("late_partner_words0", [P, HALF], U16),
+            placed("late_partner_words1", [P, HALF], U16, LATE_PARTNER_WORDS_AT),
+        ]
+        partner_words.append([gather(late_words[a][:], table[a], list_half(partner_list, 1)) for a in range(2)])
+
+        w2_second = placed("w2_second", [P, 2, HALF], U32, W2_SECOND_AT)
+        nc.sync.dma_start(w2_second[:].bitcast(I32), w2_view[:, :, HALF * SECOND : HALF * (SECOND + 1)])
+        w1_raw = {}
+        for c, a in ((c, a) for c in (FIRST, SECOND) for a in range(2)):
+            if (c, a) == (FIRST, 1):
+                lay_planes(nc.sync, late_planes, late_picked)
+            w1_raw[c, a] = placed("w1_raw%d%d" % (c, a), [P, PACK, HALF], F32, W1_AT[c, a])
+            nc.sync.dma_start(
+                w1_raw[c, a][:],
+                w1[PASS * a : PASS * (a + 1), HALF * c : HALF * (c + 1)].rearrange("(p i) r -> p i r", i=PACK),
+            )
+        w3_codes = placed("w3_codes", [P, 2, 2 * N], U8, W3_CODES_AT)
+        w3_planes = placed("w3_planes", [P, 2, N], U8, W3_PLANES_AT)
+        clinic_t = placed("clinic_t", [P, OUT_TILES], F32, CLINIC_AT)
+        zero(w3_planes[:].rearrange("p a n -> p (a n)"))
+        load_planes(nc.sync, w3_planes, w3_scales)
+        nc.sync.dma_start(w3_codes[:].bitcast(I32), w3_words.rearrange("a p b -> p a b").bitcast(I32))
+        with nc.allow_non_contiguous_dma(reason="one offset a partition"):
+            nc.sync.dma_start(clinic_t[:], clinic.rearrange("(n p) -> p n", p=P))
+
+        for a in range(2):
+            deal_planes(SECOND, a)
+        identity = placed("identity", [P, P], F32, EARLY_PICKED_AT)
+        make_identity(nc, identity[:])
+        for a in range(2):
+            deal_codes(nc.gpsimd.tensor_copy, SECOND, a, w2_second[:, a, :])
+
+        partner_planes = [early_planes[:], late_planes[:, :, 0:HALF]]
+        case_planes = [late_planes[:, :, HALF * (1 + h) : HALF * (2 + h)] for h in range(2)]
 
         def product(out_ap, stationary, moving, passes):
             for a in passes:
@@ -128,89 +210,42 @@ def tile_list_partner_invitation_scores_kernel(
                     stop=(a == passes[1]),
                 )
 
-        def picked_columns(words, planes, h, j0, width):
-            return [
-                (words[a][:, j0 : j0 + width].bitcast(FP4X4), planes[a][:, HALF * h + j0 : HALF * h + j0 + width])
-                for a in range(2)
-            ]
+        def picked_columns(words, planes, j0, width):
+            return [(words[a][:, j0 : j0 + width].bitcast(FP4X4), planes[:, a, j0 : j0 + width]) for a in range(2)]
 
         def weight_columns(weight, r0, width):
             return [(code[:, r0 : r0 + width].bitcast(FP8X4), plane[:, r0 : r0 + width]) for code, plane in weight]
 
-        def turned_stage(feature, h, words, planes, weight):
-            for jt in range(TILES):
-                bank = bank_tile(TILES * h + jt, [P, HALF])
-                product(bank[:], picked_columns(words, planes, h, P * jt, P), weight_columns(weight, 0, HALF), (1, 0))
-                nc.scalar.activation(feature[:, jt, :], bank[:], ACT.Exp)
+        stages = []
 
-        def dealt_stage(feature, c, h, words, planes, weight, passes=(1, 0)):
-            for t in range(PACK):
-                bank = bank_tile(TILES * h + t, [P, HALF])
-                product(bank[:], weight_columns(weight, P * t, P), picked_columns(words, planes, h, 0, HALF), passes)
+        def next_banks():
+            first = TILES * (len(stages) % 2)
+            stages.append(first)
+            return [bank_tile(first + index, [P, HALF]) for index in range(TILES)]
+
+        def turned_stage(feature, words, planes, weight, order):
+            for jt, bank in enumerate(next_banks()):
+                product(bank[:], picked_columns(words, planes, P * jt, P), weight_columns(weight, 0, HALF), (1, 0))
+                nc.scalar.activation(
+                    feature[:, jt, :].rearrange("p (t m) -> p t m", t=PACK), bank[:].rearrange(order, t=PACK), ACT.Exp
+                )
+
+        def dealt_stage(feature, c, words, planes, weight, passes=(1, 0)):
+            for t, bank in enumerate(next_banks()):
+                product(bank[:], weight_columns(weight, P * t, P), picked_columns(words, planes, 0, HALF), passes)
                 nc.scalar.activation(feature[:, t, :], bank[:], ACT.Exp, bias=bias[:, c, t : t + 1])
 
-        nc.scalar.activation(log_gain[:], gain_t[:], ACT.Ln)
-        nc.scalar.activation(bias[:], log_gain[:], ACT.Identity, scale=-1.0)
-        nc.scalar.activation(gain_inv[:], log_gain[:, SECOND, :], ACT.Exp, scale=-1.0)
+        turned = (SECOND, 0)
+        dealt = [(FIRST, 0), (FIRST, 1), (SECOND, 1)]
+        rb = {q: held("rb%d%d" % q, [P, PACK, HALF], F32) for q in dealt + [turned]}
+        ra = {q: held("ra%d%d" % q, [P, PACK, HALF], F32) for q in dealt + [turned]}
 
-        partner_planes = gather_scales("partner", partner_list)
-        nc.sync.dma_start(w2_codes[FIRST][:, 1, :].bitcast(I32), w2_view[:, 1, HALF * FIRST : HALF * (FIRST + 1)])
-        dealt_codes = [held("dealt_codes%d" % c, [P, 2, HALF], U32) for c in range(2)]
-        dealt_planes = [held("dealt_planes%d" % c, [P, 2, HALF], U8) for c in range(2)]
-
-        def deal_planes(c, a):
-            nc.gpsimd.tensor_copy(
-                dealt_planes[c][:, a, :].rearrange("p (t m) -> p t m", t=PACK),
-                w2_planes[:, a, HALF * c : HALF * (c + 1)].rearrange("p (m t) -> p t m", t=PACK),
-            )
-
-        def deal_codes(copy, c, a):
-            copy(
-                dealt_codes[c][:, a, :].rearrange("p (t n e) -> p n t e", t=PACK, e=PACK),
-                w2_codes[c][:, a, :].rearrange("p (n e t) -> p n t e", t=PACK, e=PACK),
-            )
-
-        for a in range(2):
-            deal_codes(nc.scalar.copy, FIRST, a)
-            deal_planes(FIRST, a)
-        lower_scales(nc.scalar, partner_planes)
-        nc.sync.dma_start(w2_codes[SECOND][:].bitcast(I32), w2_view[:, :, HALF * SECOND : HALF * (SECOND + 1)])
-        nc.sync.dma_start(case_list[:], offs)
-        for a in range(2):
-            deal_planes(SECOND, a)
-        for a in range(2):
-            deal_codes(nc.gpsimd.tensor_copy, SECOND, a)
-        partner_words = [gather_words(held("partner_words%d" % h, [P, 2, HALF], U16), partner_list, h) for h in range(2)]
-        case_planes = gather_scales("case", case_list)
-        w1_raw = {}
-        for index, (c, a) in enumerate((c, a) for c in (FIRST, SECOND) for a in range(2)):
-            if (c, a) == (SECOND, 1):
-                lower_scales(nc.sync, case_planes)
-            w1_raw[c, a] = placed("w1_raw%d%d" % (c, a), [P, PACK, HALF], F32, RAW_AT + 8192 * index)
-            nc.sync.dma_start(
-                w1_raw[c, a][:],
-                w1[PASS * a : PASS * (a + 1), HALF * c : HALF * (c + 1)].rearrange("(p i) r -> p i r", i=PACK),
-            )
-        nc.sync.dma_start(w3_codes[:].bitcast(I32), w3_words.rearrange("a p b -> p a b").bitcast(I32))
-        load_planes(nc.sync, w3_planes, w3_scales)
-        with nc.allow_non_contiguous_dma(reason="one offset a partition"):
-            nc.sync.dma_start(clinic_t[:], clinic.rearrange("(n p) -> p n", p=P))
-
-        quarters = [(c, h) for c in (FIRST, SECOND) for h in range(2)]
-        turned = quarters[-1]
-        rb = {q: held("rb%d%d" % q, [P, PACK, HALF], F32) for q in quarters}
-        ra = {q: held("ra%d%d" % q, [P, PACK, HALF], F32) for q in quarters}
-
-        def stage(feature, c, h, words, planes, weight, passes=(1, 0)):
-            if (c, h) == turned:
-                turned_stage(feature[c, h], h, words, planes, weight)
-            else:
-                dealt_stage(feature[c, h], c, h, words, planes, weight, passes)
-
-        for c, h in quarters:
-            w2_dealt = [(dealt_codes[c][:, a, :], dealt_planes[c][:, a, :]) for a in range(2)]
-            passes = (0, 1) if (c, h) == quarters[0] else (1, 0)
-            stage(rb, c, h, partner_words[h], partner_planes, w2_dealt, passes)
+        w2_dealt = [[(dealt_codes[c][:, a, :], dealt_planes[c][:, a, :]) for a in range(2)] for c in range(2)]
+        w2_loaded = [(w2_second[:, a, :], w2_planes[:, a, HALF * SECOND : HALF * (SECOND + 1)]) for a in range(2)]
+        dealt_stage(rb[FIRST, 0], FIRST, partner_words[0], partner_planes[0], w2_dealt[FIRST], (0, 1))
+        turned_stage(rb[turned], partner_words[0], partner_planes[0], w2_loaded, "p (m t) -> p t m")
+        for c in (FIRST, SECOND):
+            dealt_stage(rb[c, 1], c, partner_words[1], partner_planes[1], w2_dealt[c])
 
         def dealt_view(c, a):
             return w1_raw[c, a][:].rearrange("p i (m t) -> p m t i", t=PACK)
@@ -219,8 +254,8 @@ def tile_list_partner_invitation_scores_kernel(
             code = placed(name, [P, HALF], U32, offset) if offset else held(name, [P, HALF], U32)
             return code[:], held(name + "_plane", [P, HALF], U8)[:]
 
-        def quantise_w1(c, offsets, weight):
-            rounded = [placed("rounded%d%d" % (c, a), [P, PACK, P, PACK], BF16, offsets[a]) for a in range(2)]
+        def quantise_w1(c, weight):
+            rounded = [placed("rounded%d%d" % (c, a), [P, PACK, P, PACK], BF16, ROUNDED_AT[c, a]) for a in range(2)]
             values = [tile[:].rearrange("p t m i -> p m t i") for tile in rounded]
             for m0 in range(0, P, P // 2):
                 piece = slice(m0, m0 + P // 2)
@@ -232,22 +267,25 @@ def tile_list_partner_invitation_scores_kernel(
                     slices = tile[:, 2 * u : 2 * u + 2].rearrange("p t m i -> p (t m i)")
                     quantise(code[:, columns], plane[:, columns], slices)
 
-        case_words = [gather_words(held("case_words0", [P, 2, HALF], U16), case_list, 0)]
-        w1_first = [packed("w1_first%d" % a) for a in range(2)]
-        quantise_w1(FIRST, (0, 4096), w1_first)
-        case_words.append(gather_words(placed("case_words1", [P, 2, HALF], U16, 5120), case_list, 1))
-        for h in range(2):
-            stage(ra, FIRST, h, case_words[h], case_planes, w1_first)
+        def gather_cases(words, h):
+            return [gather(words[:, a, :], table[a], list_half(case_list, h)) for a in range(2)]
 
-        w1_second = [packed("w1_second0", RAW_AT + 32768), packed("w1_second1")]
-        quantise_w1(SECOND, (7168, 11264), w1_second)
+        case_words = [gather_cases(held("case_words0", [P, 2, HALF], U16), 0)]
+        w1_first = [packed("w1_first%d" % a, W1_CODES_AT + 2048 * (1 + a)) for a in range(2)]
+        quantise_w1(FIRST, w1_first)
+        case_words.append(gather_cases(placed("case_words1", [P, 2, HALF], U16, LATE_CASE_WORDS_AT), 1))
         for h in range(2):
-            stage(ra, SECOND, h, case_words[h], case_planes, w1_second)
+            dealt_stage(ra[FIRST, h], FIRST, case_words[h], case_planes[h], w1_first)
 
-        total = placed("total", [P, 3, PACK, HALF], F32, 13312)
-        for index, q in enumerate(quarters[:-1]):
+        w1_second = [packed("w1_second0", W1_CODES_AT), packed("w1_second1")]
+        quantise_w1(SECOND, w1_second)
+        dealt_stage(ra[SECOND, 1], SECOND, case_words[1], case_planes[1], w1_second)
+        turned_stage(ra[turned], case_words[0], case_planes[0], w1_second, "p (t m) -> p t m")
+
+        total = placed("total", [P, 3, PACK, HALF], F32, TOTAL_AT)
+        for index, q in enumerate(dealt):
             nc.vector.tensor_tensor(total[:, index], ra[q][:], rb[q][:], ALU.add)
-        sums = [bank_tile(t, [P, HALF]) for t in range(PACK)]
+        sums = next_banks()
         for jt in range(TILES):
             for t in range(PACK):
                 for index, term in enumerate((rb[turned], ra[turned])):
@@ -260,9 +298,9 @@ def tile_list_partner_invitation_scores_kernel(
                         is_transpose=True,
                     )
 
-        starts = [sum(CHUNKS[:index]) for index in range(len(CHUNKS))]
+        starts = [(TILES + sum(CHUNKS[:index])) % (2 * TILES) for index in range(len(CHUNKS))]
         steps = [(starts[index], tiles, c) for index, tiles in enumerate(CHUNKS) for c in (FIRST, SECOND)]
-        roots = placed("roots", [P, 4 * PACK * HALF], F32, RAW_AT + 2048)
+        roots = placed("roots", [P, 4 * PACK * HALF], F32, ROOTS_AT)
         y, places = {}, {"used": 0, "bank": 0}
 
         def root_room(width):
@@ -275,7 +313,7 @@ def tile_list_partner_invitation_scores_kernel(
             h, jt = divmod(first, TILES)
             if (c, h) != turned:
                 y[step] = root_room(P * tiles)
-                values = total[:, quarters.index((c, h)), :, P * jt : P * (jt + tiles)]
+                values = total[:, dealt.index((c, h)), :, P * jt : P * (jt + tiles)]
                 nc.scalar.activation(y[step], values, ACT.Abs_reciprocal_sqrt)
                 return
             if jt % 2 == 0:

@@ -35,20 +35,21 @@ ROUNDED_AT = {(FIRST, 0): 0, (FIRST, 1): 4096, (SECOND, 0): 7168, (SECOND, 1): 1
 LATE_CASE_WORDS_AT = 5120
 TOTAL_AT = 13312
 W2_SECOND_AT = 15360
-W2_FIRST_AT = 18432
-W1_AT = {(FIRST, 0): 19456, (FIRST, 1): 27648, (SECOND, 0): 38656, (SECOND, 1): 46848}
-TABLE_SCALES_AT = 34816
-LATE_PARTNER_WORDS_AT = 35840
-W3_PLANES_AT = 37888
-LATE_PICKED_AT = 54528
-CLINIC_AT = 55040
-W3_CODES_AT = 55104
-ROOTS_AT = 56640
+W2_FIRST_AT = 18944
+MIDDLE_PLANES_AT = 19456
+W1_AT = {(FIRST, 0): 20480, (FIRST, 1): 28672, (SECOND, 0): 36864, (SECOND, 1): 48128}
+EARLY_PICKED_AT = 36608
+TABLE_SCALES_AT = 45056
+W3_PLANES_AT = 45056
+CLINIC_AT = 45824
+W3_CODES_AT = 45888
+ROOTS_AT = 56320
 TABLE_AT = ROOTS_AT
 DEALT_AT = TABLE_AT + 16384
 W1_CODES_AT = DEALT_AT + 8192
 EARLY_WORDS_AT = W1_CODES_AT + 6144
-EARLY_PICKED_AT = EARLY_WORDS_AT + 2048
+IDENTITY_AT = EARLY_WORDS_AT + 2048
+LATE_PLANES_AT = IDENTITY_AT + 512
 
 
 def tile_list_partner_invitation_scores_kernel(
@@ -92,18 +93,16 @@ def tile_list_partner_invitation_scores_kernel(
         case_list = keep.tile([P, S // 16], U16, name="case_list")
         table = [placed("table%d" % a, [P, T], U16, TABLE_AT + 2 * T * a) for a in range(2)]
         table_scales = placed("table_scales", [P, T], U8, TABLE_SCALES_AT)
-        w2_first = [placed("w2_first0", [P, HALF], U32, W2_FIRST_AT), held("w2_first1", [P, HALF], U32)]
+        w2_first = [placed("w2_first0", [P, HALF], U32, W2_FIRST_AT), placed("w2_first1", [P, HALF], U32, LATE_PLANES_AT)]
         w2_planes = held("w2_planes", [P, 2, H], U8)
         gain_t = held("gain_t", [P, 2, PACK], F32)
         log_gain = placed("log_gain", [P, 2, PACK], F32, DEALT_AT + 4096 * FIRST)
         bias = held("bias", [P, 2, PACK], F32)
         gain_inv = held("gain_inv", [P, PACK], F32)
         early_planes = held("early_planes", [P, 2, HALF], U8)
-        late_planes = held("late_planes", [P, 2, HALF + S], U8)
 
         zero(table_scales[0:ROWS_AT, :])
         zero(early_planes[:].rearrange("p a n -> p (a n)"))
-        zero(late_planes[:].rearrange("p a n -> p (a n)"))
         nc.gpsimd.memset(w2_planes[:].bitcast(I32), 0)
         load_planes(nc.gpsimd, w2_planes, w2_scales)
 
@@ -135,10 +134,11 @@ def tile_list_partner_invitation_scores_kernel(
         nc.scalar.activation(gain_inv[:], log_gain[:, SECOND, :], ACT.Exp, scale=-1.0)
 
         early_picked = placed("early_picked", [P, HALF], U8, EARLY_PICKED_AT)
-        late_picked = placed("late_picked", [P, HALF + S], U8, LATE_PICKED_AT)
+        middle_picked = placed("middle_picked", [P, HALF], U8, IDENTITY_AT)
+        late_picked = held("late_picked", [P, S], U8)
         gather(early_picked[:], table_scales, list_half(partner_list, 0))
         lay_planes(nc.scalar, early_planes, early_picked)
-        gather(late_picked[:, 0:HALF], table_scales, list_half(partner_list, 1))
+        gather(middle_picked[:], table_scales, list_half(partner_list, 1))
 
         dealt_codes = [placed("dealt_codes%d" % c, [P, 2, HALF], U32, DEALT_AT + 4096 * c) for c in range(2)]
         dealt_planes = [held("dealt_planes%d" % c, [P, 2, HALF], U8) for c in range(2)]
@@ -161,18 +161,19 @@ def tile_list_partner_invitation_scores_kernel(
 
         early_words = placed("early_words", [P, 2, HALF], U16, EARLY_WORDS_AT)
         partner_words = [[gather(early_words[:, a, :], table[a], list_half(partner_list, 0)) for a in range(2)]]
-        gather(late_picked[:, HALF:], table_scales, case_list[:])
-        late_words = [
-            held("late_partner_words0", [P, HALF], U16),
-            placed("late_partner_words1", [P, HALF], U16, LATE_PARTNER_WORDS_AT),
-        ]
-        partner_words.append([gather(late_words[a][:], table[a], list_half(partner_list, 1)) for a in range(2)])
+        late_words = held("late_words", [P, 2, HALF], U16)
+        partner_words.append([gather(late_words[:, a, :], table[a], list_half(partner_list, 1)) for a in range(2)])
+        gather(late_picked[:], table_scales, case_list[:])
 
         w2_second = placed("w2_second", [P, 2, HALF], U32, W2_SECOND_AT)
         nc.sync.dma_start(w2_second[:].bitcast(I32), w2_view[:, :, HALF * SECOND : HALF * (SECOND + 1)])
         w1_raw = {}
         for c, a in ((c, a) for c in (FIRST, SECOND) for a in range(2)):
             if (c, a) == (FIRST, 1):
+                middle_planes = placed("middle_planes", [P, 2, HALF], U8, MIDDLE_PLANES_AT)
+                lay_planes(nc.sync, middle_planes, middle_picked)
+            if (c, a) == (SECOND, 1):
+                late_planes = placed("late_planes", [P, 2, S], U8, LATE_PLANES_AT)
                 lay_planes(nc.sync, late_planes, late_picked)
             w1_raw[c, a] = placed("w1_raw%d%d" % (c, a), [P, PACK, HALF], F32, W1_AT[c, a])
             nc.sync.dma_start(
@@ -182,7 +183,6 @@ def tile_list_partner_invitation_scores_kernel(
         w3_codes = placed("w3_codes", [P, 2, 2 * N], U8, W3_CODES_AT)
         w3_planes = placed("w3_planes", [P, 2, N], U8, W3_PLANES_AT)
         clinic_t = placed("clinic_t", [P, OUT_TILES], F32, CLINIC_AT)
-        zero(w3_planes[:].rearrange("p a n -> p (a n)"))
         load_planes(nc.sync, w3_planes, w3_scales)
         nc.sync.dma_start(w3_codes[:].bitcast(I32), w3_words.rearrange("a p b -> p a b").bitcast(I32))
         with nc.allow_non_contiguous_dma(reason="one offset a partition"):
@@ -190,13 +190,13 @@ def tile_list_partner_invitation_scores_kernel(
 
         for a in range(2):
             deal_planes(SECOND, a)
-        identity = placed("identity", [P, P], F32, EARLY_PICKED_AT)
+        identity = placed("identity", [P, P], F32, IDENTITY_AT)
         make_identity(nc, identity[:])
         for a in range(2):
             deal_codes(nc.gpsimd.tensor_copy, SECOND, a, w2_second[:, a, :])
 
-        partner_planes = [early_planes[:], late_planes[:, :, 0:HALF]]
-        case_planes = [late_planes[:, :, HALF * (1 + h) : HALF * (2 + h)] for h in range(2)]
+        partner_planes = [early_planes[:], middle_planes[:]]
+        case_planes = [late_planes[:, :, HALF * h : HALF * (1 + h)] for h in range(2)]
 
         def product(out_ap, stationary, moving, passes):
             for a in passes:
@@ -223,12 +223,10 @@ def tile_list_partner_invitation_scores_kernel(
             stages.append(first)
             return [bank_tile(first + index, [P, HALF]) for index in range(TILES)]
 
-        def turned_stage(feature, words, planes, weight, order):
+        def turned_stage(feature, words, planes, weight):
             for jt, bank in enumerate(next_banks()):
                 product(bank[:], picked_columns(words, planes, P * jt, P), weight_columns(weight, 0, HALF), (1, 0))
-                nc.scalar.activation(
-                    feature[:, jt, :].rearrange("p (t m) -> p t m", t=PACK), bank[:].rearrange(order, t=PACK), ACT.Exp
-                )
+                nc.scalar.activation(feature[:, jt, :], bank[:], ACT.Exp)
 
         def dealt_stage(feature, c, words, planes, weight, passes=(1, 0)):
             for t, bank in enumerate(next_banks()):
@@ -243,7 +241,7 @@ def tile_list_partner_invitation_scores_kernel(
         w2_dealt = [[(dealt_codes[c][:, a, :], dealt_planes[c][:, a, :]) for a in range(2)] for c in range(2)]
         w2_loaded = [(w2_second[:, a, :], w2_planes[:, a, HALF * SECOND : HALF * (SECOND + 1)]) for a in range(2)]
         dealt_stage(rb[FIRST, 0], FIRST, partner_words[0], partner_planes[0], w2_dealt[FIRST], (0, 1))
-        turned_stage(rb[turned], partner_words[0], partner_planes[0], w2_loaded, "p (m t) -> p t m")
+        turned_stage(rb[turned], partner_words[0], partner_planes[0], w2_loaded)
         for c in (FIRST, SECOND):
             dealt_stage(rb[c, 1], c, partner_words[1], partner_planes[1], w2_dealt[c])
 
@@ -280,7 +278,7 @@ def tile_list_partner_invitation_scores_kernel(
         w1_second = [packed("w1_second0", W1_CODES_AT), packed("w1_second1")]
         quantise_w1(SECOND, w1_second)
         dealt_stage(ra[SECOND, 1], SECOND, case_words[1], case_planes[1], w1_second)
-        turned_stage(ra[turned], case_words[0], case_planes[0], w1_second, "p (t m) -> p t m")
+        turned_stage(ra[turned], case_words[0], case_planes[0], w1_second)
 
         total = placed("total", [P, 3, PACK, HALF], F32, TOTAL_AT)
         for index, q in enumerate(dealt):
@@ -288,10 +286,10 @@ def tile_list_partner_invitation_scores_kernel(
         sums = next_banks()
         for jt in range(TILES):
             for t in range(PACK):
-                for index, term in enumerate((rb[turned], ra[turned])):
+                for index, term in enumerate((rb[turned][:, jt, t:HALF:PACK], ra[turned][:, jt, P * t : P * (t + 1)])):
                     nc.tensor.matmul(
                         sums[t][:, P * jt : P * (jt + 1)],
-                        term[:, jt, P * t : P * (t + 1)],
+                        term,
                         identity[:],
                         start=(index == 0),
                         stop=(index == 1),

@@ -35,10 +35,9 @@ ROUNDED_AT = {(FIRST, 0): 0, (FIRST, 1): 4096, (SECOND, 0): 7168, (SECOND, 1): 1
 LATE_CASE_WORDS_AT = 5120
 TOTAL_AT = 13312
 W2_SECOND_AT = 15360
-W2_FIRST_AT = 18944
-MIDDLE_PLANES_AT = 19456
-W1_AT = {(FIRST, 0): 20480, (FIRST, 1): 28672, (SECOND, 0): 36864, (SECOND, 1): 48128}
-EARLY_PICKED_AT = 36608
+W2_FIRST_AT = 18432
+W1_AT = {(FIRST, 0): 19456, (FIRST, 1): 28672, (SECOND, 0): 36864, (SECOND, 1): 48128}
+EARLY_PICKED_AT = 36352
 TABLE_SCALES_AT = 45056
 W3_PLANES_AT = 45056
 CLINIC_AT = 45824
@@ -48,8 +47,7 @@ TABLE_AT = ROOTS_AT
 DEALT_AT = TABLE_AT + 16384
 W1_CODES_AT = DEALT_AT + 8192
 EARLY_WORDS_AT = W1_CODES_AT + 6144
-IDENTITY_AT = EARLY_WORDS_AT + 2048
-LATE_PLANES_AT = IDENTITY_AT + 512
+LATE_PLANES_AT = EARLY_WORDS_AT + 2048
 
 
 def tile_list_partner_invitation_scores_kernel(
@@ -99,12 +97,14 @@ def tile_list_partner_invitation_scores_kernel(
         log_gain = placed("log_gain", [P, 2, PACK], F32, DEALT_AT + 4096 * FIRST)
         bias = held("bias", [P, 2, PACK], F32)
         gain_inv = held("gain_inv", [P, PACK], F32)
-        early_planes = held("early_planes", [P, 2, HALF], U8)
+        early_planes = held("early_planes", [P, 2, S], U8)
+        identity = held("identity", [P, P], F32)
 
         zero(table_scales[0:ROWS_AT, :])
         zero(early_planes[:].rearrange("p a n -> p (a n)"))
         nc.gpsimd.memset(w2_planes[:].bitcast(I32), 0)
         load_planes(nc.gpsimd, w2_planes, w2_scales)
+        make_identity(nc, identity[:])
 
         w2_view = w2_words.rearrange("a p c i -> p a (c i)").bitcast(I32)
         first_columns = slice(HALF * FIRST, HALF * (FIRST + 1))
@@ -133,12 +133,10 @@ def tile_list_partner_invitation_scores_kernel(
         nc.scalar.activation(bias[:], log_gain[:], ACT.Identity, scale=-1.0)
         nc.scalar.activation(gain_inv[:], log_gain[:, SECOND, :], ACT.Exp, scale=-1.0)
 
-        early_picked = placed("early_picked", [P, HALF], U8, EARLY_PICKED_AT)
-        middle_picked = placed("middle_picked", [P, HALF], U8, IDENTITY_AT)
+        early_picked = placed("early_picked", [P, S], U8, EARLY_PICKED_AT)
         late_picked = held("late_picked", [P, S], U8)
-        gather(early_picked[:], table_scales, list_half(partner_list, 0))
+        gather(early_picked[:], table_scales, partner_list[:])
         lay_planes(nc.scalar, early_planes, early_picked)
-        gather(middle_picked[:], table_scales, list_half(partner_list, 1))
 
         dealt_codes = [placed("dealt_codes%d" % c, [P, 2, HALF], U32, DEALT_AT + 4096 * c) for c in range(2)]
         dealt_planes = [held("dealt_planes%d" % c, [P, 2, HALF], U8) for c in range(2)]
@@ -169,9 +167,6 @@ def tile_list_partner_invitation_scores_kernel(
         nc.sync.dma_start(w2_second[:].bitcast(I32), w2_view[:, :, HALF * SECOND : HALF * (SECOND + 1)])
         w1_raw = {}
         for c, a in ((c, a) for c in (FIRST, SECOND) for a in range(2)):
-            if (c, a) == (FIRST, 1):
-                middle_planes = placed("middle_planes", [P, 2, HALF], U8, MIDDLE_PLANES_AT)
-                lay_planes(nc.sync, middle_planes, middle_picked)
             if (c, a) == (SECOND, 1):
                 late_planes = placed("late_planes", [P, 2, S], U8, LATE_PLANES_AT)
                 lay_planes(nc.sync, late_planes, late_picked)
@@ -190,15 +185,13 @@ def tile_list_partner_invitation_scores_kernel(
 
         for a in range(2):
             deal_planes(SECOND, a)
-        identity = placed("identity", [P, P], F32, IDENTITY_AT)
-        make_identity(nc, identity[:])
         for a in range(2):
             deal_codes(nc.gpsimd.tensor_copy, SECOND, a, w2_second[:, a, :])
 
-        partner_planes = [early_planes[:], middle_planes[:]]
+        partner_planes = [early_planes[:, :, HALF * h : HALF * (1 + h)] for h in range(2)]
         case_planes = [late_planes[:, :, HALF * h : HALF * (1 + h)] for h in range(2)]
 
-        def product(out_ap, stationary, moving, passes):
+        def product(out_ap, stationary, moving, passes=(1, 0), opening=1):
             for a in passes:
                 nc.tensor.matmul_mx(
                     out=out_ap,
@@ -206,8 +199,8 @@ def tile_list_partner_invitation_scores_kernel(
                     lhsT_scale=stationary[a][1],
                     rhs=moving[a][0],
                     rhs_scale=moving[a][1],
-                    start=(a == passes[0]),
-                    stop=(a == passes[1]),
+                    start=(a == opening),
+                    stop=(a != opening),
                 )
 
         def picked_columns(words, planes, j0, width):
@@ -225,25 +218,31 @@ def tile_list_partner_invitation_scores_kernel(
 
         def turned_stage(feature, words, planes, weight):
             for jt, bank in enumerate(next_banks()):
-                product(bank[:], picked_columns(words, planes, P * jt, P), weight_columns(weight, 0, HALF), (1, 0))
+                product(bank[:], picked_columns(words, planes, P * jt, P), weight_columns(weight, 0, HALF))
                 nc.scalar.activation(feature[:, jt, :], bank[:], ACT.Exp)
 
-        def dealt_stage(feature, c, words, planes, weight, passes=(1, 0)):
-            for t, bank in enumerate(next_banks()):
-                product(bank[:], weight_columns(weight, P * t, P), picked_columns(words, planes, 0, HALF), passes)
+        def dealt_stage(feature, c, words, planes, weight, early=False):
+            banks = next_banks()
+            moving = picked_columns(words, planes, 0, HALF)
+            if early:
+                for t, bank in enumerate(banks):
+                    product(bank[:], weight_columns(weight, P * t, P), moving, (0,), 0)
+            for t, bank in enumerate(banks):
+                if early:
+                    product(bank[:], weight_columns(weight, P * t, P), moving, (1,), 0)
+                else:
+                    product(bank[:], weight_columns(weight, P * t, P), moving)
                 nc.scalar.activation(feature[:, t, :], bank[:], ACT.Exp, bias=bias[:, c, t : t + 1])
 
-        turned = (SECOND, 0)
-        dealt = [(FIRST, 0), (FIRST, 1), (SECOND, 1)]
+        turned = (SECOND, 1)
+        dealt = [(FIRST, 0), (FIRST, 1), (SECOND, 0)]
         rb = {q: held("rb%d%d" % q, [P, PACK, HALF], F32) for q in dealt + [turned]}
         ra = {q: held("ra%d%d" % q, [P, PACK, HALF], F32) for q in dealt + [turned]}
 
         w2_dealt = [[(dealt_codes[c][:, a, :], dealt_planes[c][:, a, :]) for a in range(2)] for c in range(2)]
-        w2_loaded = [(w2_second[:, a, :], w2_planes[:, a, HALF * SECOND : HALF * (SECOND + 1)]) for a in range(2)]
-        dealt_stage(rb[FIRST, 0], FIRST, partner_words[0], partner_planes[0], w2_dealt[FIRST], (0, 1))
-        turned_stage(rb[turned], partner_words[0], partner_planes[0], w2_loaded)
-        for c in (FIRST, SECOND):
-            dealt_stage(rb[c, 1], c, partner_words[1], partner_planes[1], w2_dealt[c])
+        for c, h in dealt:
+            dealt_stage(rb[c, h], c, partner_words[h], partner_planes[h], w2_dealt[c], (c, h) == dealt[0])
+        turned_stage(rb[turned], partner_words[1], partner_planes[1], w2_dealt[SECOND])
 
         def dealt_view(c, a):
             return w1_raw[c, a][:].rearrange("p i (m t) -> p m t i", t=PACK)
@@ -277,8 +276,8 @@ def tile_list_partner_invitation_scores_kernel(
 
         w1_second = [packed("w1_second0", W1_CODES_AT), packed("w1_second1")]
         quantise_w1(SECOND, w1_second)
-        dealt_stage(ra[SECOND, 1], SECOND, case_words[1], case_planes[1], w1_second)
-        turned_stage(ra[turned], case_words[0], case_planes[0], w1_second)
+        dealt_stage(ra[SECOND, 0], SECOND, case_words[0], case_planes[0], w1_second)
+        turned_stage(ra[turned], case_words[1], case_planes[1], w1_second)
 
         total = placed("total", [P, 3, PACK, HALF], F32, TOTAL_AT)
         for index, q in enumerate(dealt):
@@ -286,17 +285,17 @@ def tile_list_partner_invitation_scores_kernel(
         sums = next_banks()
         for jt in range(TILES):
             for t in range(PACK):
-                for index, term in enumerate((rb[turned][:, jt, t:HALF:PACK], ra[turned][:, jt, P * t : P * (t + 1)])):
+                for index, term in enumerate((rb[turned], ra[turned])):
                     nc.tensor.matmul(
                         sums[t][:, P * jt : P * (jt + 1)],
-                        term,
+                        term[:, jt, P * t : P * (t + 1)],
                         identity[:],
                         start=(index == 0),
                         stop=(index == 1),
                         is_transpose=True,
                     )
 
-        starts = [(TILES + sum(CHUNKS[:index])) % (2 * TILES) for index in range(len(CHUNKS))]
+        starts = [sum(CHUNKS[:index]) for index in range(len(CHUNKS))]
         steps = [(starts[index], tiles, c) for index, tiles in enumerate(CHUNKS) for c in (FIRST, SECOND)]
         roots = placed("roots", [P, 4 * PACK * HALF], F32, ROOTS_AT)
         y, places = {}, {"used": 0, "bank": 0}

@@ -32,7 +32,6 @@ CHUNKS = (1, 1, 2, 2, 1, 1)
 AHEAD = 4
 
 ROUNDED_AT = {(FIRST, 0): 0, (FIRST, 1): 4096, (SECOND, 0): 7168, (SECOND, 1): 11264}
-LATE_CASE_WORDS_AT = 5120
 TOTAL_AT = 13312
 W2_SECOND_AT = 15360
 W2_FIRST_AT = 18432
@@ -254,10 +253,16 @@ def tile_list_partner_invitation_scores_kernel(
         def quantise_w1(c, weight):
             rounded = [placed("rounded%d%d" % (c, a), [P, PACK, P, PACK], BF16, ROUNDED_AT[c, a]) for a in range(2)]
             values = [tile[:].rearrange("p t m i -> p m t i") for tile in rounded]
-            for m0 in range(0, P, P // 2):
-                piece = slice(m0, m0 + P // 2)
-                nc.gpsimd.tensor_scalar(values[0][:, piece], dealt_view(c, 0)[:, piece], 1.0, 0.0, ALU.mult, ALU.add)
-            nc.vector.tensor_copy(values[1], dealt_view(c, 1))
+            if c == FIRST:
+                for a, m0 in ((0, 0), (0, P // 2), (1, 0)):
+                    piece = slice(m0, m0 + P // 2)
+                    nc.gpsimd.tensor_scalar(
+                        values[a][:, piece], dealt_view(c, a)[:, piece], 1.0, 0.0, ALU.mult, ALU.add
+                    )
+                nc.vector.tensor_copy(values[1][:, P // 2 :], dealt_view(c, 1)[:, P // 2 :])
+            else:
+                for a in range(2):
+                    nc.vector.tensor_copy(values[a], dealt_view(c, a))
             for u in range(2):
                 columns = slice(2 * P * u, 2 * P * (u + 1))
                 for (code, plane), tile in zip(weight, rounded):
@@ -267,10 +272,9 @@ def tile_list_partner_invitation_scores_kernel(
         def gather_cases(words, h):
             return [gather(words[:, a, :], table[a], list_half(case_list, h)) for a in range(2)]
 
-        case_words = [gather_cases(held("case_words0", [P, 2, HALF], U16), 0)]
+        case_words = [gather_cases(held("case_words%d" % h, [P, 2, HALF], U16), h) for h in range(2)]
         w1_first = [packed("w1_first%d" % a, W1_CODES_AT + 2048 * (1 + a)) for a in range(2)]
         quantise_w1(FIRST, w1_first)
-        case_words.append(gather_cases(placed("case_words1", [P, 2, HALF], U16, LATE_CASE_WORDS_AT), 1))
         for h in range(2):
             dealt_stage(ra[FIRST, h], FIRST, case_words[h], case_planes[h], w1_first)
 

@@ -29,7 +29,8 @@ NEIGHBOURS = 2
 ROWS_AT = 96
 FIRST, SECOND = 1, 0
 CHUNKS = (1, 1, 2, 2, 1, 1)
-AHEAD = 4
+HALVED = (0, 4)
+AHEAD = 6
 
 ROUNDED_AT = {(FIRST, 0): 0, (FIRST, 1): 4096, (SECOND, 0): 7168, (SECOND, 1): 11264}
 TOTAL_AT = 13312
@@ -95,7 +96,7 @@ def tile_list_partner_invitation_scores_kernel(
         gain_t = held("gain_t", [P, 2, PACK], F32)
         log_gain = placed("log_gain", [P, 2, PACK], F32, DEALT_AT + 4096 * FIRST)
         bias = held("bias", [P, 2, PACK], F32)
-        gain_inv = held("gain_inv", [P, PACK], F32)
+        gain_inv = held("gain_inv", [P, 2, PACK], F32)
         early_planes = held("early_planes", [P, 2, S], U8)
         identity = held("identity", [P, P], F32)
 
@@ -108,11 +109,11 @@ def tile_list_partner_invitation_scores_kernel(
         w2_view = w2_words.rearrange("a p c i -> p a (c i)").bitcast(I32)
         first_columns = slice(HALF * FIRST, HALF * (FIRST + 1))
         nc.scalar.dma_start(gain_t[:], gain.rearrange("(c p t) -> p c t", c=2, t=PACK))
+        nc.scalar.dma_start(w2_first[0][:].bitcast(I32), w2_view[:, 0, first_columns])
         nc.sync.dma_start(partner_list[:], offs2)
         nc.sync.dma_start(
             table_scales[ROWS_AT:P, :].bitcast(I32), tab_scales.rearrange("a b t -> b a t").bitcast(I32)
         )
-        nc.sync.dma_start(w2_first[0][:].bitcast(I32), w2_view[:, 0, first_columns])
         nc.sync.dma_start(table[0][:].bitcast(I32), tab_words[0].bitcast(I32))
         nc.sync.dma_start(table[1][:].bitcast(I32), tab_words[1].bitcast(I32))
         nc.sync.dma_start(w2_first[1][:].bitcast(I32), w2_view[:, 1, first_columns])
@@ -130,7 +131,7 @@ def tile_list_partner_invitation_scores_kernel(
 
         nc.scalar.activation(log_gain[:], gain_t[:], ACT.Ln)
         nc.scalar.activation(bias[:], log_gain[:], ACT.Identity, scale=-1.0)
-        nc.scalar.activation(gain_inv[:], log_gain[:, SECOND, :], ACT.Exp, scale=-1.0)
+        nc.scalar.activation(gain_inv[:], log_gain[:], ACT.Exp, scale=-1.0)
 
         early_picked = placed("early_picked", [P, S], U8, EARLY_PICKED_AT)
         late_picked = held("late_picked", [P, S], U8)
@@ -220,7 +221,7 @@ def tile_list_partner_invitation_scores_kernel(
                 product(bank[:], picked_columns(words, planes, P * jt, P), weight_columns(weight, 0, HALF))
                 nc.scalar.activation(feature[:, jt, :], bank[:], ACT.Exp)
 
-        def dealt_stage(feature, c, words, planes, weight, early=False):
+        def dealt_stage(feature, c, words, planes, weight, early=False, biased=True):
             banks = next_banks()
             moving = picked_columns(words, planes, 0, HALF)
             if early:
@@ -231,7 +232,10 @@ def tile_list_partner_invitation_scores_kernel(
                     product(bank[:], weight_columns(weight, P * t, P), moving, (1,), 0)
                 else:
                     product(bank[:], weight_columns(weight, P * t, P), moving)
-                nc.scalar.activation(feature[:, t, :], bank[:], ACT.Exp, bias=bias[:, c, t : t + 1])
+                if biased:
+                    nc.scalar.activation(feature[:, t, :], bank[:], ACT.Exp, bias=bias[:, c, t : t + 1])
+                else:
+                    nc.scalar.activation(feature[:, t, :], bank[:], ACT.Exp)
 
         turned = (SECOND, 1)
         dealt = [(FIRST, 0), (FIRST, 1), (SECOND, 0)]
@@ -240,7 +244,7 @@ def tile_list_partner_invitation_scores_kernel(
 
         w2_dealt = [[(dealt_codes[c][:, a, :], dealt_planes[c][:, a, :]) for a in range(2)] for c in range(2)]
         for c, h in dealt:
-            dealt_stage(rb[c, h], c, partner_words[h], partner_planes[h], w2_dealt[c], (c, h) == dealt[0])
+            dealt_stage(rb[c, h], c, partner_words[h], partner_planes[h], w2_dealt[c], (c, h) == dealt[0], False)
         turned_stage(rb[turned], partner_words[1], partner_planes[1], w2_dealt[SECOND])
 
         def dealt_view(c, a):
@@ -285,7 +289,10 @@ def tile_list_partner_invitation_scores_kernel(
 
         total = placed("total", [P, 3, PACK, HALF], F32, TOTAL_AT)
         for index, q in enumerate(dealt):
-            nc.vector.tensor_tensor(total[:, index], ra[q][:], rb[q][:], ALU.add)
+            for t in range(PACK):
+                nc.vector.scalar_tensor_tensor(
+                    total[:, index, t], rb[q][:, t], gain_inv[:, q[0], t : t + 1], ra[q][:, t], ALU.mult, ALU.add
+                )
         sums = next_banks()
         for jt in range(TILES):
             for t in range(PACK):
@@ -309,13 +316,18 @@ def tile_list_partner_invitation_scores_kernel(
             places["used"] = used + PACK * width
             return roots[:, used : used + PACK * width].rearrange("p (t j) -> p t j", t=PACK)
 
+        def pieces(step):
+            width = P * steps[step][1]
+            return [slice(0, width // 2), slice(width // 2, width)] if step in HALVED else [slice(0, width)]
+
         def make_root(step):
             first, tiles, c = steps[step]
             h, jt = divmod(first, TILES)
             if (c, h) != turned:
                 y[step] = root_room(P * tiles)
                 values = total[:, dealt.index((c, h)), :, P * jt : P * (jt + tiles)]
-                nc.scalar.activation(y[step], values, ACT.Abs_reciprocal_sqrt)
+                for piece in pieces(step):
+                    nc.scalar.activation(y[step][:, :, piece], values[:, :, piece], ACT.Abs_reciprocal_sqrt)
                 return
             if jt % 2 == 0:
                 places["turned"] = root_room(2 * P)
@@ -324,16 +336,17 @@ def tile_list_partner_invitation_scores_kernel(
                         places["turned"][:, t, :],
                         sums[t][:, P * jt : P * (jt + 2)],
                         ACT.Abs_reciprocal_sqrt,
-                        scale=gain_inv[:, t : t + 1],
+                        scale=gain_inv[:, SECOND, t : t + 1],
                     )
             y[step] = places["turned"][:, :, P * (jt % 2) : P * (jt % 2 + tiles)]
 
         def square(step):
             width = P * steps[step][1]
             grouped = held("h_grouped%d" % step, [P, width, PACK], BF16)
-            values = y[step].rearrange("p t (n e) -> p n t e", e=NEIGHBOURS)
-            target = grouped[:].rearrange("p (n e) t -> p n t e", e=NEIGHBOURS)
-            nc.vector.tensor_tensor(target, values, values, ALU.mult)
+            for piece in pieces(step):
+                values = y[step][:, :, piece].rearrange("p t (n e) -> p n t e", e=NEIGHBOURS)
+                target = grouped[:, piece, :].rearrange("p (n e) t -> p n t e", e=NEIGHBOURS)
+                nc.vector.tensor_tensor(target, values, values, ALU.mult)
             return grouped[:].rearrange("p n t -> p (n t)")
 
         def quantise_h(step):

@@ -254,6 +254,12 @@ def tile_list_partner_invitation_scores_kernel(
             code = placed(name, [P, HALF], U32, offset) if offset else held(name, [P, HALF], U32)
             return code[:], held(name + "_plane", [P, HALF], U8)[:]
 
+        def round_w1(tile, c, a, ms, ts):
+            nc.vector.tensor_copy(
+                tile[:].rearrange("p t m (u e) -> p m u t e", e=2)[:, ms, :, ts],
+                w1_raw[c, a][:].rearrange("p (u e) (m t) -> p m u t e", e=2, t=PACK)[:, ms, :, ts],
+            )
+
         def quantise_w1(c, weight):
             rounded = [placed("rounded%d%d" % (c, a), [P, PACK, P, PACK], BF16, ROUNDED_AT[c, a]) for a in range(2)]
             values = [tile[:].rearrange("p t m i -> p m t i") for tile in rounded]
@@ -263,14 +269,14 @@ def tile_list_partner_invitation_scores_kernel(
                     nc.gpsimd.tensor_scalar(
                         values[a][:, piece], dealt_view(c, a)[:, piece], 1.0, 0.0, ALU.mult, ALU.add
                     )
-                nc.vector.tensor_copy(values[1][:, P // 2 :], dealt_view(c, 1)[:, P // 2 :])
-            else:
-                for a in range(2):
-                    nc.vector.tensor_copy(values[a], dealt_view(c, a))
-            for u in range(2):
-                columns = slice(2 * P * u, 2 * P * (u + 1))
-                for (code, plane), tile in zip(weight, rounded):
-                    slices = tile[:, 2 * u : 2 * u + 2].rearrange("p t m i -> p (t m i)")
+                round_w1(rounded[1], c, 1, slice(P // 2, P), slice(0, PACK))
+            for t in range(0, PACK, 2):
+                columns = slice(P * t, P * (t + 2))
+                if c == SECOND:
+                    for a in range(2):
+                        round_w1(rounded[a], c, a, slice(0, P), slice(t, t + 2))
+                for a, (code, plane) in enumerate(weight):
+                    slices = rounded[a][:, t : t + 2].rearrange("p t m i -> p (t m i)")
                     quantise(code[:, columns], plane[:, columns], slices)
 
         def gather_cases(words, h):

@@ -30,6 +30,7 @@ ROWS_AT = 96
 FIRST, SECOND = 1, 0
 CHUNKS = (1, 1, 2, 2, 1, 1)
 HALVED = (0, 4)
+SHARE = 32
 AHEAD = 6
 
 ROUNDED_AT = {(FIRST, 0): 0, (FIRST, 1): 4096, (SECOND, 0): 7168, (SECOND, 1): 11264}
@@ -244,7 +245,7 @@ def tile_list_partner_invitation_scores_kernel(
 
         w2_dealt = [[(dealt_codes[c][:, a, :], dealt_planes[c][:, a, :]) for a in range(2)] for c in range(2)]
         for c, h in dealt:
-            dealt_stage(rb[c, h], c, partner_words[h], partner_planes[h], w2_dealt[c], (c, h) == dealt[0], False)
+            dealt_stage(rb[c, h], c, partner_words[h], partner_planes[h], w2_dealt[c], (c, h) == dealt[0])
         turned_stage(rb[turned], partner_words[1], partner_planes[1], w2_dealt[SECOND])
 
         def dealt_view(c, a):
@@ -264,15 +265,15 @@ def tile_list_partner_invitation_scores_kernel(
             rounded = [placed("rounded%d%d" % (c, a), [P, PACK, P, PACK], BF16, ROUNDED_AT[c, a]) for a in range(2)]
             values = [tile[:].rearrange("p t m i -> p m t i") for tile in rounded]
             if c == FIRST:
-                for a, m0 in ((0, 0), (0, P // 2), (1, 0)):
-                    piece = slice(m0, m0 + P // 2)
+                for a, m0, m1 in ((0, 0, P // 2), (0, P // 2, P), (1, 0, SHARE)):
                     nc.gpsimd.tensor_scalar(
-                        values[a][:, piece], dealt_view(c, a)[:, piece], 1.0, 0.0, ALU.mult, ALU.add
+                        values[a][:, m0:m1], dealt_view(c, a)[:, m0:m1], 1.0, 0.0, ALU.mult, ALU.add
                     )
-                round_w1(rounded[1], c, 1, slice(P // 2, P), slice(0, PACK))
             for t in range(0, PACK, 2):
                 columns = slice(P * t, P * (t + 2))
-                if c == SECOND:
+                if c == FIRST:
+                    round_w1(rounded[1], c, 1, slice(SHARE, P), slice(t, t + 2))
+                else:
                     for a in range(2):
                         round_w1(rounded[a], c, a, slice(0, P), slice(t, t + 2))
                 for a, (code, plane) in enumerate(weight):
@@ -286,18 +287,18 @@ def tile_list_partner_invitation_scores_kernel(
         w1_first = [packed("w1_first%d" % a, W1_CODES_AT + 2048 * (1 + a)) for a in range(2)]
         quantise_w1(FIRST, w1_first)
         for h in range(2):
-            dealt_stage(ra[FIRST, h], FIRST, case_words[h], case_planes[h], w1_first)
+            dealt_stage(ra[FIRST, h], FIRST, case_words[h], case_planes[h], w1_first, biased=False)
 
         w1_second = [packed("w1_second0", W1_CODES_AT), packed("w1_second1")]
         quantise_w1(SECOND, w1_second)
-        dealt_stage(ra[SECOND, 0], SECOND, case_words[0], case_planes[0], w1_second)
+        dealt_stage(ra[SECOND, 0], SECOND, case_words[0], case_planes[0], w1_second, biased=False)
         turned_stage(ra[turned], case_words[1], case_planes[1], w1_second)
 
         total = placed("total", [P, 3, PACK, HALF], F32, TOTAL_AT)
         for index, q in enumerate(dealt):
             for t in range(PACK):
                 nc.vector.scalar_tensor_tensor(
-                    total[:, index, t], rb[q][:, t], gain_inv[:, q[0], t : t + 1], ra[q][:, t], ALU.mult, ALU.add
+                    total[:, index, t], ra[q][:, t], gain_inv[:, q[0], t : t + 1], rb[q][:, t], ALU.mult, ALU.add
                 )
         sums = next_banks()
         for jt in range(TILES):

@@ -29,6 +29,8 @@ NEIGHBOURS = 2
 ROWS_AT = 96
 FIRST, SECOND = 1, 0
 CHUNKS = (1, 1, 2, 2, 1, 1)
+GROUPS = ((0, 1, 2), (3,), (4,), (5,))
+SCORE_BANKS = ((4, 5, 6), (7, 0, 1), (2, 3, 4), (5, 6, 7))
 HALVED = (0, 4)
 SHARE = 32
 AHEAD = 6
@@ -222,21 +224,27 @@ def tile_list_partner_invitation_scores_kernel(
                 product(bank[:], picked_columns(words, planes, P * jt, P), weight_columns(weight, 0, HALF))
                 nc.scalar.activation(feature[:, jt, :], bank[:], ACT.Exp)
 
-        def dealt_stage(feature, c, words, planes, weight, early=False, biased=True):
-            banks = next_banks()
-            moving = picked_columns(words, planes, 0, HALF)
+        def dealt_stage(feature, c, slices, words, planes, weight, early=False, biased=True):
+            work = list(zip(next_banks(), slices))
             if early:
-                for t, bank in enumerate(banks):
-                    product(bank[:], weight_columns(weight, P * t, P), moving, (0,), 0)
-            for t, bank in enumerate(banks):
+                for bank, (h, t) in work:
+                    product(bank[:], weight_columns(weight, P * t, P), picked_columns(words[h], planes[h], 0, HALF), (0,), 0)
+            for bank, (h, t) in work:
+                moving = picked_columns(words[h], planes[h], 0, HALF)
                 if early:
                     product(bank[:], weight_columns(weight, P * t, P), moving, (1,), 0)
                 else:
                     product(bank[:], weight_columns(weight, P * t, P), moving)
                 if biased:
-                    nc.scalar.activation(feature[:, t, :], bank[:], ACT.Exp, bias=bias[:, c, t : t + 1])
+                    nc.scalar.activation(feature[c, h][:, t, :], bank[:], ACT.Exp, bias=bias[:, c, t : t + 1])
                 else:
-                    nc.scalar.activation(feature[:, t, :], bank[:], ACT.Exp)
+                    nc.scalar.activation(feature[c, h][:, t, :], bank[:], ACT.Exp)
+
+        def all_slices(h):
+            return [(h, t) for t in range(PACK)]
+
+        def slice_pair(t0):
+            return [(h, t) for h in range(2) for t in (t0, t0 + 1)]
 
         turned = (SECOND, 1)
         dealt = [(FIRST, 0), (FIRST, 1), (SECOND, 0)]
@@ -245,7 +253,7 @@ def tile_list_partner_invitation_scores_kernel(
 
         w2_dealt = [[(dealt_codes[c][:, a, :], dealt_planes[c][:, a, :]) for a in range(2)] for c in range(2)]
         for c, h in dealt:
-            dealt_stage(rb[c, h], c, partner_words[h], partner_planes[h], w2_dealt[c], (c, h) == dealt[0])
+            dealt_stage(rb, c, all_slices(h), partner_words, partner_planes, w2_dealt[c], (c, h) == dealt[0])
         turned_stage(rb[turned], partner_words[1], partner_planes[1], w2_dealt[SECOND])
 
         def dealt_view(c, a):
@@ -286,12 +294,12 @@ def tile_list_partner_invitation_scores_kernel(
         case_words = [gather_cases(held("case_words%d" % h, [P, 2, HALF], U16), h) for h in range(2)]
         w1_first = [packed("w1_first%d" % a, W1_CODES_AT + 2048 * (1 + a)) for a in range(2)]
         quantise_w1(FIRST, w1_first)
-        for h in range(2):
-            dealt_stage(ra[FIRST, h], FIRST, case_words[h], case_planes[h], w1_first, biased=False)
+        for t0 in (0, 2):
+            dealt_stage(ra, FIRST, slice_pair(t0), case_words, case_planes, w1_first, biased=False)
 
         w1_second = [packed("w1_second0", W1_CODES_AT), packed("w1_second1")]
         quantise_w1(SECOND, w1_second)
-        dealt_stage(ra[SECOND, 0], SECOND, case_words[0], case_planes[0], w1_second, biased=False)
+        dealt_stage(ra, SECOND, all_slices(0), case_words, case_planes, w1_second, biased=False)
         turned_stage(ra[turned], case_words[1], case_planes[1], w1_second)
 
         total = placed("total", [P, 3, PACK, HALF], F32, TOTAL_AT)
@@ -316,7 +324,7 @@ def tile_list_partner_invitation_scores_kernel(
         starts = [sum(CHUNKS[:index]) for index in range(len(CHUNKS))]
         steps = [(starts[index], tiles, c) for index, tiles in enumerate(CHUNKS) for c in (FIRST, SECOND)]
         roots = placed("roots", [P, 4 * PACK * HALF], F32, ROOTS_AT)
-        y, places = {}, {"used": 0, "bank": 0}
+        y, places = {}, {"used": 0}
 
         def root_room(width):
             used = places["used"]
@@ -364,22 +372,19 @@ def tile_list_partner_invitation_scores_kernel(
             return code[:], plane[:]
 
         def multiply(chunk, operands):
-            width = P * CHUNKS[chunk]
-            last = chunk == len(CHUNKS) - 1
-            per_bank = 1 if last else HALF // width
-            views = []
-            for n0 in range(0, OUT_TILES, per_bank):
-                index = n0 if last else TILES + places["bank"] % TILES
-                places["bank"] = places["bank"] + 1
-                bank = bank_tile(index, [P, min(per_bank, OUT_TILES - n0), width])
-                views.extend(bank[:, n, :] for n in range(bank.shape[1]))
+            group = [index for index, members in enumerate(GROUPS) if chunk in members][0]
+            opening = GROUPS[group][0]
+            if chunk == opening:
+                reach = P * sum(CHUNKS[member] for member in GROUPS[group])
+                places["scores"] = [bank_tile(index, [P, reach]) for index in SCORE_BANKS[group]]
+            columns = slice(P * (starts[chunk] - starts[opening]), P * (starts[chunk] - starts[opening] + CHUNKS[chunk]))
             halves = list(zip((FIRST, SECOND), operands))
             passes = [(n, half) for n in range(OUT_TILES) for half in halves]
-            if last:
+            if chunk == len(CHUNKS) - 1:
                 passes = [(n, half) for half in halves for n in range(OUT_TILES)]
             for n, (c, (code, plane)) in passes:
                 nc.tensor.matmul_mx(
-                    out=views[n],
+                    out=places["scores"][n][:, columns],
                     lhsT=w3_codes[:, c, 2 * P * n : 2 * P * (n + 1)].bitcast(FP4X4),
                     lhsT_scale=w3_planes[:, c, P * n : P * (n + 1)],
                     rhs=code.bitcast(FP8X4),
@@ -387,16 +392,17 @@ def tile_list_partner_invitation_scores_kernel(
                     start=(c == FIRST),
                     stop=(c == SECOND),
                 )
-            return views
+            if chunk == GROUPS[group][-1]:
+                store(opening, places["scores"])
 
-        def store(chunk, views):
-            first, width = starts[chunk], P * CHUNKS[chunk]
+        def store(chunk, banks):
+            first, width = starts[chunk], banks[0].shape[1]
             for n in range(OUT_TILES):
                 scores = held("scores%d%d" % (chunk, n), [P, width], F32)
                 if chunk == len(CHUNKS) - 1 and n == 1:
-                    nc.vector.tensor_scalar(scores[:], views[n], clinic_t[:, n : n + 1], None, ALU.add)
+                    nc.vector.tensor_scalar(scores[:], banks[n][:], clinic_t[:, n : n + 1], None, ALU.add)
                 else:
-                    nc.scalar.activation(scores[:], views[n], ACT.Identity, bias=clinic_t[:, n : n + 1])
+                    nc.scalar.activation(scores[:], banks[n][:], ACT.Identity, bias=clinic_t[:, n : n + 1])
                 nc.sync.dma_start(out[P * n : P * (n + 1), P * first : P * first + width], scores[:])
 
         count = len(steps)
@@ -411,4 +417,4 @@ def tile_list_partner_invitation_scores_kernel(
             if step > 0:
                 made.append(quantise_h(step - 1))
                 if step % 2 == 0:
-                    store(step // 2 - 1, multiply(step // 2 - 1, made[-2:]))
+                    multiply(step // 2 - 1, made[-2:])

@@ -31,6 +31,7 @@ FIRST, SECOND = 1, 0
 CHUNKS = (1, 1, 2, 2, 1, 1)
 GROUPS = ((0, 1, 2), (3,), (4,), (5,))
 SCORE_BANKS = ((4, 5, 6), (7, 0, 1), (2, 3, 4), (5, 6, 7))
+EARLY = 1
 HALVED = (0, 4)
 SHARE = 32
 AHEAD = 6
@@ -227,11 +228,11 @@ def tile_list_partner_invitation_scores_kernel(
         def dealt_stage(feature, c, slices, words, planes, weight, early=False, biased=True):
             work = list(zip(next_banks(), slices))
             if early:
-                for bank, (h, t) in work:
+                for bank, (h, t) in work[:EARLY]:
                     product(bank[:], weight_columns(weight, P * t, P), picked_columns(words[h], planes[h], 0, HALF), (0,), 0)
             for bank, (h, t) in work:
                 moving = picked_columns(words[h], planes[h], 0, HALF)
-                if early:
+                if early and t < EARLY:
                     product(bank[:], weight_columns(weight, P * t, P), moving, (1,), 0)
                 else:
                     product(bank[:], weight_columns(weight, P * t, P), moving)

from contextlib import ExitStack

import concourse.mybir as mybir
from concourse.masks import make_identity

K, T, S, H, N = 1024, 4096, 1024, 1024, 384
FLOPS = 2 * (2 * K * H * S + H * N * S)

F32 = mybir.dt.float32
BF16 = mybir.dt.bfloat16
I32 = mybir.dt.int32
U32 = mybir.dt.uint32
U16 = mybir.dt.uint16
U8 = mybir.dt.uint8
FP8X4 = mybir.dt.float8_e4m3fn_x4
FP4X4 = mybir.dt.float4_e2m1fn_x4
ACT = mybir.ActivationFunctionType
ALU = mybir.AluOpType

P = 128
PACK = 4
PASS = P * PACK
QUADRANTS = 4
HALF = 512
TILES = HALF // P
OUT_TILES = N // P
LIST_COLUMNS = HALF // 16
NEIGHBOURS = 2
ROWS_AT = 96
FIRST, SECOND = 1, 0
CHUNKS = (1, 1, 2, 2, 1, 1)
GROUPS = ((0, 1, 2), (3,), (4,), (5,))
SCORE_BANKS = ((4, 5, 6), (7, 0, 1), (2, 3, 4), (5, 6, 7))
EARLY = 1
HALVED = (0, 4)
SHARE = 32
AHEAD = 6

ROUNDED_AT = {(FIRST, 0): 0, (FIRST, 1): 4096, (SECOND, 0): 7168, (SECOND, 1): 11264}
TOTAL_AT = 13312
W2_SECOND_AT = 15360
W2_FIRST_AT = 18432
W1_AT = {(FIRST, 0): 19456, (FIRST, 1): 28672, (SECOND, 0): 36864, (SECOND, 1): 48128}
EARLY_PICKED_AT = 36352
TABLE_SCALES_AT = 45056
W3_PLANES_AT = 45056
CLINIC_AT = 45824
W3_CODES_AT = 45888
ROOTS_AT = 56320
TABLE_AT = ROOTS_AT
DEALT_AT = TABLE_AT + 16384
W1_CODES_AT = DEALT_AT + 8192
EARLY_WORDS_AT = W1_CODES_AT + 6144
LATE_PLANES_AT = EARLY_WORDS_AT + 2048


def tile_list_partner_invitation_scores_kernel(
    tc, tab_words, tab_scales, offs, offs2, w1, w2_words, w2_scales, gain, w3_words, w3_scales, clinic, out
):
    nc = tc.nc
    with ExitStack() as ctx:
        keep = ctx.enter_context(tc.tile_pool(name="keep", bufs=1))
        reused = ctx.enter_context(tc.tile_pool(name="reused", bufs=1))
        psum = ctx.enter_context(tc.psum_pool(name="psum", bufs=1))

        def held(name, shape, dtype):
            return keep.tile(shape, dtype, name=name, align_bytes=64)

        def placed(name, shape, dtype, offset):
            return reused.tile(shape, dtype, name=name, align_bytes=64, offset=offset)

        def bank_tile(index, shape):
            return psum.tile(shape, F32, name="bank%d" % index, tag="bank%d" % index)

        def zero(rows):
            words = rows.bitcast(I32)
            nc.vector.memset(words[:, 0:1], 0)
            nc.vector.memset(words[:, 1:], 0)

        def load_planes(queue, planes, scales):
            for q in range(QUADRANTS):
                queue.dma_start(
                    planes[32 * q : 32 * q + 4, :, :].bitcast(I32),
                    scales[:, 4 * q : 4 * q + 4, :].rearrange("a r c -> r a c").bitcast(I32),
                )

        def lay_planes(queue, planes, picked):
            for q in range(QUADRANTS):
                queue.dma_start(
                    planes[32 * q : 32 * q + 4, :, :].bitcast(I32),
                    picked[ROWS_AT + 8 * q : ROWS_AT + 8 * (q + 1), :].bitcast(I32),
                )

        partner_list = keep.tile([P, S // 16], U16, name="partner_list")
        case_list = keep.tile([P, S // 16], U16, name="case_list")
        table = [placed("table%d" % a, [P, T], U16, TABLE_AT + 2 * T * a) for a in range(2)]
        table_scales = placed("table_scales", [P, T], U8, TABLE_SCALES_AT)
        w2_first = [placed("w2_first0", [P, HALF], U32, W2_FIRST_AT), placed("w2_first1", [P, HALF], U32, LATE_PLANES_AT)]
        w2_planes = held("w2_planes", [P, 2, H], U8)
        gain_t = held("gain_t", [P, 2, PACK], F32)
        log_gain = placed("log_gain", [P, 2, PACK], F32, DEALT_AT + 4096 * FIRST)
        bias = held("bias", [P, 2, PACK], F32)
        gain_inv = held("gain_inv", [P, 2, PACK], F32)
        early_planes = held("early_planes", [P, 2, S], U8)
        identity = held("identity", [P, P], F32)

        zero(table_scales[0:ROWS_AT, :])
        zero(early_planes[:].rearrange("p a n -> p (a n)"))
        nc.gpsimd.memset(w2_planes[:].bitcast(I32), 0)
        load_planes(nc.gpsimd, w2_planes, w2_scales)
        make_identity(nc, identity[:])

        w2_view = w2_words.rearrange("a p c i -> p a (c i)").bitcast(I32)
        first_columns = slice(HALF * FIRST, HALF * (FIRST + 1))
        nc.scalar.dma_start(gain_t[:], gain.rearrange("(c p t) -> p c t", c=2, t=PACK))
        nc.scalar.dma_start(w2_first[0][:].bitcast(I32), w2_view[:, 0, first_columns])
        nc.sync.dma_start(partner_list[:], offs2)
        nc.sync.dma_start(
            table_scales[ROWS_AT:P, :].bitcast(I32), tab_scales.rearrange("a b t -> b a t").bitcast(I32)
        )
        nc.sync.dma_start(table[0][:].bitcast(I32), tab_words[0].bitcast(I32))
        nc.sync.dma_start(table[1][:].bitcast(I32), tab_words[1].bitcast(I32))
        nc.sync.dma_start(w2_first[1][:].bitcast(I32), w2_view[:, 1, first_columns])
        nc.sync.dma_start(case_list[:], offs)

        def list_half(offsets, h):
            return offsets[:, LIST_COLUMNS * h : LIST_COLUMNS * (h + 1)]

        def gather(picked, window, offsets):
            nc.vector.tensor_copy(picked, window[:].indirect(offsets))
            return picked

        def quantise(code, plane, values):
            nc.vector.quantize_mx(out=code.bitcast(FP8X4), scales=plane, in_=values)

        nc.scalar.activation(log_gain[:], gain_t[:], ACT.Ln)
        nc.scalar.activation(bias[:], log_gain[:], ACT.Identity, scale=-1.0)
        nc.scalar.activation(gain_inv[:], log_gain[:], ACT.Exp, scale=-1.0)

        early_picked = placed("early_picked", [P, S], U8, EARLY_PICKED_AT)
        late_picked = held("late_picked", [P, S], U8)
        gather(early_picked[:], table_scales, partner_list[:])
        lay_planes(nc.scalar, early_planes, early_picked)

        dealt_codes = [placed("dealt_codes%d" % c, [P, 2, HALF], U32, DEALT_AT + 4096 * c) for c in range(2)]
        dealt_planes = [held("dealt_planes%d" % c, [P, 2, HALF], U8) for c in range(2)]

        def deal_planes(c, a):
            nc.gpsimd.tensor_copy(
                dealt_planes[c][:, a, :].rearrange("p (t m) -> p t m", t=PACK),
                w2_planes[:, a, HALF * c : HALF * (c + 1)].rearrange("p (m t) -> p t m", t=PACK),
            )

        def deal_codes(copy, c, a, words):
            copy(
                dealt_codes[c][:, a, :].rearrange("p (t n e) -> p n t e", t=PACK, e=PACK),
                words.rearrange("p (n e t) -> p n t e", t=PACK, e=PACK),
            )

        for a in range(2):
            deal_codes(nc.scalar.copy, FIRST, a, w2_first[a][:])
            deal_planes(FIRST, a)

        early_words = placed("early_words", [P, 2, HALF], U16, EARLY_WORDS_AT)
        partner_words = [[gather(early_words[:, a, :], table[a], list_half(partner_list, 0)) for a in range(2)]]
        late_words = held("late_words", [P, 2, HALF], U16)
        partner_words.append([gather(late_words[:, a, :], table[a], list_half(partner_list, 1)) for a in range(2)])
        gather(late_picked[:], table_scales, case_list[:])

        w2_second = placed("w2_second", [P, 2, HALF], U32, W2_SECOND_AT)
        nc.sync.dma_start(w2_second[:].bitcast(I32), w2_view[:, :, HALF * SECOND : HALF * (SECOND + 1)])
        w1_raw = {}
        for c, a in ((c, a) for c in (FIRST, SECOND) for a in range(2)):
            if (c, a) == (SECOND, 1):
                late_planes = placed("late_planes", [P, 2, S], U8, LATE_PLANES_AT)
                lay_planes(nc.sync, late_planes, late_picked)
            w1_raw[c, a] = placed("w1_raw%d%d" % (c, a), [P, PACK, HALF], F32, W1_AT[c, a])
            nc.sync.dma_start(
                w1_raw[c, a][:],
                w1[PASS * a : PASS * (a + 1), HALF * c : HALF * (c + 1)].rearrange("(p i) r -> p i r", i=PACK),
            )
        w3_codes = placed("w3_codes", [P, 2, 2 * N], U8, W3_CODES_AT)
        w3_planes = placed("w3_planes", [P, 2, N], U8, W3_PLANES_AT)
        clinic_t = placed("clinic_t", [P, OUT_TILES], F32, CLINIC_AT)
        load_planes(nc.sync, w3_planes, w3_scales)
        nc.sync.dma_start(w3_codes[:].bitcast(I32), w3_words.rearrange("a p b -> p a b").bitcast(I32))
        with nc.allow_non_contiguous_dma(reason="one offset a partition"):
            nc.sync.dma_start(clinic_t[:], clinic.rearrange("(n p) -> p n", p=P))

        for a in range(2):
            deal_planes(SECOND, a)
        for a in range(2):
            deal_codes(nc.gpsimd.tensor_copy, SECOND, a, w2_second[:, a, :])

        partner_planes = [early_planes[:, :, HALF * h : HALF * (1 + h)] for h in range(2)]
        case_planes = [late_planes[:, :, HALF * h : HALF * (1 + h)] for h in range(2)]

        def product(out_ap, stationary, moving, passes=(1, 0), opening=1):
            for a in passes:
                nc.tensor.matmul_mx(
                    out=out_ap,
                    lhsT=stationary[a][0],
                    lhsT_scale=stationary[a][1],
                    rhs=moving[a][0],
                    rhs_scale=moving[a][1],
                    start=(a == opening),
                    stop=(a != opening),
                )

        def picked_columns(words, planes, j0, width):
            return [(words[a][:, j0 : j0 + width].bitcast(FP4X4), planes[:, a, j0 : j0 + width]) for a in range(2)]

        def weight_columns(weight, r0, width):
            return [(code[:, r0 : r0 + width].bitcast(FP8X4), plane[:, r0 : r0 + width]) for code, plane in weight]

        stages = []

        def next_banks():
            first = TILES * (len(stages) % 2)
            stages.append(first)
            return [bank_tile(first + index, [P, HALF]) for index in range(TILES)]

        def turned_stage(feature, words, planes, weight):
            for jt, bank in enumerate(next_banks()):
                product(bank[:], picked_columns(words, planes, P * jt, P), weight_columns(weight, 0, HALF))
                nc.scalar.activation(feature[:, jt, :], bank[:], ACT.Exp)

        def dealt_stage(feature, c, slices, words, planes, weight, early=False, biased=True):
            work = list(zip(next_banks(), slices))
            if early:
                for bank, (h, t) in work[:EARLY]:
                    product(bank[:], weight_columns(weight, P * t, P), picked_columns(words[h], planes[h], 0, HALF), (0,), 0)
            for bank, (h, t) in work:
                moving = picked_columns(words[h], planes[h], 0, HALF)
                if early and t < EARLY:
                    product(bank[:], weight_columns(weight, P * t, P), moving, (1,), 0)
                else:
                    product(bank[:], weight_columns(weight, P * t, P), moving)
                if biased:
                    nc.scalar.activation(feature[c, h][:, t, :], bank[:], ACT.Exp, bias=bias[:, c, t : t + 1])
                else:
                    nc.scalar.activation(feature[c, h][:, t, :], bank[:], ACT.Exp)

        def all_slices(h):
            return [(h, t) for t in range(PACK)]

        def slice_pair(t0):
            return [(h, t) for h in range(2) for t in (t0, t0 + 1)]

        turned = (SECOND, 1)
        dealt = [(FIRST, 0), (FIRST, 1), (SECOND, 0)]
        rb = {q: held("rb%d%d" % q, [P, PACK, HALF], F32) for q in dealt + [turned]}
        ra = {q: held("ra%d%d" % q, [P, PACK, HALF], F32) for q in dealt + [turned]}

        w2_dealt = [[(dealt_codes[c][:, a, :], dealt_planes[c][:, a, :]) for a in range(2)] for c in range(2)]
        for c, h in dealt:
            dealt_stage(rb, c, all_slices(h), partner_words, partner_planes, w2_dealt[c], (c, h) == dealt[0])
        turned_stage(rb[turned], partner_words[1], partner_planes[1], w2_dealt[SECOND])

        def dealt_view(c, a):
            return w1_raw[c, a][:].rearrange("p i (m t) -> p m t i", t=PACK)

        def packed(name, offset=None):
            code = placed(name, [P, HALF], U32, offset) if offset else held(name, [P, HALF], U32)
            return code[:], held(name + "_plane", [P, HALF], U8)[:]

        def round_w1(tile, c, a, ms, ts):
            nc.vector.tensor_copy(
                tile[:].rearrange("p t m (u e) -> p m u t e", e=2)[:, ms, :, ts],
                w1_raw[c, a][:].rearrange("p (u e) (m t) -> p m u t e", e=2, t=PACK)[:, ms, :, ts],
            )

        def quantise_w1(c, weight):
            rounded = [placed("rounded%d%d" % (c, a), [P, PACK, P, PACK], BF16, ROUNDED_AT[c, a]) for a in range(2)]
            values = [tile[:].rearrange("p t m i -> p m t i") for tile in rounded]
            if c == FIRST:
                for a, m0, m1 in ((0, 0, P // 2), (0, P // 2, P), (1, 0, SHARE)):
                    nc.gpsimd.tensor_scalar(
                        values[a][:, m0:m1], dealt_view(c, a)[:, m0:m1], 1.0, 0.0, ALU.mult, ALU.add
                    )
            for t in range(0, PACK, 2):
                columns = slice(P * t, P * (t + 2))
                if c == FIRST:
                    round_w1(rounded[1], c, 1, slice(SHARE, P), slice(t, t + 2))
                else:
                    for a in range(2):
                        round_w1(rounded[a], c, a, slice(0, P), slice(t, t + 2))
                for a, (code, plane) in enumerate(weight):
                    slices = rounded[a][:, t : t + 2].rearrange("p t m i -> p (t m i)")
                    quantise(code[:, columns], plane[:, columns], slices)

        def gather_cases(words, h):
            return [gather(words[:, a, :], table[a], list_half(case_list, h)) for a in range(2)]

        case_words = [gather_cases(held("case_words%d" % h, [P, 2, HALF], U16), h) for h in range(2)]
        w1_first = [packed("w1_first%d" % a, W1_CODES_AT + 2048 * (1 + a)) for a in range(2)]
        quantise_w1(FIRST, w1_first)
        for t0 in (0, 2):
            dealt_stage(ra, FIRST, slice_pair(t0), case_words, case_planes, w1_first, biased=False)

        w1_second = [packed("w1_second0", W1_CODES_AT), packed("w1_second1")]
        quantise_w1(SECOND, w1_second)
        dealt_stage(ra, SECOND, all_slices(0), case_words, case_planes, w1_second, biased=False)
        turned_stage(ra[turned], case_words[1], case_planes[1], w1_second)

        total = placed("total", [P, 3, PACK, HALF], F32, TOTAL_AT)
        for index, q in enumerate(dealt):
            for t in range(PACK):
                nc.vector.scalar_tensor_tensor(
                    total[:, index, t], ra[q][:, t], gain_inv[:, q[0], t : t + 1], rb[q][:, t], ALU.mult, ALU.add
                )
        sums = next_banks()
        for jt in range(TILES):
            for t in range(PACK):
                for index, term in enumerate((rb[turned], ra[turned])):
                    nc.tensor.matmul(
                        sums[t][:, P * jt : P * (jt + 1)],
                        term[:, jt, P * t : P * (t + 1)],
                        identity[:],
                        start=(index == 0),
                        stop=(index == 1),
                        is_transpose=True,
                    )

        starts = [sum(CHUNKS[:index]) for index in range(len(CHUNKS))]
        steps = [(starts[index], tiles, c) for index, tiles in enumerate(CHUNKS) for c in (FIRST, SECOND)]
        roots = placed("roots", [P, 4 * PACK * HALF], F32, ROOTS_AT)
        y, places = {}, {"used": 0}

        def root_room(width):
            used = places["used"]
            places["used"] = used + PACK * width
            return roots[:, used : used + PACK * width].rearrange("p (t j) -> p t j", t=PACK)

        def pieces(step):
            width = P * steps[step][1]
            return [slice(0, width // 2), slice(width // 2, width)] if step in HALVED else [slice(0, width)]

        def make_root(step):
            first, tiles, c = steps[step]
            h, jt = divmod(first, TILES)
            if (c, h) != turned:
                y[step] = root_room(P * tiles)
                values = total[:, dealt.index((c, h)), :, P * jt : P * (jt + tiles)]
                for piece in pieces(step):
                    nc.scalar.activation(y[step][:, :, piece], values[:, :, piece], ACT.Abs_reciprocal_sqrt)
                return
            if jt % 2 == 0:
                places["turned"] = root_room(2 * P)
                for t in range(PACK):
                    nc.scalar.activation(
                        places["turned"][:, t, :],
                        sums[t][:, P * jt : P * (jt + 2)],
                        ACT.Abs_reciprocal_sqrt,
                        scale=gain_inv[:, SECOND, t : t + 1],
                    )
            y[step] = places["turned"][:, :, P * (jt % 2) : P * (jt % 2 + tiles)]

        def square(step):
            width = P * steps[step][1]
            grouped = held("h_grouped%d" % step, [P, width, PACK], BF16)
            for piece in pieces(step):
                values = y[step][:, :, piece].rearrange("p t (n e) -> p n t e", e=NEIGHBOURS)
                target = grouped[:, piece, :].rearrange("p (n e) t -> p n t e", e=NEIGHBOURS)
                nc.vector.tensor_tensor(target, values, values, ALU.mult)
            return grouped[:].rearrange("p n t -> p (n t)")

        def quantise_h(step):
            width = P * steps[step][1]
            code = held("h_codes%d" % step, [P, width], U32)
            plane = held("h_plane%d" % step, [P, width], U8)
            quantise(code[:], plane[:], squared[step])
            return code[:], plane[:]

        def multiply(chunk, operands):
            group = [index for index, members in enumerate(GROUPS) if chunk in members][0]
            opening = GROUPS[group][0]
            if chunk == opening:
                reach = P * sum(CHUNKS[member] for member in GROUPS[group])
                places["scores"] = [bank_tile(index, [P, reach]) for index in SCORE_BANKS[group]]
            columns = slice(P * (starts[chunk] - starts[opening]), P * (starts[chunk] - starts[opening] + CHUNKS[chunk]))
            halves = list(zip((FIRST, SECOND), operands))
            passes = [(n, half) for n in range(OUT_TILES) for half in halves]
            if chunk == len(CHUNKS) - 1:
                passes = [(n, half) for half in halves for n in range(OUT_TILES)]
            for n, (c, (code, plane)) in passes:
                nc.tensor.matmul_mx(
                    out=places["scores"][n][:, columns],
                    lhsT=w3_codes[:, c, 2 * P * n : 2 * P * (n + 1)].bitcast(FP4X4),
                    lhsT_scale=w3_planes[:, c, P * n : P * (n + 1)],
                    rhs=code.bitcast(FP8X4),
                    rhs_scale=plane,
                    start=(c == FIRST),
                    stop=(c == SECOND),
                )
            if chunk == GROUPS[group][-1]:
                store(opening, places["scores"])

        def store(chunk, banks):
            first, width = starts[chunk], banks[0].shape[1]
            for n in range(OUT_TILES):
                scores = held("scores%d%d" % (chunk, n), [P, width], F32)
                if chunk == len(CHUNKS) - 1 and n == 1:
                    nc.vector.tensor_scalar(scores[:], banks[n][:], clinic_t[:, n : n + 1], None, ALU.add)
                else:
                    nc.scalar.activation(scores[:], banks[n][:], ACT.Identity, bias=clinic_t[:, n : n + 1])
                nc.sync.dma_start(out[P * n : P * (n + 1), P * first : P * first + width], scores[:])

        count = len(steps)
        squared, made = {}, []
        for step in range(AHEAD):
            make_root(step)
        for step in range(count + 1):
            if step + AHEAD < count:
                make_root(step + AHEAD)
            if step < count:
                squared[step] = square(step)
            if step > 0:
                made.append(quantise_h(step - 1))
                if step % 2 == 0:
                    multiply(step // 2 - 1, made[-2:])
